import numpy as np, ml_dtypes
CORES = [6,15,38,47]
N = 4
BF = ml_dtypes.bfloat16
W, L, CAP, T, D = 8192, 256, 2, 5, 1
def place(s, p):
    return ((((s & 4095) * (2 * p + 1)) >> 3) + 37 * s + 613 * p) & (W - 1)
def cells(lf, p):
    return place((32768 + lf)[..., None] >> np.arange(16), p[..., None])
def page(w, z):
    return np.add.reduce(w[..., 0:1] * z, axis=-2) & 255
def pack(x, c, z, lf, w, th):
    return {"x0": x.reshape(N, 128, W).astype(np.float32).astype(BF), "c0": c.reshape(N, 8, W).astype(np.float32).astype(BF), "z0": z.reshape(N, 128, L).astype(np.float32).astype(BF),
            "leaf": np.ascontiguousarray(lf).astype(np.int32), "wt": np.ascontiguousarray(w.reshape(N, 128, 2)).astype(np.int32), "th": np.ascontiguousarray(th.reshape(N, 8, 1)).astype(np.int32)}
def parts(rng):
    x = rng.integers(0, 16, (N, 8, 16, W)); c = rng.integers(0, CAP, (N, 8, W))
    pool = rng.integers(0, 16, (N, 8, 16, 64)); z = np.take_along_axis(pool, rng.integers(0, 64, (N, 8, 1, L)), 3)
    z = np.where(rng.random((N, 8, 1, L)) < 0.5, z, rng.integers(0, 16, (N, 8, 16, L)))
    few = rng.integers(0, 32768, (N, 8, 16)); lf = np.take_along_axis(few, rng.integers(0, 16, (N, 8, L)), 2)
    lf = np.where(rng.random((N, 8, L)) < 0.25, lf, rng.integers(0, 32768, (N, 8, L)))
    return x, c, z, lf, rng.integers(1, 256, (N, 8, 16, 2)), rng.integers(50, 81, (N, 8))
def setup_inputs(rng):
    return pack(*parts(rng))
def setup_inputs_spread(rng):
    def uneven(n):
        v = np.minimum((np.exp2(4 * rng.random((N, 8, 1, n))) * rng.random((N, 8, 16, n))).astype(np.int64), 15)
        return np.where(rng.random((N, 8, 1, n)) < 0.5, v, 15 - v)
    c = np.where(rng.random((N, 8, W)) < rng.random((N, 8, 1)), CAP - 1, rng.integers(0, CAP, (N, 8, W)))
    lf = np.minimum(np.exp2(15 * rng.random((N, 8, L))).astype(np.int64), 32767)
    w = np.minimum(np.maximum(np.exp2(8 * rng.random((N, 8, 16, 2))).astype(np.int64), 1), 255)
    return pack(uneven(W), c, uneven(L), lf, w, rng.integers(0, 121, (N, 8)))
def setup_inputs_ends(rng):
    def ends(n):
        one = rng.integers(0, 2, (N, 8, 1, n)); el = rng.integers(0, 2, (N, 8, 16, n))
        return np.where(rng.random((N, 8, 1, n)) < 0.5, one, el) * 15
    x = ends(W); z = ends(L); c = (CAP - 1) * rng.integers(0, 2, (N, 8, W)); lf = 32767 * rng.integers(0, 2, (N, 8, L))
    w = 1 + 254 * rng.integers(0, 2, (N, 8, 16, 2)); w[:, 1::3] = 255; w[:, 0, 0] = 1; w[:, 0, 15] = 255
    th = 120 * ((np.arange(8)[None, :] + rng.integers(0, 2, (N, 1))) & 1)
    for q in range(N):
        for g in range(8):
            if g % 3 == 1:
                z[q, g][:, [1, L - 2]] = 15; lf[q, g, [1, L - 2]] = 32767
                x[q, g][:, cells(np.array([32767]), np.array([(16 * 15 * 255) & 255]))[0]] = 0
            z[q, g][:, [2, L - 3]] = 0; lf[q, g, [2, L - 3]] = 0
            order = rng.permutation(16)
            for m in (16, 0) + tuple(range(1, 16)):
                v = 15 * (order < m).astype(np.int64); p = int(np.dot(w[q, g, :, 0], v)) & 255
                k = np.flatnonzero(place(32768 + np.arange(32768), p) == W - 1)
                if k.size:
                    lone = int(rng.choice(k))
                    z[q, g][:, [0, L - 1]] = v[:, None]; lf[q, g, [0, L - 1]] = lone
                    x[q, g][:, W - 1] = v if (q + g) % 2 == 0 else 15 - v
                    above = int(place((32768 + lone) >> 1, p))
                    if (q + g) % 2 == 1 and above != W - 1:
                        x[q, g][:, above] = v; c[q, g, W - 1] = CAP - 1
                    break
    return pack(x, c, z, lf, w, th)
def near(z, n):
    i = np.arange(16)[:, None]; d = (n >> 4)[None, :] + (i < (n & 15)[None, :])
    return np.where(z < 8, z + d, z - d)
def setup_inputs_corners(rng):
    x, c, z, lf, w, th = parts(rng)
    th = rng.choice(np.array([0, 1, 20, 40, 120]), (N, 8)); kind = (np.arange(8)[None, :] + rng.integers(0, 3, (N, 1))) % 3
    c = np.where(kind[:, :, None] == 0, 0, np.where(kind[:, :, None] == 1, CAP - 1, c))
    lf = np.where(rng.random((N, 8, L)) < 0.5, rng.choice(np.array([0, 1, 16383, 16384, 32766, 32767]), (N, 8, L)), lf); lf[:, :, 0] = 0; lf[:, :, L - 1] = 32767
    wk = rng.integers(0, 4, (N, 8, 1, 2)); w = np.where(wk == 0, 1, np.where(wk == 1, 255, w))
    zk = rng.random((N, 8, 1, L)); z = np.where(zk < 0.05, 0, np.where(zk > 0.95, 15, z))
    for q in range(N):
        for g in range(8):
            h = cells(lf[q, g], page(w[q, g], z[q, g]))
            lv = rng.choice(np.array([0, 1, 7, 14]), L); n = np.maximum(th[q, g] + rng.integers(-1, 2, L), 0)
            x[q, g][:, h[np.arange(L), lv]] = near(z[q, g], n)
            e = np.array([th[q, g], th[q, g] + 1])
            x[q, g][:, h[[0, L - 1], 0]] = near(z[q, g][:, [0, L - 1]], e)
    return pack(x, c, z, lf, w, th)
def setup_inputs_crowd(rng):
    x, c, z, lf, w, th = parts(rng)
    for q in range(N):
        if q % 3 < 2:
            x[q] = rng.integers(0, 4, (8, 16, W)); z[q] = rng.integers(12, 16, (8, 16, L)); th[q] = rng.integers(0, 61, 8)
        lone = 0 if q & 1 else L - 1
        for g in range(8):
            if g % 4 == 0: ix = np.full(L, int(rng.integers(0, L)))
            elif g % 4 == 1: ix = np.full(L, lone ^ 1); ix[lone] = lone
            elif g % 4 == 2: ix = rng.integers(0, 4, L)
            else: ix = np.arange(L)
            z[q, g] = z[q, g][:, ix]; lf[q, g] = lf[q, g][ix]
            if q % 3 == 1 and g == 1:
                pg = page(w[q, g], z[q, g]); other = cells(lf[q, g, [lone ^ 1]], pg[[lone ^ 1]])[0]
                some = rng.permutation(32768)[:256]; hs = place(32768 + some, pg[lone])
                k = int(np.argmax(~np.isin(hs, other)))
                lf[q, g, lone] = some[k]; x[q, g][:, hs[k]] = z[q, g][:, lone]
    return pack(x, c, z, lf, w, th)
def setup_inputs_full(rng):
    x, c, z, lf, w, th = parts(rng); th = rng.integers(0, 9, (N, 8)); c[:, [0, 1, 4, 5]] = CAP - 1
    for q in range(N):
        for g in range(8):
            a, b = rng.permutation(16)[:2]; w[q, g, a, 0] = 1; w[q, g, b, 0] = 16
            zz = rng.integers(0, 16, (16, L)); zz[[a, b]] = 0
            pg = np.full(L, int(rng.integers(0, 256))) if g % 4 == 3 else rng.permutation(256)[:L]
            left = (pg - page(w[q, g], zz)) & 255; zz[a] = left & 15; zz[b] = left >> 4; z[q, g] = zz
            cand = rng.integers(0, 32768, (L, 24)); lv = rng.integers(1, 16, (L, 24))
            if g % 2 == 0: lv[:, :16] = 15
            h = cells(cand, pg[:, None]).tolist(); lv = lv.tolist(); taken = set(); hits = set(); at = []; who = []
            for l in range(L):
                for m in range(24):
                    v = lv[l][m]; way = h[l][m]
                    if way[v - 1] not in taken and (v == 15 or (way[v] not in hits and way[v] not in way[:v])): break
                lf[q, g, l] = cand[l, m]; taken.add(way[v - 1])
                if v < 15: hits.add(way[v]); at.append(way[v]); who.append(l)
            if at: x[q, g][:, np.array(at)] = near(zz[:, np.array(who)], rng.integers(0, int(th[q, g]) + 1, len(at)))
    return pack(x, c, z, lf, w, th)
def check_inputs(d):
    bad = []
    for k, lo, hi in (("x0", 0, 15), ("c0", 0, CAP - 1), ("z0", 0, 15), ("leaf", 0, 32767), ("wt", 1, 255), ("th", 0, 120)):
        a = np.asarray(d[k]).astype(np.float64)
        if not (np.min(a) >= lo and np.max(a) <= hi): bad.append("range of " + k)
        elif np.any(a != np.floor(a)): bad.append("whole numbers in " + k)
    return bad
def reference(x0, c0, z0, leaf, wt, th):
    X = x0.astype(np.float32).astype(np.int64).reshape(N, 8, 16, W); C = c0.astype(np.float32).astype(np.int64).reshape(N, 8, W)
    z = z0.astype(np.float32).astype(np.int64).reshape(N, 8, 16, L); lf = leaf.astype(np.int64)
    w = wt.astype(np.int64).reshape(N, 8, 16, 2); lim = th.astype(np.int64).reshape(N, 8, 1, 1); A = np.zeros(N, np.int64); zs = []
    for t in range(T):
        home = (np.arange(N) - D * t) % N
        zq = z[home]; lq = lf[home]
        h = cells(lq, page(w, zq))
        xk = np.take_along_axis(X, h.reshape(N, 8, 1, L * 16), 3).reshape(N, 8, 16, L, 16)
        dist = np.add.reduce(np.abs(xk - zq[..., None]), axis=2)
        hit = dist <= lim + (A & 15).reshape(N, 1, 1, 1); hit[..., 15] = True
        j = np.argmax(hit, axis=-1)
        y = np.take_along_axis(xk, j[:, :, None, :, None], 4)[..., 0]
        for q in range(N):
            for g in range(8):
                m = np.flatnonzero(j[q, g] > 0); named = h[q, g, m, j[q, g, m] - 1]
                cell, first = np.unique(named, return_index=True); who = m[first]
                C[q, g, cell] += 1; full = C[q, g, cell] == CAP
                X[q, g][:, cell[full]] = y[q, g][:, who[full]]; C[q, g, cell[full]] = 0
                cell, first = np.unique(h[q, g, :, 15], return_index=True)
                X[q, g][:, cell] = (xk[q, g][:, first, 15] + zq[q, g][:, first]) >> 1
        A = np.add.reduce((j == 15).astype(np.int64).reshape(N, 8 * L), axis=1)
        zq = np.abs(zq - y); z = np.zeros_like(zq); z[home] = zq; zs.append(z)
        if t < T - 1: lf[home] = (8 * lq + np.add.reduce(w[..., 1:2] * zq, axis=2)) & 32767
    return {"zs": np.concatenate(zs, axis=3).reshape(N, 128, T * L).astype(np.float32).astype(BF), "xs": np.add.reduce(w[..., 0:1] * X, axis=2).astype(np.float32), "cs": C.astype(np.float32)}

@@ -1,0 +1,362 @@
+from concourse.mybir import AluOpType, ActivationFunctionType, AxisListType
+
+CB = 8208
+NW = 16416
+B2, F4, I4, U2 = "bfloat16", "float32", "int32", "uint16"
+SCRATCH = {"win": ("sbuf", [128, NW], B2), "sh": ("sbuf", [128, 15, 8, 16], B2), "vals": ("sbuf", [128, 16, 32], B2),
+           "diff": ("sbuf", [128, 4096], B2),
+           "ad": ("sbuf", [128, 256, 16], B2),
+           "eye": ("sbuf", [128, 8, 16], B2), "neye": ("sbuf", [128, 8, 16], B2), "lh": ("sbuf", [128, 8, 128], B2),
+           "wd": ("sbuf", [128, 16, 128], B2),
+           "xa": ("sbuf", [128, 16, 128], B2),
+           "eq": ("sbuf", [128, 15, 32], B2), "ts": ("sbuf", [128, 4, 2, 4, 4], F4), "oi": ("sbuf", [128, 4, 2, 4], I4),
+           "pg": ("psum", [128, 4, 8, 16], F4), "pd": ("psum", [128, 32, 16], F4), "pq": ("psum", [128, 16, 32], F4),
+           "pf": ("psum", [128, 512], F4), "pn": ("psum", [128, 512], F4), "pr": ("psum", [128, 512], F4),
+           "px": ("psum", [128, 512], F4)}
+for _d, _l in ((B2, "ones:128 blk1:128 blk:128 eye2:128 zz:16 thb:1 j15:16 hl:64 rw:256 rv:256 zh1:256 zh2:256 z2:256 yv:256 nc:256"),
+               (F4, "p15:1 gp1:1 gp0:1 wf:2 wp:2 thc:1 mc:1 lu:32 lt:32 e16:16 e3:256 hc:256 rr:256 b8:64 sp:256 aa:256 hf:256 "
+                    "hd:256 ms:256 sc:256 sn:256 ac:1 nr:32 uu:32 u2:16 un:32 ur:16 xo:512"),
+               (I4, "pidx:1 p15i:1 gpi:1 wti:2 thi:1 lfi:16 qi:16 fi:16 ss:256 bi:64 ww:256 hh:256 ai:1 am:1 ri:16 rn:16"),
+               (U2, "li:256 lo:16 nl:16 rl:32 rt:32")):
+    for _x in _l.split():
+        SCRATCH[_x.split(":")[0]] = ("sbuf", [128, int(_x.split(":")[1])], _d)
+for _t in range(5):
+    SCRATCH["zi%d" % _t] = ("sbuf", [128, 4, 4, 16], B2)
+    SCRATCH["zn%d" % _t] = ("sbuf", [128, 256], B2)
+    SCRATCH["fw%d" % _t] = ("sbuf", [128, 4, 2, 4], F4)
+    SCRATCH["add%d" % _t] = ("sbuf", [128, 4, 2, 4], F4)
+SEMAPHORES = ["qv", "qt", "qs", "qg", "ls", "wp", "gd", "dc", "h1", "h2"] + ["za%d" % t for t in range(1, 5)] + \
+    ["fa%d" % t for t in range(1, 5)] + ["d%d" % k for k in range(12)]
+
+
+def state(g, T):
+    return {"g": g, "T": T, "q": {"v": g.vector, "t": g.tensor, "s": g.scalar, "g": g, "y": g.sync},
+            "known": {k: {} for k in "vtsgy"}, "count": {}, "w": {}, "r": {}, "nd": 0}
+
+
+def norm(x):
+    return (x, 0, 1 << 30) if isinstance(x, str) else x
+
+
+def need(S, q, ev):
+    kn = S["known"][q]
+    sem, val, clock = ev
+    if kn.get(sem, 0) >= val:
+        return
+    S["q"][q].wait_ge(S["T"].sem[sem], val)
+    for k in clock:
+        kn[k] = max(kn.get(k, 0), clock[k])
+    kn[sem] = max(kn.get(sem, 0), val)
+
+
+def deps(S, q, reads, writes):
+    todo = []
+    for x, old in [(x, S["w"]) for x in reads] + [(x, S["w"]) for x in writes] + [(x, S["r"]) for x in writes]:
+        n, lo, hi = norm(x)
+        for (a, b, ev) in old.get(n, []):
+            if lo < b and a < hi and not (q == "t" and ev[0] == "qt"):
+                todo.append(ev)
+    for ev in sorted(todo, key=lambda e: -e[1]):
+        need(S, q, ev)
+
+
+def note(S, reads, writes, ev):
+    for x in reads:
+        n, lo, hi = norm(x)
+        l = S["r"].setdefault(n, [])
+        l[:] = [e for e in l if not (e[2][0] == ev[0] and lo <= e[0] and e[1] <= hi)] + [(lo, hi, ev)]
+    for x in writes:
+        n, lo, hi = norm(x)
+        for key in ("w", "r"):
+            l = S[key].setdefault(n, [])
+            l[:] = [e for e in l if not (lo <= e[0] and e[1] <= hi)]
+        S["w"][n].append((lo, hi, ev))
+
+
+def op(S, q, fn, reads, writes):
+    deps(S, q, reads, writes)
+    sem = "q" + q
+    S["count"][sem] = S["count"].get(sem, 0) + 1
+    fn().then_inc(S["T"].sem[sem], 1)
+    clock = dict(S["known"][q])
+    clock[sem] = S["count"][sem]
+    note(S, reads, writes, (sem, S["count"][sem], clock))
+
+
+def dma(S, q, fn, reads, writes, sem=None, parts=1):
+    deps(S, q, reads, writes)
+    if sem is None:
+        sem = "d%d" % S["nd"]
+        S["nd"] += 1
+    for k in range(parts):
+        (fn(k) if parts > 1 else fn()).then_inc(S["T"].sem[sem], 16)
+    clock = dict(S["known"][q])
+    clock[sem] = S["count"][sem] = 16 * parts
+    note(S, reads, writes, (sem, 16 * parts, clock))
+
+
+def arrival(S, sem, val, writes):
+    S["count"][sem] = val
+    note(S, [], writes, (sem, val, {}))
+
+
+def rank_program(g, core, T, topo):
+    rank = T.rank_of(core)
+    if rank is None:
+        return
+    A, F = AluOpType, ActivationFunctionType
+    S = state(g, T)
+    V, P, C = g.vector, g.tensor, g.scalar
+    cores = list(T.cores)
+    N = len(cores)
+    nxt, prv = cores[(rank + 1) % N], cores[(rank - 1) % N]
+    E = len(topo.engines(prv, core))
+
+    def v(fn, reads, writes):
+        op(S, "v", fn, reads, writes)
+
+    def s(fn, reads, writes):
+        op(S, "s", fn, reads, writes)
+
+    def vs(o, i, a, b, p, q, reads, writes):
+        if q is None:
+            v(lambda: V.tensor_scalar(o, i, a, b, p), reads, writes)
+        else:
+            v(lambda: V.tensor_scalar(o, i, a, b, p, q), reads, writes)
+
+    def vt(o, x, y, p, reads, writes):
+        v(lambda: V.tensor_tensor(o, x, y, p), reads, writes)
+
+    def copy(o, i, reads, writes, bias=0.0, scale=1.0):
+        s(lambda: C.activation(o, i, F.Copy, bias=bias, scale=scale), reads, writes)
+
+    def mm(out, lhsT, rhs, start, stop, reads, writes):
+        op(S, "t", lambda: P.matmul(out, lhsT, rhs, start=start, stop=stop), reads, writes)
+
+    def send(dst, out, src, sem, reads):
+        deps(S, "g", reads, [])
+        rid, pid, _ = topo.addr(dst)
+        g.remote_dma(out, src, T.sem[sem], T.sem.ls, pid, rid, topo.mask(core, dst))
+        S["count"]["ls"] = S["count"].get("ls", 0) + len(topo.engines(core, dst))
+
+    dma(S, "y", lambda: g.sync.dma_start(T.wti[:], T.wt[:]), [], ["wti"])
+    dma(S, "s", lambda: C.dma_start(T.lfi[:], T.leaf[:]), [], ["lfi"])
+    dma(S, "y", lambda: g.sync.dma_start(T.zi0[:], T.z0[:]), [], ["zi0"])
+    dma(S, "y", lambda: g.sync.dma_start(T.win[:, 16:CB], T.x0[:]), [], [("win", 16, CB)])
+    dma(S, "y", lambda i: g.sync.dma_start(T.win[i:128:16, CB + 16:NW], T.c0[:]), [], [("win", CB + 16, NW)], "dc", 16)
+    op(S, "g", lambda: g.iota(T.pidx[:], [[0, 1]], 0, 1), [], ["pidx"])
+    for n, x in [("ones", 1.0), ("thi", 0), ("lh", 0.0), ("add0", 1.0), ("wd", 0.0), ("zz", 0.0), ("e3", -256.0), ("hd", 0.0)] + \
+            [("fw%d" % t, 1.0) for t in range(4)]:
+        v(lambda: V.memset(T[n][:], x), [], [n])
+    v(lambda: V.memset(T.win[:, 0:16], 0.0), [], [("win", 0, 16)])
+    v(lambda: V.memset(T.win[:, CB:CB + 16], 0.0), [], [("win", CB, CB + 16)])
+    dma(S, "s", lambda: C.dma_start(T.thi[0:128:16, :], T.th[:]), [], ["thi"])
+    op(S, "g", lambda: g.affine_select(T.blk1[:], T.ones[:], [[-16, 8], [0, 16]], A.is_ge, 0.0, 0, 1), ["ones"], ["blk1"])
+    op(S, "g", lambda: g.affine_select(T.blk[:], T.blk1[:], [[16, 8], [0, 16]], A.is_ge, 0.0, 15, -1), ["blk1"], ["blk"])
+    op(S, "g", lambda: g.affine_select(T.eye[:], T.ones[:], [[-1, 128]], A.is_equal, 0.0, 0, 1), ["ones"], ["eye"])
+    vs(T.p15i[:], T.pidx[:], 15, None, A.bitwise_and, None, ["pidx"], ["p15i"])
+    vs(T.gpi[:], T.pidx[:], 4, 1, A.arith_shift_right, A.bitwise_and, ["pidx"], ["gpi"])
+    v(lambda: V.tensor_copy(T.p15[:], T.p15i[:]), ["p15i"], ["p15"])
+    v(lambda: V.tensor_copy(T.gp1[:], T.gpi[:]), ["gpi"], ["gp1"])
+    vs(T.gp0[:], T.gpi[:], -1.0, 1.0, A.mult, A.add, ["gpi"], ["gp0"])
+    for i in range(16):
+        copy(T.wd[:, i, i::16], T.blk[:, 0::16], ["blk", "wd"], [("wd", i, i + 1)])
+    v(lambda: V.tensor_copy(T.wf[:], T.wti[:]), ["wti"], ["wf"])
+    for gs in range(2):
+        for c0 in range(4):
+            vs(T.lh[:, gs * 4 + c0, c0::32], T.blk[:, 16 * gs::32], T.wf[:, 0:1], 2.0, A.mult, A.mult,
+               ["blk", "wf"], [("lh", 2 * (gs * 4 + c0), 2 * (gs * 4 + c0) + 1)])
+    vs(T.lu[:, 0:16], T.lfi[:], T.gp0[:, 0:1], None, A.mult, None, ["lfi", "gp0"], [("lu", 0, 16)])
+    vs(T.lu[:, 16:32], T.lfi[:], T.gp1[:, 0:1], None, A.mult, None, ["lfi", "gp1"], [("lu", 16, 32)])
+    v(lambda: V.transpose(T.lt[:], T.lu[:]), ["lu"], ["lt"])
+    vt(T.fi[:], T.lt[:, 0:16], T.lt[:, 16:32], A.add, ["lt"], ["fi"])
+    send(nxt, T.wp[:], T.wf[:], "wp", ["wf"])
+    arrival(S, "wp", E, ["wp"])
+
+    def rest_one():
+        vs(T.neye[:], T.eye[:], -1.0, None, A.mult, None, ["eye"], ["neye"])
+        vs(T.eye2[:], T.eye[:], 2.0, None, A.mult, None, ["eye"], ["eye2"])
+        mm(T.pd[:, 0:16, 0], T.blk[:], T.zz[:], True, True, ["blk", "zz"], ["pd"])
+        op(S, "g", lambda: g.iota(T.e16[:], [[16, 16]], 3840, 0, allow_small_or_imprecise_dtypes=True), [], ["e16"])
+        op(S, "g", lambda: g.iota(T.hc[:], [[16384, 16], [0, 16]], 16400, 0, allow_small_or_imprecise_dtypes=True), [], ["hc"])
+        for k in range(1, 16):
+            op(S, "g", lambda: g.affine_select(T.sh[:, k - 1, :, k:16], T.neye[:, :, k:16], [[-16, 8], [-1, 16 - k]], A.not_equal,
+                                               1.0, 0, 1), ["neye"], [("sh", 2 * k, 2 * k + 1)])
+
+    def rest_two():
+        vs(T.e3[:, 15::16], T.e16[:], T.p15[:, 0:1], None, A.add, None, ["e16", "p15"], ["e3"])
+        v(lambda: V.tensor_copy(T.thb[:], T.thi[:]), ["thi"], ["thb"])
+        mm(T.px[:, 0:1], T.blk[:], T.thb[:], True, True, ["blk", "thb"], ["px"])
+        v(lambda: V.tensor_copy(T.thc[:], T.px[:, 0:1]), ["px"], ["thc"])
+
+    def lhb():
+        for gs in range(2):
+            for c0 in range(4):
+                q = gs * 4 + c0
+                copy(T.lh[:, q, 16 + c0::32], T.blk[:, 16 * gs::32], ["blk", "wp"], [("lh", 2 * q + 1, 2 * q + 2)], scale=T.wp[:, 1:2])
+
+    def chain(t):
+        zi, ad = "zi%d" % t, "add%d" % t
+
+        def sums():
+            copy(T.z2[:], T[zi][:], [zi], ["z2"])
+            for gs in range(2):
+                for c0 in range(4):
+                    q = gs * 4 + c0
+                    mm(T.pg[:, :, gs, :], T.lh[:, q, :], T[zi][:, :, c0, :], c0 == 0, c0 == 3,
+                       [("lh", 2 * q, 2 * q + (2 if t else 1)), zi], ["pg"])
+            v(lambda: V.transpose(T.ts[:], T.pg[:, :, 0:2, :]), ["pg"], ["ts"])
+
+        def rdoub():
+            vs(T.rr[:, 0:16], T.qi[:], 296.0, None, A.add, None, ["qi"], [("rr", 0, 16)])
+            for n in (16, 32, 64, 128):
+                copy(T.rr[:, n:2 * n], T.rr[:, 0:n], [("rr", 0, n)], [("rr", n, 2 * n)])
+
+        def sdoub(k, n):
+            return lambda: vs(T.ss[:, n:2 * n], T.ss[:, 0:n], k, None, A.arith_shift_right, None, [("ss", 0, n)], [("ss", n, 2 * n)])
+
+        def fwd():
+            fw, to = "fw%d" % t, "add%d" % (t + 1)
+            vs(T[fw][:, :, 1, :], T.fi[:], 8.0, None, A.mult, None, ["fi"], [fw])
+            send(nxt, T[to][:], T[fw][:], "fa%d" % (t + 1), [fw])
+            arrival(S, "fa%d" % (t + 1), E, [to])
+
+        s0 = ("ss", 0, 64)
+        out = [sums, lambda: vt(T.oi[:], T.ts[:, :, :, 0, :], T[ad][:], A.add, ["ts", ad], ["oi"])]
+        if t:
+            out.append(lambda: vs(T.fi[:], T.oi[:, :, 1, :], 32767, None, A.bitwise_and, None, ["oi"], ["fi"]))
+        out += [lambda: vs(T.qi[:], T.oi[:, :, 0, :], 511, None, A.bitwise_and, None, ["oi"], ["qi"]),
+                lambda: vs(T.ss[:, 0:16], T.fi[:], 32768.0, None, A.add, None, ["fi"], [("ss", 0, 16)]),
+                rdoub, sdoub(1, 16), sdoub(2, 32), sdoub(4, 64), sdoub(8, 128)]
+        if t < 4:
+            out.append(fwd)
+        out += [lambda: vs(T.bi[:], T.ss[:, 0:64], 4096, None, A.bitwise_and, None, [s0], ["bi"]),
+                lambda: vs(T.ss[:, 0:64], T.ss[:, 0:64], 4095, None, A.bitwise_and, None, [s0], [s0]),
+                lambda: vs(T.b8[:], T.bi[:], 8.0, None, A.mult, None, ["bi"], ["b8"]),
+                lambda: vs(T.sp[:], T.ss[:], 2452.0, None, A.add, None, ["ss"], ["sp"]),
+                lambda: vt(T.aa[:], T.sp[:], T.rr[:], A.mult, ["sp", "rr"], ["aa"]),
+                lambda: vt(T.aa[:, 0:64], T.aa[:, 0:64], T.b8[:], A.add, ["aa", "b8"], [("aa", 0, 64)]),
+                lambda: vs(T.ww[:], T.aa[:], 0.125, -91030.9375, A.mult, A.add, ["aa"], ["ww"]),
+                lambda: vs(T.hh[:], T.ww[:], 8191, None, A.bitwise_and, None, ["ww"], ["hh"]),
+                lambda: vs(T.li[:], T.hh[:], 16.0, None, A.add, None, ["hh"], ["li"])]
+        return out
+
+    def gather(t):
+        ends = {5: (10, 16), 10: (5, 10), 14: (1, 5)}
+        for k in [15] + list(range(15)):
+            kk = 15 - k
+            d = ("diff", 256 * kk, 256 * kk + 256)
+            vt(T.diff[:, 256 * kk:256 * kk + 256], T.win[:, 0:CB].indirect(T.li[:, 16 * k:16 * k + 16]), T.z2[:], A.subtract,
+               [("win", 0, CB), "li", "z2"], [d])
+            if k < 15:
+                s(lambda: C.activation(T.ad[:, :, kk], T.diff[:, 256 * kk:256 * kk + 256], F.Abs), [d], [("ad", kk, kk + 1)])
+                if t == 0:
+                    copy(T.sh[:, k, :, 0:k + 1], T.neye[:, :, 0:k + 1], ["neye"], [("sh", 2 * k + 3, 2 * k + 4)])
+            if k == 7 and t == 0:
+                rest_two()
+            if k in ends:
+                a, b = ends[k]
+                for i in range(16):
+                    mm(T.pd[:, 0:16, a:b], T.wd[:, i, :], T.ad[:, i::16, a:b], i == 0, i == 15,
+                       [("wd", i, i + 1), ("ad", a, b)], ["pd"])
+            if k == 1:
+                vt(T.hf[:], T.hh[:], T.hc[:], A.add, ["hh", "hc"], ["hf"])
+                vs(T.nr[:, 16:32], T.hh[:, 240:256], 16.0, None, A.add, None, ["hh"], [("nr", 16, 32)])
+                for m in range(15):
+                    op(S, "g", lambda: g.affine_select(T.hd[:, 15 - m::16], T.hf[:, 16 * m:16 * m + 16], [[0, 16]], A.is_gt, 0.0, 1, 0),
+                       ["hf"], [("hd", 15 - m, 16 - m)])
+            if k == 6:
+                mm(T.pr[:, 0:256], T.eye[:], T.diff[:, 0:256], True, False, ["eye", ("diff", 0, 256)], ["pr"])
+                mm(T.pr[:, 0:256], T.eye2[:], T.z2[:], False, True, ["eye2", "z2"], ["pr"])
+
+    def answer(t):
+        zn, mc = "zn%d" % t, "mc" if t else "thc"
+        vs(T.ms[:], T.pd[:, 0:16, :], T[mc][:, 0:1], None, A.is_gt, None, ["pd", mc], ["ms"])
+        v(lambda: V.tensor_tensor_scan(T.sc[:], T.ms[:], T.e3[:], 0.0, A.mult, A.add), ["ms", "e3"], ["sc"])
+        v(lambda: V.tensor_copy(T.lo[:], T.sc[:, 15::16]), ["sc"], ["lo"])
+        s(lambda: C.activation(T[zn][:], T.diff[:, 0:4096].indirect(T.lo[:]), F.Abs), ["diff", "lo"], [zn])
+        if t < 4:
+            send(nxt, T["zi%d" % (t + 1)][:], T[zn][:], "za%d" % (t + 1), [zn])
+            arrival(S, "za%d" % (t + 1), E, ["zi%d" % (t + 1)])
+        if t in (1, 2):
+            send(cores[(rank - t) % N], T["zh%d" % t][:], T[zn][:], "h%d" % t, [zn])
+        if t in (0, 4):
+            dma(S, "y", lambda: g.sync.dma_start(T.zs[:, 256 * t:256 * t + 256], T[zn][:]), [zn], [])
+
+    def update(t):
+        n16 = ("nr", 0, 16)
+        v(lambda: V.tensor_tensor_scan(T.sn[:], T.hd[:], T.ms[:], 0.0, A.max, A.mult), ["hd", "ms"], ["sn"])
+        v(lambda: V.tensor_copy(T.ri[:], T.sn[:, 15::16]), ["sn"], ["ri"])
+        vt(T.yv[:], T.diff[:, 0:4096].indirect(T.lo[:]), T.z2[:], A.add, ["diff", "lo", "z2"], ["yv"])
+        vs(T.rn[:], T.ri[:], 16383, None, A.bitwise_and, None, ["ri"], ["rn"])
+        if t < 4:
+            vs(T.j15[:], T.sc[:, 15::16], 255.5, None, A.is_lt, None, ["sc"], ["j15"])
+        vs(T.nr[:, 0:16], T.rn[:], T.p15[:, 0:1], None, A.max, None, ["rn", "p15"], [n16])
+        v(lambda: V.tensor_copy(T.hl[:, 0:32], T.nr[:]), ["nr"], [("hl", 0, 32)])
+        v(lambda: V.tensor_copy(T.nl[:], T.nr[:, 0:16]), [n16], ["nl"])
+        vt(T.hl[:, 32:64], T.nr[:], T.hl[:, 0:32], A.subtract, ["nr", ("hl", 0, 32)], [("hl", 32, 64)])
+        copy(T.nc[:], T.win[:, CB:NW].indirect(T.nl[:]), [("win", CB, NW), "nl"], ["nc"], bias=1.0, scale=-1.0)
+        copy(T.vals[:, :, 0:16], T.yv[:], ["yv"], [("vals", 0, 1)])
+        copy(T.vals[:, :, 16:32], T.nc[:], ["nc"], [("vals", 1, 2)])
+        copy(T.rw[:], T.pr[:, 0:256], ["pr"], ["rw"], bias=127.8, scale=0.5)
+        copy(T.rv[:], T.rw[:], ["rw"], ["rv"], bias=-128.0)
+        if t == 0:
+            lhb()
+        if t == 1:
+            copy(T.xa[:], T.wd[:], ["wd", "wf"], ["xa"], scale=T.wf[:, 0:1])
+        for k in range(15):
+            for h in range(2):
+                mm(T.pq[:, k, :], T.sh[:, k, :, :], T.hl[:, 32 * h:32 * h + 32], h == 0, h == 1,
+                   [("sh", 2 * k + 2, 2 * k + 4), ("hl", 32 * h, 32 * h + 32)], ["pq"])
+        if t < 4:
+            mm(T.px[:, 0:16], T.ones[:], T.j15[:], True, True, ["ones", "j15"], ["px"])
+        vs(T.eq[:], T.pq[:, 0:15, :], 0.0, None, A.is_equal, None, ["pq"], ["eq"])
+        for i in range(16):
+            mm(T.pn[:, 0:16], T.wd[:, i, :], T.nc[:, i::16], i == 0, i == 15, ["wd", "nc"], ["pn"])
+        for k in range(15):
+            mm(T.pf[:, 0:32], T.eye[:], T.eq[:, k, :], k == 0, k == 14, ["eye", "eq"], ["pf"])
+        if t < 4:
+            v(lambda: V.tensor_reduce(T.ac[:], T.px[:, 0:16], AxisListType.X, A.add), ["px"], ["ac"])
+            v(lambda: V.tensor_copy(T.ai[:], T.ac[:]), ["ac"], ["ai"])
+            vs(T.am[:], T.ai[:], 15, None, A.bitwise_and, None, ["ai"], ["am"])
+            vs(T.mc[:], T.am[:], T.thc[:, 0:1], None, A.add, None, ["am", "thc"], ["mc"])
+        vs(T.u2[:], T.pn[:, 0:16], 0.5, None, A.is_lt, None, ["pn"], ["u2"])
+        vs(T.uu[:], T.pf[:, 0:32], 0.5, None, A.is_lt, None, ["pf"], ["uu"])
+        vt(T.un[:], T.uu[:], T.nr[:], A.mult, ["uu", "nr"], ["un"])
+        vt(T.ur[:], T.un[:, 0:16], T.u2[:], A.mult, ["un", "u2"], ["ur"])
+        vs(T.rl[:, 1::2], T.un[:, 0:16], T.p15[:, 0:1], float(CB), A.max, A.add, ["un", "p15"], [("rl", 1, 2)])
+        vs(T.rt[:, 0::2], T.un[:, 16:32], T.p15[:, 0:1], None, A.max, None, ["un", "p15"], ["rt"])
+        vs(T.rl[:, 0::2], T.ur[:], T.p15[:, 0:1], None, A.max, None, ["ur", "p15"], [("rl", 0, 1)])
+        return [lambda c=c: v(lambda: V.tensor_copy(T.win[:, 0:NW].indirect(T.rl[:, 2 * c:2 * c + 2]), T.vals[:, c, :]),
+                              ["rl", "vals"], ["win"]) for c in range(15, -1, -1)] + \
+               [lambda c=c: v(lambda: V.tensor_copy(T.win[:, 0:CB].indirect(T.rt[:, 2 * c:2 * c + 1]), T.rv[:, 16 * c:16 * c + 16]),
+                              ["rt", "rv"], [("win", 0, CB)]) for c in range(15, -1, -1)]
+
+    for f in chain(0):
+        f()
+    rest_one()
+    for t in range(5):
+        gather(t)
+        answer(t)
+        sc = update(t)
+        ch = chain(t + 1) if t < 4 else []
+        for _ in range(6):
+            sc.pop(0)()
+        while ch or sc:
+            if ch:
+                ch.pop(0)()
+            for _ in range(2 if len(sc) > len(ch) else 1):
+                if sc:
+                    sc.pop(0)()
+    for q in range(16):
+        mm(T.px[:], T.xa[:, q, :], T.win[:, 16 + 512 * q:528 + 512 * q], q == 0, q == 15, ["xa", ("win", 0, CB)], ["px"])
+    v(lambda: V.tensor_copy(T.xo[:], T.px[:]), ["px"], ["xo"])
+    dma(S, "g", lambda: g.dma_start(T.cs[:], T.win[0:128:16, CB + 16:NW]), [("win", CB, NW)], [], "gd")
+    for t, b, sem in ((1, "zh1", "h1"), (2, "zh2", "h2")):
+        arrival(S, sem, len(topo.engines(cores[(rank + t) % N], core)), [b])
+        dma(S, "y", lambda: g.sync.dma_start(T.zs[:, 256 * t:256 * t + 256], T[b][:]), [b], [])
+    dma(S, "y", lambda: g.sync.dma_start(T.zs[:, 768:1024], T.zi4[:]), ["zi4"], [])
+    dma(S, "y", lambda: g.sync.dma_start(T.xs[:], T.xo[:]), ["xo"], [])
+    for sem in SEMAPHORES:
+        if S["count"].get(sem, 0):
+            need(S, "g", (sem, S["count"][sem], {}))

@@ -1,32 +1,38 @@
-from concourse.mybir import AluOpType, ActivationFunctionType, AxisListType
+from concourse.mybir import AluOpType, ActivationFunctionType
 
-CB = 8208
-NW = 16416
+NW = 8208
+BIG = 16384.0
 B2, F4, I4, U2 = "bfloat16", "float32", "int32", "uint16"
-SCRATCH = {"win": ("sbuf", [128, NW], B2), "sh": ("sbuf", [128, 15, 8, 16], B2), "vals": ("sbuf", [128, 16, 32], B2),
+SCRATCH = {"win": ("sbuf", [128, NW], B2), "cw": ("sbuf", [128, NW], F4),
+           "sh": ("sbuf", [128, 8, 8, 16], B2),
+           "ro": ("sbuf", [128, 8, 128], B2),
            "diff": ("sbuf", [128, 4096], B2),
            "ad": ("sbuf", [128, 256, 16], B2),
            "eye": ("sbuf", [128, 8, 16], B2), "neye": ("sbuf", [128, 8, 16], B2), "lh": ("sbuf", [128, 8, 128], B2),
-           "wd": ("sbuf", [128, 16, 128], B2),
-           "xa": ("sbuf", [128, 16, 128], B2),
-           "eq": ("sbuf", [128, 15, 32], B2), "ts": ("sbuf", [128, 4, 2, 4, 4], F4), "oi": ("sbuf", [128, 4, 2, 4], I4),
-           "pg": ("psum", [128, 4, 8, 16], F4), "pd": ("psum", [128, 32, 16], F4), "pq": ("psum", [128, 16, 32], F4),
-           "pf": ("psum", [128, 512], F4), "pn": ("psum", [128, 512], F4), "pr": ("psum", [128, 512], F4),
-           "px": ("psum", [128, 512], F4)}
-for _d, _l in ((B2, "ones:128 blk1:128 blk:128 eye2:128 zz:16 thb:1 j15:16 hl:64 rw:256 rv:256 zh1:256 zh2:256 z2:256 yv:256 nc:256"),
-               (F4, "p15:1 gp1:1 gp0:1 wf:2 wp:2 thc:1 mc:1 lu:32 lt:32 e16:16 e3:256 hc:256 rr:256 b8:64 sp:256 aa:256 hf:256 "
-                    "hd:256 ms:256 sc:256 sn:256 ac:1 nr:32 uu:32 u2:16 un:32 ur:16 xo:512"),
-               (I4, "pidx:1 p15i:1 gpi:1 wti:2 thi:1 lfi:16 qi:16 fi:16 ss:256 bi:64 ww:256 hh:256 ai:1 am:1 ri:16 rn:16"),
-               (U2, "li:256 lo:16 nl:16 rl:32 rt:32")):
+           "wd": ("sbuf", [128, 2048], B2),
+           "xa": ("sbuf", [128, 2048], B2),
+           "eq": ("sbuf", [128, 8, 16], B2), "er": ("sbuf", [128, 8, 16], B2),
+           "ts": ("sbuf", [128, 4, 2, 4, 4], F4), "oi": ("sbuf", [128, 4, 2, 4], I4), "oa": ("sbuf", [128, 4, 2, 4], I4)}
+PSUM = {"pg": [128, 4, 8, 16], "pd": [128, 16, 32], "pq": [128, 32, 16], "pa": [128, 512], "pb": [128, 512], "pr": [128, 512],
+        "ph": [128, 512], "px": [128, 512]}
+for _n in PSUM:
+    SCRATCH[_n] = ("psum", PSUM[_n], F4)
+for _d, _l in ((B2, "ones:128 blk1:128 blk:128 eye2:128 dm:128 dm1:128 n128:16 thb:1 j15:16 hl:32 pp:16 rw:256 zh1:256 zh2:256 z2:512 "
+                    "ys:256 nc:256 junk:16"),
+               (F4, "p15:1 lane:1 gp1:1 gp0:1 wf:2 wa:1 wp:2 wb:1 thc:1 th2:1 mc:1 lu:32 lt:32 e16:16 e240:240 aa:256 hf:240 "
+                    "hd:272 ms:272 sn:272 ac:1 at:1 nr:16 mv:256 nf:256 xo:512 co:512 c2:512 k8:8 k16:8 tk:8 tl:8 t6:6 oh:6 bm:6 sb:5 "
+                    "sm:1 sf:1 nb:1 jb:1 m120:1"),
+               (I4, "pidx:1 p15i:1 gpi:1 wti:2 thi:1 lfi:16 raw:64 r12:64 ss:256 bi:64 ww:256 hh:256 qq:16 q16:1 ri:16 rn:16 jm:128 jn:128"),
+               (U2, "li:256 lo:16 nl:16 rl:32 cl:32 rt:32")):
     for _x in _l.split():
         SCRATCH[_x.split(":")[0]] = ("sbuf", [128, int(_x.split(":")[1])], _d)
 for _t in range(5):
     SCRATCH["zi%d" % _t] = ("sbuf", [128, 4, 4, 16], B2)
     SCRATCH["zn%d" % _t] = ("sbuf", [128, 256], B2)
-    SCRATCH["fw%d" % _t] = ("sbuf", [128, 4, 2, 4], F4)
     SCRATCH["add%d" % _t] = ("sbuf", [128, 4, 2, 4], F4)
-SEMAPHORES = ["qv", "qt", "qs", "qg", "ls", "wp", "gd", "dc", "h1", "h2"] + ["za%d" % t for t in range(1, 5)] + \
-    ["fa%d" % t for t in range(1, 5)] + ["d%d" % k for k in range(12)]
+SCRATCH["fw"] = ("sbuf", [128, 4, 4, 2, 4], F4)
+SEMAPHORES = ["qv", "qt", "qs", "qg", "ls", "wp", "h1", "h2"] + ["za%d" % t for t in range(1, 5)] + \
+    ["fa%d" % t for t in range(1, 5)] + ["d%d" % k for k in range(16)]
 
 
 def state(g, T):
@@ -74,6 +80,8 @@ def note(S, reads, writes, ev):
 
 
 def op(S, q, fn, reads, writes):
+    writes = writes + [x for x in reads if x in PSUM]
+    reads = [x for x in reads if x not in PSUM]
     deps(S, q, reads, writes)
     sem = "q" + q
     S["count"][sem] = S["count"].get(sem, 0) + 1
@@ -83,21 +91,30 @@ def op(S, q, fn, reads, writes):
     note(S, reads, writes, (sem, S["count"][sem], clock))
 
 
-def dma(S, q, fn, reads, writes, sem=None, parts=1):
+def dma(S, q, fn, reads, writes):
     deps(S, q, reads, writes)
-    if sem is None:
-        sem = "d%d" % S["nd"]
-        S["nd"] += 1
-    for k in range(parts):
-        (fn(k) if parts > 1 else fn()).then_inc(S["T"].sem[sem], 16)
+    sem = "d%d" % S["nd"]
+    S["nd"] += 1
+    fn().then_inc(S["T"].sem[sem], 16)
     clock = dict(S["known"][q])
-    clock[sem] = S["count"][sem] = 16 * parts
-    note(S, reads, writes, (sem, 16 * parts, clock))
+    clock[sem] = S["count"][sem] = 16
+    note(S, reads, writes, (sem, 16, clock))
 
 
 def arrival(S, sem, val, writes):
     S["count"][sem] = val
     note(S, [], writes, (sem, val, {}))
+
+
+def weave(main, fill, first=0, each=1):
+    for _ in range(first):
+        if fill:
+            fill.pop(0)()
+    for f in main:
+        f()
+        for _ in range(each):
+            if fill:
+                fill.pop(0)()
 
 
 def rank_program(g, core, T, topo):
@@ -127,11 +144,27 @@ def rank_program(g, core, T, topo):
     def vt(o, x, y, p, reads, writes):
         v(lambda: V.tensor_tensor(o, x, y, p), reads, writes)
 
+    def vc(o, i, reads, writes):
+        v(lambda: V.tensor_copy(o, i), reads, writes)
+
+    def fill(ap, x, name):
+        v(lambda: V.memset(ap, x), [], [name])
+
     def copy(o, i, reads, writes, bias=0.0, scale=1.0):
-        s(lambda: C.activation(o, i, F.Copy, bias=bias, scale=scale), reads, writes)
+        f = F.Copy if isinstance(bias, float) else F.Identity
+        s(lambda: C.activation(o, i, f, bias=bias, scale=scale), reads, writes)
 
     def mm(out, lhsT, rhs, start, stop, reads, writes):
         op(S, "t", lambda: P.matmul(out, lhsT, rhs, start=start, stop=stop), reads, writes)
+
+    def iota(name, pattern, base, cm=0):
+        if SCRATCH[name][2] == I4:
+            op(S, "g", lambda: g.iota(T[name][:], pattern, base, cm), [], [name])
+        else:
+            op(S, "g", lambda: g.iota(T[name][:], pattern, base, cm, allow_small_or_imprecise_dtypes=True), [], [name])
+
+    def select(o, i, pattern, cmp, x, base, cm, reads, writes):
+        op(S, "g", lambda: g.affine_select(o, i, pattern, cmp, x, base, cm), reads, writes)
 
     def send(dst, out, src, sem, reads):
         deps(S, "g", reads, [])
@@ -139,223 +172,278 @@ def rank_program(g, core, T, topo):
         g.remote_dma(out, src, T.sem[sem], T.sem.ls, pid, rid, topo.mask(core, dst))
         S["count"]["ls"] = S["count"].get("ls", 0) + len(topo.engines(core, dst))
 
+    def lane_w(name, i):
+        return T[name][:, 128 * i:128 * i + 128]
+
     dma(S, "y", lambda: g.sync.dma_start(T.wti[:], T.wt[:]), [], ["wti"])
     dma(S, "s", lambda: C.dma_start(T.lfi[:], T.leaf[:]), [], ["lfi"])
     dma(S, "y", lambda: g.sync.dma_start(T.zi0[:], T.z0[:]), [], ["zi0"])
-    dma(S, "y", lambda: g.sync.dma_start(T.win[:, 16:CB], T.x0[:]), [], [("win", 16, CB)])
-    dma(S, "y", lambda i: g.sync.dma_start(T.win[i:128:16, CB + 16:NW], T.c0[:]), [], [("win", CB + 16, NW)], "dc", 16)
-    op(S, "g", lambda: g.iota(T.pidx[:], [[0, 1]], 0, 1), [], ["pidx"])
-    for n, x in [("ones", 1.0), ("thi", 0), ("lh", 0.0), ("add0", 1.0), ("wd", 0.0), ("zz", 0.0), ("e3", -256.0), ("hd", 0.0)] + \
-            [("fw%d" % t, 1.0) for t in range(4)]:
-        v(lambda: V.memset(T[n][:], x), [], [n])
-    v(lambda: V.memset(T.win[:, 0:16], 0.0), [], [("win", 0, 16)])
-    v(lambda: V.memset(T.win[:, CB:CB + 16], 0.0), [], [("win", CB, CB + 16)])
+    dma(S, "y", lambda: g.sync.dma_start(T.win[:, 16:NW], T.x0[:]), [], [("win", 16, NW)])
+    iota("pidx", [[0, 1]], 0, 1)
+    for n, x in [("ones", 1.0), ("thi", 0), ("wd", 0.0), ("lh", 0.0), ("add0", 64.0)]:
+        fill(T[n][:], x, n)
     dma(S, "s", lambda: C.dma_start(T.thi[0:128:16, :], T.th[:]), [], ["thi"])
-    op(S, "g", lambda: g.affine_select(T.blk1[:], T.ones[:], [[-16, 8], [0, 16]], A.is_ge, 0.0, 0, 1), ["ones"], ["blk1"])
-    op(S, "g", lambda: g.affine_select(T.blk[:], T.blk1[:], [[16, 8], [0, 16]], A.is_ge, 0.0, 15, -1), ["blk1"], ["blk"])
-    op(S, "g", lambda: g.affine_select(T.eye[:], T.ones[:], [[-1, 128]], A.is_equal, 0.0, 0, 1), ["ones"], ["eye"])
+
+    def zeros(a):
+        s(lambda: C.activation(T.cw[:, a:a + 2048], T.wd[:], F.Sigmoid, bias=T.m120[:, 0:1], scale=0.0), ["wd", "m120"], [("cw", a, a + 2048)])
+
+    fill(T.m120[:], -120.0, "m120")
+    select(T.blk1[:], T.ones[:], [[-16, 8], [0, 16]], A.is_ge, 0.0, 0, 1, ["ones"], ["blk1"])
+    select(T.blk[:], T.blk1[:], [[16, 8], [0, 16]], A.is_ge, 0.0, 15, -1, ["blk1"], ["blk"])
+    select(T.eye[:], T.ones[:], [[-1, 128]], A.is_equal, 0.0, 0, 1, ["ones"], ["eye"])
     vs(T.p15i[:], T.pidx[:], 15, None, A.bitwise_and, None, ["pidx"], ["p15i"])
     vs(T.gpi[:], T.pidx[:], 4, 1, A.arith_shift_right, A.bitwise_and, ["pidx"], ["gpi"])
-    v(lambda: V.tensor_copy(T.p15[:], T.p15i[:]), ["p15i"], ["p15"])
-    v(lambda: V.tensor_copy(T.gp1[:], T.gpi[:]), ["gpi"], ["gp1"])
+    for n, pattern, base, cm in [("jm", [[1, 128]], 128, -1), ("k8", [[1, 8]], 1, 0), ("k16", [[-1, 8]], 15, 0), ("t6", [[1, 6]], 0, 0),
+                                 ("e16", [[-1, 16]], 15, 0), ("e240", [[-1, 240]], 255, 0)]:
+        iota(n, pattern, base, cm)
+    for gr in range(8):
+        copy(T.wd[:, 16 * gr::129], T.blk[:, 16 * gr:16 * gr + 16], ["blk"], ["wd"] if gr == 0 else [("wd", gr, gr + 1)])
+    vc(T.gp1[:], T.gpi[:], ["gpi"], ["gp1"])
     vs(T.gp0[:], T.gpi[:], -1.0, 1.0, A.mult, A.add, ["gpi"], ["gp0"])
-    for i in range(16):
-        copy(T.wd[:, i, i::16], T.blk[:, 0::16], ["blk", "wd"], [("wd", i, i + 1)])
-    v(lambda: V.tensor_copy(T.wf[:], T.wti[:]), ["wti"], ["wf"])
-    for gs in range(2):
-        for c0 in range(4):
-            vs(T.lh[:, gs * 4 + c0, c0::32], T.blk[:, 16 * gs::32], T.wf[:, 0:1], 2.0, A.mult, A.mult,
-               ["blk", "wf"], [("lh", 2 * (gs * 4 + c0), 2 * (gs * 4 + c0) + 1)])
+    vs(T.wa[:], T.wti[:, 0:1], 128.0, None, A.mult, None, ["wti"], ["wa"])
+    vc(T.wf[:], T.wti[:], ["wti"], ["wf"])
+    vs(T.neye[:], T.eye[:], -1.0, None, A.mult, None, ["eye"], ["neye"])
+    for q in range(8):
+        copy(T.lh[:, q, q % 4::32], T.blk[:, 16 * (q // 4)::32], ["blk", "wa"], [("lh", 2 * q, 2 * q + 1)], scale=T.wa[:, 0:1])
     vs(T.lu[:, 0:16], T.lfi[:], T.gp0[:, 0:1], None, A.mult, None, ["lfi", "gp0"], [("lu", 0, 16)])
     vs(T.lu[:, 16:32], T.lfi[:], T.gp1[:, 0:1], None, A.mult, None, ["lfi", "gp1"], [("lu", 16, 32)])
     v(lambda: V.transpose(T.lt[:], T.lu[:]), ["lu"], ["lt"])
-    vt(T.fi[:], T.lt[:, 0:16], T.lt[:, 16:32], A.add, ["lt"], ["fi"])
+    vt(T.add0[:, :, 1, :], T.lt[:, 0:16], T.lt[:, 16:32], A.add, ["lt"], ["add0"])
     send(nxt, T.wp[:], T.wf[:], "wp", ["wf"])
     arrival(S, "wp", E, ["wp"])
+    for k in range(1, 9):
+        select(T.sh[:, k - 1, :, k:16], T.neye[:, :, k:16], [[-16, 8], [-1, 16 - k]], A.not_equal, 1.0, k - k, 1,
+               ["neye"], [("sh", 2 * k, 2 * k + 1)])
+        select(T.sh[:, k - 1, :, 0:k], T.neye[:, :, 0:k], [[-16, 8], [-1, k]], A.not_equal, 1.0, k - 16, 1,
+               ["neye"], [("sh", 2 * k + 1, 2 * k + 2)])
 
-    def rest_one():
-        vs(T.neye[:], T.eye[:], -1.0, None, A.mult, None, ["eye"], ["neye"])
-        vs(T.eye2[:], T.eye[:], 2.0, None, A.mult, None, ["eye"], ["eye2"])
-        mm(T.pd[:, 0:16, 0], T.blk[:], T.zz[:], True, True, ["blk", "zz"], ["pd"])
-        op(S, "g", lambda: g.iota(T.e16[:], [[16, 16]], 3840, 0, allow_small_or_imprecise_dtypes=True), [], ["e16"])
-        op(S, "g", lambda: g.iota(T.hc[:], [[16384, 16], [0, 16]], 16400, 0, allow_small_or_imprecise_dtypes=True), [], ["hc"])
-        for k in range(1, 16):
-            op(S, "g", lambda: g.affine_select(T.sh[:, k - 1, :, k:16], T.neye[:, :, k:16], [[-16, 8], [-1, 16 - k]], A.not_equal,
-                                               1.0, 0, 1), ["neye"], [("sh", 2 * k, 2 * k + 1)])
+    rest = [lambda: vc(T.p15[:], T.p15i[:], ["p15i"], ["p15"]),
+            lambda: vs(T.jn[:], T.jm[:], 15, None, A.bitwise_and, None, ["jm"], ["jn"]),
+            lambda: vs(T.tk[:], T.k8[:], T.p15[:, 0:1], None, A.is_gt, None, ["k8", "p15"], ["tk"]),
+            lambda: vs(T.dm[:], T.jn[:], 1.0, None, A.add, None, ["jn"], ["dm"]),
+            lambda: vt(T.tl[:], T.tk[:], T.k16[:], A.mult, ["tk", "k16"], ["tl"]),
+            lambda: vs(T.oh[:], T.t6[:], T.p15[:, 0:1], None, A.is_equal, None, ["t6", "p15"], ["oh"]),
+            lambda: vt(T.dm1[:], T.dm[:], T.blk[:], A.mult, ["dm", "blk"], ["dm1"]),
+            lambda: vs(T.tk[:], T.tl[:], 1.0, None, A.add, None, ["tl"], ["tk"]),
+            lambda: vs(T.bm[:], T.oh[:], 240.0, -120.0, A.mult, A.add, ["oh"], ["bm"]),
+            lambda: vs(T.sb[:], T.oh[:, 1:6], T.oh[:, 0:1], -BIG, A.subtract, A.mult, ["oh"], ["sb"]),
+            lambda: vs(T.sm[:], T.oh[:, 0:1], 240.0, None, A.mult, None, ["oh"], ["sm"]),
+            lambda: vs(T.sf[:], T.oh[:, 0:1], -240.0, None, A.mult, None, ["oh"], ["sf"]),
+            lambda: vs(T.nb[:], T.oh[:, 0:1], 0.25 - BIG, None, A.mult, None, ["oh"], ["nb"]),
+            lambda: vs(T.lane[:], T.p15[:], 4080.0, None, A.add, None, ["p15"], ["lane"]),
+            lambda: vs(T.eye2[:], T.eye[:], 2.0, None, A.mult, None, ["eye"], ["eye2"]),
+            lambda: fill(T.win[:, 0:16], 0.0, ("win", 0, 16)),
+            lambda: fill(T.hd[:], 0.0, "hd"), lambda: fill(T.fw[:], 64.0, "fw")]
 
-    def rest_two():
-        vs(T.e3[:, 15::16], T.e16[:], T.p15[:, 0:1], None, A.add, None, ["e16", "p15"], ["e3"])
-        v(lambda: V.tensor_copy(T.thb[:], T.thi[:]), ["thi"], ["thb"])
+    def last_constants():
+        zeros(4112)
+        zeros(6160)
+        op(S, "g", lambda: g.iota(T.cw[:, 0:1536], [[0, 1536]], 0, 0, allow_small_or_imprecise_dtypes=True), [], [("cw", 0, 1536)])
+        fill(T.cw[:, 1536:4112], 0.0, ("cw", 1536, 4112))
+        dma(S, "g", lambda: g.dma_start(T.cw[0:128:16, 16:NW], T.c0[:]), [], ["cw"])
+        vs(T.ph[:, 256:496], T.e240[:], BIG, 16.0, A.mult, A.add, ["e240"], ["ph"])
+        for k in range(8):
+            vs(T.ro[:, k, :], T.dm1[:], T.tk[:, k:k + 1], -BIG, A.is_equal, A.mult, ["dm1", "tk"], [("ro", k, k + 1)])
+
+    def under_first_gathers():
+        fill(T.n128[:], -128.0, "n128")
+        fill(T.jb[:], 0.5 - 240 * BIG, "jb")
+        fill(T.pd[:, :, 0], 0.0, "pd")
+        fill(T.pd[:, :, 16], 1000.0, "pd")
+        vc(T.thb[:], T.thi[:], ["thi"], ["thb"])
         mm(T.px[:, 0:1], T.blk[:], T.thb[:], True, True, ["blk", "thb"], ["px"])
-        v(lambda: V.tensor_copy(T.thc[:], T.px[:, 0:1]), ["px"], ["thc"])
+        vs(T.hd[:, 16::17], T.e16[:], BIG, T.p15[:, 0:1], A.mult, A.add, ["e16", "p15"], [("hd", 16, 17)])
+        vc(T.thc[:], T.px[:, 0:1], ["px"], ["thc"])
+        vs(T.th2[:], T.px[:, 0:1], 1024.0, None, A.add, None, ["px"], ["th2"])
 
-    def lhb():
-        for gs in range(2):
-            for c0 in range(4):
-                q = gs * 4 + c0
-                copy(T.lh[:, q, 16 + c0::32], T.blk[:, 16 * gs::32], ["blk", "wp"], [("lh", 2 * q + 1, 2 * q + 2)], scale=T.wp[:, 1:2])
+    def sums(t):
+        zi = "zi%d" % t
+        for q in range(8):
+            mm(T.pg[:, :, q // 4, :], T.lh[:, q, :], T[zi][:, :, q % 4, :], q % 4 == 0, q % 4 == 3,
+               [("lh", 2 * q, 2 * q + (2 if t else 1)), zi], ["pg"])
 
     def chain(t):
-        zi, ad = "zi%d" % t, "add%d" % t
+        ad = "add%d" % t
 
-        def sums():
-            copy(T.z2[:], T[zi][:], [zi], ["z2"])
-            for gs in range(2):
-                for c0 in range(4):
-                    q = gs * 4 + c0
-                    mm(T.pg[:, :, gs, :], T.lh[:, q, :], T[zi][:, :, c0, :], c0 == 0, c0 == 3,
-                       [("lh", 2 * q, 2 * q + (2 if t else 1)), zi], ["pg"])
-            v(lambda: V.transpose(T.ts[:], T.pg[:, :, 0:2, :]), ["pg"], ["ts"])
+        def down(a, n, src, name, has):
+            c = 2452.0 - has * 2452.0 / 2 ** n - 0.5 + 0.5 / 2 ** n
+            return lambda: vs(T.ss[:, a:a + 64], src, 1.0 / 2 ** n, c, A.mult, A.add, [name], [("ss", a, a + 64)])
 
-        def rdoub():
-            vs(T.rr[:, 0:16], T.qi[:], 296.0, None, A.add, None, ["qi"], [("rr", 0, 16)])
+        def rr0():
+            vs(T.ph[:, 0:16], T.oa[:, :, 0, :], 1.0 / 64, 296.0, A.mult, A.add, ["oa"], ["ph"])
             for n in (16, 32, 64, 128):
-                copy(T.rr[:, n:2 * n], T.rr[:, 0:n], [("rr", 0, n)], [("rr", n, 2 * n)])
+                copy(T.ph[:, n:2 * n], T.ph[:, 0:n], [], ["ph"])
+            copy(T.pp[:], T.ph[:, 0:16], ["ph"], ["pp"], bias=-148.5, scale=0.5)
 
-        def sdoub(k, n):
-            return lambda: vs(T.ss[:, n:2 * n], T.ss[:, 0:n], k, None, A.arith_shift_right, None, [("ss", 0, n)], [("ss", n, 2 * n)])
-
-        def fwd():
-            fw, to = "fw%d" % t, "add%d" % (t + 1)
-            vs(T[fw][:, :, 1, :], T.fi[:], 8.0, None, A.mult, None, ["fi"], [fw])
-            send(nxt, T[to][:], T[fw][:], "fa%d" % (t + 1), [fw])
-            arrival(S, "fa%d" % (t + 1), E, [to])
-
-        s0 = ("ss", 0, 64)
-        out = [sums, lambda: vt(T.oi[:], T.ts[:, :, :, 0, :], T[ad][:], A.add, ["ts", ad], ["oi"])]
-        if t:
-            out.append(lambda: vs(T.fi[:], T.oi[:, :, 1, :], 32767, None, A.bitwise_and, None, ["oi"], ["fi"]))
-        out += [lambda: vs(T.qi[:], T.oi[:, :, 0, :], 511, None, A.bitwise_and, None, ["oi"], ["qi"]),
-                lambda: vs(T.ss[:, 0:16], T.fi[:], 32768.0, None, A.add, None, ["fi"], [("ss", 0, 16)]),
-                rdoub, sdoub(1, 16), sdoub(2, 32), sdoub(4, 64), sdoub(8, 128)]
-        if t < 4:
-            out.append(fwd)
-        out += [lambda: vs(T.bi[:], T.ss[:, 0:64], 4096, None, A.bitwise_and, None, [s0], ["bi"]),
-                lambda: vs(T.ss[:, 0:64], T.ss[:, 0:64], 4095, None, A.bitwise_and, None, [s0], [s0]),
-                lambda: vs(T.b8[:], T.bi[:], 8.0, None, A.mult, None, ["bi"], ["b8"]),
-                lambda: vs(T.sp[:], T.ss[:], 2452.0, None, A.add, None, ["ss"], ["sp"]),
-                lambda: vt(T.aa[:], T.sp[:], T.rr[:], A.mult, ["sp", "rr"], ["aa"]),
-                lambda: vt(T.aa[:, 0:64], T.aa[:, 0:64], T.b8[:], A.add, ["aa", "b8"], [("aa", 0, 64)]),
+        return [lambda: v(lambda: V.transpose(T.ts[:], T.pg[:, :, 0:2, :]), ["pg"], ["ts"]),
+                lambda: vt(T.oi[:], T.ts[:, :, :, 0, :], T[ad][:], A.add, ["ts", ad], ["oi"]),
+                lambda: vs(T.oa[:], T.oi[:], 32767, None, A.bitwise_and, None, ["oi"], ["oa"]),
+                rr0,
+                lambda: vs(T.raw[:, 48:64], T.oa[:, :, 1, :], 32768.0, None, A.add, None, ["oa"], [("raw", 48, 64)]),
+                lambda: vs(T.raw[:, 32:48], T.raw[:, 48:64], 1, None, A.arith_shift_right, None, [("raw", 48, 64)], [("raw", 32, 48)]),
+                lambda: vs(T.raw[:, 0:32], T.raw[:, 32:64], 2, None, A.arith_shift_right, None, [("raw", 32, 64)], [("raw", 0, 32)]),
+                down(128, 4, T.raw[:], "raw", 0),
+                lambda: vs(T.r12[:], T.raw[:], 4095, None, A.bitwise_and, None, ["raw"], ["r12"]),
+                down(64, 8, T.raw[:], "raw", 0),
+                down(0, 8, T.ss[:, 128:192], ("ss", 128, 192), 1),
+                lambda: vs(T.ss[:, 192:256], T.r12[:], 2452.0, None, A.add, None, ["r12"], [("ss", 192, 256)]),
+                lambda: vs(T.bi[:], T.raw[:], 4096, None, A.bitwise_and, None, ["raw"], ["bi"]),
+                lambda: vt(T.aa[:], T.ss[:], T.ph[:, 0:256], A.mult, ["ss", "ph"], ["aa"]),
                 lambda: vs(T.ww[:], T.aa[:], 0.125, -91030.9375, A.mult, A.add, ["aa"], ["ww"]),
+                lambda: vt(T.ww[:, 192:256], T.ww[:, 192:256], T.bi[:], A.add, ["ww", "bi"], [("ww", 192, 256)]),
                 lambda: vs(T.hh[:], T.ww[:], 8191, None, A.bitwise_and, None, ["ww"], ["hh"]),
                 lambda: vs(T.li[:], T.hh[:], 16.0, None, A.add, None, ["hh"], ["li"])]
-        return out
 
-    def gather(t):
-        ends = {5: (10, 16), 10: (5, 10), 14: (1, 5)}
-        for k in [15] + list(range(15)):
-            kk = 15 - k
-            d = ("diff", 256 * kk, 256 * kk + 256)
-            vt(T.diff[:, 256 * kk:256 * kk + 256], T.win[:, 0:CB].indirect(T.li[:, 16 * k:16 * k + 16]), T.z2[:], A.subtract,
-               [("win", 0, CB), "li", "z2"], [d])
-            if k < 15:
-                s(lambda: C.activation(T.ad[:, :, kk], T.diff[:, 256 * kk:256 * kk + 256], F.Abs), [d], [("ad", kk, kk + 1)])
+    def twice(t):
+        for h in range(2):
+            copy(T.z2[:, 256 * h:256 * h + 256], T["zi%d" % t][:], ["zi%d" % t], [("z2", h, h + 1)])
+
+    def sigmoids(vals, lst):
+        return [lambda c=c: s(lambda: C.activation(T.cw[:, 0:NW].indirect(T[lst][:, 2 * c:2 * c + 1]), T[vals][:, 16 * c:16 * c + 16],
+                                                   F.Sigmoid), [lst, vals], ["cw"]) for c in range(16)]
+
+    def gather(t, late):
+        marks = sigmoids("mv", "rt")
+        for k in range(8):
+            mm(T.pq[:, 8 + k, :], T.sh[:, k, :, :], T.pp[:], True, True, [("sh", 2 * k + 2, 2 * k + 4), "pp"], ["pq"])
+        while late:
+            late.pop(0)()
+        for a, b in [(0, 2), (2, 4), (4, 6), (6, 8), (8, 10), (10, 12), (12, 14), (14, 15), (15, 16)]:
+            vt(T.diff[:, 256 * a:256 * b], T.win[:, 0:NW].indirect(T.li[:, 16 * a:16 * b]), T.z2[:, 0:256 * (b - a)], A.subtract,
+               ["win", "li", "z2"], [("diff", a, b)])
+            for k in range(max(a, 1), b):
+                s(lambda: C.activation(T.ad[:, :, k], T.diff[:, 256 * k:256 * k + 256], F.Abs), [("diff", k, k + 1)], [("ad", k, k + 1)])
+                if k in (4, 8, 12, 15):
+                    k0 = k - 3 + k // 15
+                    for i in range(16):
+                        mm(T.pd[:, :, k0:k + 1], lane_w("wd", i), T.ad[:, i::16, k0:k + 1], i == 0, i == 15,
+                           ["wd", ("ad", k0, k + 1)], ["pd"])
+            if a == (0 if t else 6):
+                copy(T.mv[:], T.cw[:, 0:NW].indirect(T.li[:, 0:16]), ["cw", "li", "sm", "bm"], ["mv"], bias=T.bm[:, t + 1:t + 2],
+                     scale=T.sm[:, 0:1])
+            if a == 0:
+                mm(T.pr[:, 0:256], T.eye2[:], T.z2[:, 0:256], True, False, ["eye2", "z2"], ["pr"])
+                mm(T.pr[:, 0:256], T.eye[:], T.diff[:, 0:256], False, True, ["eye", ("diff", 0, 1)], ["pr"])
+                vs(T.er[:], T.pq[:, 8:16, :], 0.0, None, A.is_equal, None, ["pq"], ["er"])
+                for k in range(8):
+                    mm(T.pa[:, 0:16], T.ro[:, k, :], T.er[:, k, :], k == 0, k == 7, ["ro", "er"], ["pa"])
+                vt(T.hf[:], T.hh[:, 16:256], T.ph[:, 256:496], A.add, ["hh", "ph"], ["hf"])
+                for m in range(1, 16):
+                    select(T.hd[:, m::17], T.hf[:, 16 * m - 16:16 * m], [[0, 16]], A.is_gt, 0.0, 1, 0, ["hf"], [("hd", m, m + 1)])
                 if t == 0:
-                    copy(T.sh[:, k, :, 0:k + 1], T.neye[:, :, 0:k + 1], ["neye"], [("sh", 2 * k + 3, 2 * k + 4)])
-            if k == 7 and t == 0:
-                rest_two()
-            if k in ends:
-                a, b = ends[k]
-                for i in range(16):
-                    mm(T.pd[:, 0:16, a:b], T.wd[:, i, :], T.ad[:, i::16, a:b], i == 0, i == 15,
-                       [("wd", i, i + 1), ("ad", a, b)], ["pd"])
-            if k == 1:
-                vt(T.hf[:], T.hh[:], T.hc[:], A.add, ["hh", "hc"], ["hf"])
-                vs(T.nr[:, 16:32], T.hh[:, 240:256], 16.0, None, A.add, None, ["hh"], [("nr", 16, 32)])
-                for m in range(15):
-                    op(S, "g", lambda: g.affine_select(T.hd[:, 15 - m::16], T.hf[:, 16 * m:16 * m + 16], [[0, 16]], A.is_gt, 0.0, 1, 0),
-                       ["hf"], [("hd", 15 - m, 16 - m)])
-            if k == 6:
-                mm(T.pr[:, 0:256], T.eye[:], T.diff[:, 0:256], True, False, ["eye", ("diff", 0, 256)], ["pr"])
-                mm(T.pr[:, 0:256], T.eye2[:], T.z2[:], False, True, ["eye2", "z2"], ["pr"])
+                    under_first_gathers()
+            if a == 2:
+                copy(T.rw[:], T.pr[:, 0:256], ["pr"], ["rw"], bias=127.8, scale=0.5)
+                vt(T.nr[:], T.hh[:, 0:16], T.pa[:, 0:16], A.add, ["hh", "pa"], ["nr"])
+                if t < 4:
+                    fw, to = ("fw", t, t + 1), "add%d" % (t + 1)
+                    vs(T.fw[:, t, :, 1, :], T.oa[:, :, 1, :], 8.0, None, A.mult, None, ["oa"], [fw])
+                    send(nxt, T[to][:], T.fw[:, t, :, :, :], "fa%d" % (t + 1), [fw])
+                    arrival(S, "fa%d" % (t + 1), E, [to])
+                if t in (2, 3):
+                    send(cores[(rank - t + 1) % N], T["zh%d" % (t - 1)][:], T["zn%d" % (t - 1)][:], "h%d" % (t - 1), ["zn%d" % (t - 1)])
+                vs(T.rt[:, 0::2], T.nr[:], 16.0, T.p15[:, 0:1], A.add, A.max, ["nr", "p15"], ["rt"])
+            if a == 4 and t:
+                vs(T.q16[:], T.ac[:], 1.0 / 32, 63.53125, A.mult, A.add, ["ac"], ["q16"])
+            if a == 6 and t:
+                vs(T.mc[:], T.q16[:], -16.0, T.at[:, 0:1], A.mult, A.add, ["q16", "at"], ["mc"])
+            if (4 if t else 8) <= a < 14:
+                marks.pop(0)()
+        while marks:
+            marks.pop(0)()
 
-    def answer(t):
+    def roots():
+        return [lambda c=c: vt(T.win[:, 0:NW].indirect(T.rt[:, 2 * c:2 * c + 1]), T.rw[:, 16 * c:16 * c + 16], T.n128[:], A.add,
+                               ["rt", "rw", "n128"], ["win"]) for c in range(15, -1, -1)]
+
+    def answer(t, rs):
         zn, mc = "zn%d" % t, "mc" if t else "thc"
-        vs(T.ms[:], T.pd[:, 0:16, :], T[mc][:, 0:1], None, A.is_gt, None, ["pd", mc], ["ms"])
-        v(lambda: V.tensor_tensor_scan(T.sc[:], T.ms[:], T.e3[:], 0.0, A.mult, A.add), ["ms", "e3"], ["sc"])
-        v(lambda: V.tensor_copy(T.lo[:], T.sc[:, 15::16]), ["sc"], ["lo"])
-        s(lambda: C.activation(T[zn][:], T.diff[:, 0:4096].indirect(T.lo[:]), F.Abs), ["diff", "lo"], [zn])
-        if t < 4:
-            send(nxt, T["zi%d" % (t + 1)][:], T[zn][:], "za%d" % (t + 1), [zn])
-            arrival(S, "za%d" % (t + 1), E, ["zi%d" % (t + 1)])
-        if t in (1, 2):
-            send(cores[(rank - t) % N], T["zh%d" % t][:], T[zn][:], "h%d" % t, [zn])
-        if t in (0, 4):
-            dma(S, "y", lambda: g.sync.dma_start(T.zs[:, 256 * t:256 * t + 256], T[zn][:]), [zn], [])
 
-    def update(t):
-        n16 = ("nr", 0, 16)
-        v(lambda: V.tensor_tensor_scan(T.sn[:], T.hd[:], T.ms[:], 0.0, A.max, A.mult), ["hd", "ms"], ["sn"])
-        v(lambda: V.tensor_copy(T.ri[:], T.sn[:, 15::16]), ["sn"], ["ri"])
-        vt(T.yv[:], T.diff[:, 0:4096].indirect(T.lo[:]), T.z2[:], A.add, ["diff", "lo", "z2"], ["yv"])
+        def new_z():
+            vs(T.lo[:], T.qq[:], -16.0, T.lane[:, 0:1], A.mult, A.add, ["qq", "lane"], ["lo"])
+            s(lambda: C.activation(T[zn][:], T.diff[:, 0:4096].indirect(T.lo[:]), F.Abs), ["diff", "lo"], [zn])
+            if t < 4:
+                send(nxt, T["zi%d" % (t + 1)][:], T[zn][:], "za%d" % (t + 1), [zn])
+                arrival(S, "za%d" % (t + 1), E, ["zi%d" % (t + 1)])
+            if t in (0, 4):
+                dma(S, "y", lambda: g.sync.dma_start(T.zs[:, 256 * t:256 * t + 256], T[zn][:]), [zn], [])
+
+        weave([lambda: vs(T.ms[:], T.pd[:, :, 0:17], T[mc][:, 0:1], None, A.is_gt, None, ["pd", mc], ["ms"]),
+               lambda: v(lambda: V.tensor_tensor_scan(T.sn[:], T.hd[:], T.ms[:], 0.0, A.max, A.mult), ["hd", "ms"], ["sn"]),
+               lambda: vs(T.qq[:], T.sn[:, 16::17], 1.0 / BIG, -0.25, A.mult, A.add, ["sn"], ["qq"])], rs, 9, 0)
+        vc(T.ri[:], T.sn[:, 16::17], ["sn"], ["ri"])
+        new_z()
+
+    def update(t, rs):
+        zi = "zi%d" % t
         vs(T.rn[:], T.ri[:], 16383, None, A.bitwise_and, None, ["ri"], ["rn"])
-        if t < 4:
-            vs(T.j15[:], T.sc[:, 15::16], 255.5, None, A.is_lt, None, ["sc"], ["j15"])
-        vs(T.nr[:, 0:16], T.rn[:], T.p15[:, 0:1], None, A.max, None, ["rn", "p15"], [n16])
-        v(lambda: V.tensor_copy(T.hl[:, 0:32], T.nr[:]), ["nr"], [("hl", 0, 32)])
-        v(lambda: V.tensor_copy(T.nl[:], T.nr[:, 0:16]), [n16], ["nl"])
-        vt(T.hl[:, 32:64], T.nr[:], T.hl[:, 0:32], A.subtract, ["nr", ("hl", 0, 32)], [("hl", 32, 64)])
-        copy(T.nc[:], T.win[:, CB:NW].indirect(T.nl[:]), [("win", CB, NW), "nl"], ["nc"], bias=1.0, scale=-1.0)
-        copy(T.vals[:, :, 0:16], T.yv[:], ["yv"], [("vals", 0, 1)])
-        copy(T.vals[:, :, 16:32], T.nc[:], ["nc"], [("vals", 1, 2)])
-        copy(T.rw[:], T.pr[:, 0:256], ["pr"], ["rw"], bias=127.8, scale=0.5)
-        copy(T.rv[:], T.rw[:], ["rw"], ["rv"], bias=-128.0)
-        if t == 0:
-            lhb()
-        if t == 1:
-            copy(T.xa[:], T.wd[:], ["wd", "wf"], ["xa"], scale=T.wf[:, 0:1])
-        for k in range(15):
+        weave([lambda: vc(T.hl[:, 0:16], T.rn[:], ["rn"], [("hl", 0, 16)]),
+               lambda: vc(T.nl[:], T.rn[:], ["rn"], ["nl"]),
+               lambda: vt(T.hl[:, 16:32], T.rn[:], T.hl[:, 0:16], A.subtract, ["rn", ("hl", 0, 16)], [("hl", 16, 32)])], rs, 1, 0)
+        copy(T.nc[:], T.cw[:, 0:NW].indirect(T.nl[:]), ["cw", "nl", "sb", "nb"], ["nc"], bias=T.nb[:, 0:1], scale=T.sb[:, t:t + 1])
+        for k in range(8):
             for h in range(2):
-                mm(T.pq[:, k, :], T.sh[:, k, :, :], T.hl[:, 32 * h:32 * h + 32], h == 0, h == 1,
-                   [("sh", 2 * k + 2, 2 * k + 4), ("hl", 32 * h, 32 * h + 32)], ["pq"])
+                mm(T.pq[:, k, :], T.sh[:, k, :, :], T.hl[:, 16 * h:16 * h + 16], h == 0, h == 1,
+                   ["sh", ("hl", 16 * h, 16 * h + 16)], ["pq"])
+        copy(T.ys[:], T.diff[:, 0:4096].indirect(T.lo[:]), ["diff", "lo"], ["ys"])
+        copy(T.nf[:], T.cw[:, 0:NW].indirect(T.nl[:]), ["cw", "nl", "sf", "bm"], ["nf"], bias=T.bm[:, 0:1], scale=T.sf[:, 0:1])
+        if t < 4:
+            s(lambda: C.activation(T.j15[:], T.sn[:, 16::17], F.Sign, bias=T.jb[:, 0:1]), ["sn", "jb"], ["j15"])
+        while rs:
+            rs.pop(0)()
+        vs(T.eq[:], T.pq[:, 0:8, :], 0.0, None, A.is_equal, None, ["pq"], ["eq"])
+        for b in ("pa", "pb"):
+            for h in range(2):
+                mm(T[b][:, 0:16], T.eye[:], T.hl[:, 16 * h:16 * h + 16], h == 0, False, ["eye", "hl"], [b])
+            for i in range(16 if b == "pa" else 0):
+                mm(T.pa[:, 0:16], lane_w("wd", i), T.nc[:, i::16], False, False, ["wd", "nc"], ["pa"])
+            for k in range(8):
+                mm(T[b][:, 0:16], T.ro[:, k, :], T.eq[:, k, :], False, k == 7, ["ro", "eq"], [b])
+        if t == 0:
+            for q in range(8):
+                copy(T.lh[:, q, 16 + q % 4::32], T.blk[:, 16 * (q // 4)::32], ["blk", "wp"], [("lh", 2 * q + 1, 2 * q + 2)],
+                     scale=T.wp[:, 1:2])
         if t < 4:
             mm(T.px[:, 0:16], T.ones[:], T.j15[:], True, True, ["ones", "j15"], ["px"])
-        vs(T.eq[:], T.pq[:, 0:15, :], 0.0, None, A.is_equal, None, ["pq"], ["eq"])
-        for i in range(16):
-            mm(T.pn[:, 0:16], T.wd[:, i, :], T.nc[:, i::16], i == 0, i == 15, ["wd", "nc"], ["pn"])
-        for k in range(15):
-            mm(T.pf[:, 0:32], T.eye[:], T.eq[:, k, :], k == 0, k == 14, ["eye", "eq"], ["pf"])
-        if t < 4:
-            v(lambda: V.tensor_reduce(T.ac[:], T.px[:, 0:16], AxisListType.X, A.add), ["px"], ["ac"])
-            v(lambda: V.tensor_copy(T.ai[:], T.ac[:]), ["ac"], ["ai"])
-            vs(T.am[:], T.ai[:], 15, None, A.bitwise_and, None, ["ai"], ["am"])
-            vs(T.mc[:], T.am[:], T.thc[:, 0:1], None, A.add, None, ["am", "thc"], ["mc"])
-        vs(T.u2[:], T.pn[:, 0:16], 0.5, None, A.is_lt, None, ["pn"], ["u2"])
-        vs(T.uu[:], T.pf[:, 0:32], 0.5, None, A.is_lt, None, ["pf"], ["uu"])
-        vt(T.un[:], T.uu[:], T.nr[:], A.mult, ["uu", "nr"], ["un"])
-        vt(T.ur[:], T.un[:, 0:16], T.u2[:], A.mult, ["un", "u2"], ["ur"])
-        vs(T.rl[:, 1::2], T.un[:, 0:16], T.p15[:, 0:1], float(CB), A.max, A.add, ["un", "p15"], [("rl", 1, 2)])
-        vs(T.rt[:, 0::2], T.un[:, 16:32], T.p15[:, 0:1], None, A.max, None, ["un", "p15"], ["rt"])
-        vs(T.rl[:, 0::2], T.ur[:], T.p15[:, 0:1], None, A.max, None, ["ur", "p15"], [("rl", 0, 1)])
-        return [lambda c=c: v(lambda: V.tensor_copy(T.win[:, 0:NW].indirect(T.rl[:, 2 * c:2 * c + 2]), T.vals[:, c, :]),
-                              ["rl", "vals"], ["win"]) for c in range(15, -1, -1)] + \
-               [lambda c=c: v(lambda: V.tensor_copy(T.win[:, 0:CB].indirect(T.rt[:, 2 * c:2 * c + 1]), T.rv[:, 16 * c:16 * c + 16]),
-                              ["rt", "rv"], [("win", 0, CB)]) for c in range(15, -1, -1)]
+            s(lambda: C.activation(T.junk[:], T.px[:, 0:16], F.Copy, accum_out=T.ac[:]), ["px"], ["junk", "ac"])
+            copy(T.at[:], T.ac[:], ["ac", "th2"], ["at"], bias=T.th2[:, 0:1], scale=0.5)
+        else:
+            vs(T.xa[:], T.wd[:], T.wf[:, 0:1], None, A.mult, None, ["wd", "wf"], ["xa"])
+        vs(T.rl[:, 0::2], T.pa[:, 0:16], T.p15[:, 0:1], None, A.max, None, ["pa", "p15"], ["rl"])
+        named = [lambda c=c: vt(T.win[:, 0:NW].indirect(T.rl[:, 2 * c:2 * c + 1]), T.ys[:, 16 * c:16 * c + 16], T[zi][:, c // 4, c % 4, :],
+                                A.add, ["rl", "ys", zi], ["win"]) for c in range(15, -1, -1)]
+        named.pop(0)()
+        named.pop(0)()
+        named.pop(0)()
+        vs(T.cl[:, 0::2], T.pb[:, 0:16], T.p15[:, 0:1], None, A.max, None, ["pb", "p15"], ["cl"])
+        return named, sigmoids("nf", "cl")
 
-    for f in chain(0):
-        f()
-    rest_one()
+    twice(0)
+    sums(0)
+    weave(chain(0), rest)
+    last_constants()
+    late = []
     for t in range(5):
-        gather(t)
-        answer(t)
-        sc = update(t)
-        ch = chain(t + 1) if t < 4 else []
-        for _ in range(6):
-            sc.pop(0)()
-        while ch or sc:
-            if ch:
-                ch.pop(0)()
-            for _ in range(2 if len(sc) > len(ch) else 1):
-                if sc:
-                    sc.pop(0)()
+        gather(t, late)
+        rs = roots()
+        answer(t, rs)
+        named, late = update(t, rs)
+        if t < 4:
+            weave([], late, 4)
+            twice(t + 1)
+            sums(t + 1)
+            weave(chain(t + 1), named)
+    weave(late, named)
     for q in range(16):
-        mm(T.px[:], T.xa[:, q, :], T.win[:, 16 + 512 * q:528 + 512 * q], q == 0, q == 15, ["xa", ("win", 0, CB)], ["px"])
-    v(lambda: V.tensor_copy(T.xo[:], T.px[:]), ["px"], ["xo"])
-    dma(S, "g", lambda: g.dma_start(T.cs[:], T.win[0:128:16, CB + 16:NW]), [("win", CB, NW)], [], "gd")
+        mm(T.px[:], lane_w("xa", q), T.win[:, 16 + 512 * q:528 + 512 * q], q == 0, q == 15, ["xa", "win"], ["px"])
+    dma(S, "y", lambda: g.sync.dma_start(T.co[:], T.cw[0:128:16, 16:NW]), ["cw"], ["co"])
     for t, b, sem in ((1, "zh1", "h1"), (2, "zh2", "h2")):
         arrival(S, sem, len(topo.engines(cores[(rank + t) % N], core)), [b])
         dma(S, "y", lambda: g.sync.dma_start(T.zs[:, 256 * t:256 * t + 256], T[b][:]), [b], [])
     dma(S, "y", lambda: g.sync.dma_start(T.zs[:, 768:1024], T.zi4[:]), ["zi4"], [])
+    vs(T.c2[:], T.co[:], 0.5, None, A.is_gt, None, ["co"], ["c2"])
+    dma(S, "y", lambda: g.sync.dma_start(T.cs[:], T.c2[:]), ["c2"], [])
+    vc(T.xo[:], T.px[:], ["px"], ["xo"])
     dma(S, "y", lambda: g.sync.dma_start(T.xs[:], T.xo[:]), ["xo"], [])
     for sem in SEMAPHORES:
         if S["count"].get(sem, 0):

@@ -1,13 +1,22 @@
 from concourse.mybir import AluOpType, ActivationFunctionType
 
 NW = 8208
+TURN = 919
+C0, CUT = 16 + TURN, 8192 - TURN
+CHAIN = ("C C C C twice sums turn N oi N oa N pages pairs l0 N l1 l2 N l34 fw N d4 low N d8 bit N d12 d0 N ww N wb er N hh N li N* nr")
+CHAIN0 = "turn K oi K oa K pages l0 K K l1 l2 K K l34 K K d4 low K d8 bit K d12 d0 K K ww K K wb K K hh K K li K*"
+AFTER = {0: "rt", 1: "M M", 3: "M M", 5: "M", 7: "M", 9: "M", 15: "M M M M M M M M M"}
+AFTER0 = {0: "pairs", 1: "er fw", 3: "nr", 5: "rt", 7: "M", 9: "M", 11: "M", 15: "M M M M M M M M M"}
+ANSWER = ("R K R K R K R K R K R K ms R K sn R K qq ri signs z rn R M* high nl low nc R ys R nf R count R eq at once R R R* q16 rl mc "
+          "N cl N N N")
 BIG = 16384.0
 B2, F4, I4, U2 = "bfloat16", "float32", "int32", "uint16"
 SCRATCH = {"win": ("sbuf", [128, NW], B2), "cw": ("sbuf", [128, NW], F4),
            "sh": ("sbuf", [128, 8, 8, 16], B2),
            "ro": ("sbuf", [128, 8, 128], B2),
            "diff": ("sbuf", [128, 4096], B2),
-           "ad": ("sbuf", [128, 256, 16], B2),
+           "ad": ("sbuf", [128, 16, 16, 16], B2),
+           "ey2": ("sbuf", [128, 8, 32], B2), "zr": ("sbuf", [128, 16, 2, 16], B2),
            "eye": ("sbuf", [128, 8, 16], B2), "neye": ("sbuf", [128, 8, 16], B2), "lh": ("sbuf", [128, 8, 128], B2),
            "wd": ("sbuf", [128, 2048], B2),
            "xa": ("sbuf", [128, 2048], B2),
@@ -17,12 +26,12 @@ PSUM = {"pg": [128, 4, 8, 16], "pd": [128, 16, 32], "pq": [128, 32, 16], "pa": [
         "ph": [128, 512], "px": [128, 512]}
 for _n in PSUM:
     SCRATCH[_n] = ("psum", PSUM[_n], F4)
-for _d, _l in ((B2, "ones:128 blk1:128 blk:128 eye2:128 dm:128 dm1:128 n128:16 thb:1 j15:16 hl:32 pp:16 rw:256 zh1:256 zh2:256 z2:512 "
+for _d, _l in ((B2, "ones:256 blk1:128 blk:128 eye2:128 ey4:128 ck:128 z1:256 dm:128 dm1:128 n128:16 thb:1 j15:16 hl:32 pp:16 rw:256 zh1:256 zh2:256 z2:512 "
                     "ys:256 nc:256 junk:16"),
-               (F4, "p15:1 lane:1 gp1:1 gp0:1 wf:2 wa:1 wp:2 wb:1 thc:1 th2:1 mc:1 lu:32 lt:32 e16:16 e240:240 aa:256 hf:240 "
-                    "hd:272 ms:272 sn:272 ac:1 at:1 nr:16 mv:256 nf:256 xo:512 co:512 c2:512 k8:8 k16:8 tk:8 tl:8 t6:6 oh:6 bm:6 sb:5 "
+               (F4, "p15:1 lane:1 gp1:1 gp0:1 wf:2 wa:1 wp:2 th2:1 mc:1 lu:32 lt:32 e16:16 plc:256 hf:256 "
+                    "hd:272 ms:272 sn:272 ac:1 at:1 nr:16 mv:256 nf:256 xo:512 k8:8 k16:8 tk:8 tl:8 t6:6 oh:6 bm:6 sb:5 "
                     "sm:1 sf:1 nb:1 jb:1 m120:1"),
-               (I4, "pidx:1 p15i:1 gpi:1 wti:2 thi:1 lfi:16 raw:64 r12:64 ss:256 bi:64 ww:256 hh:256 qq:16 q16:1 ri:16 rn:16 jm:128 jn:128"),
+               (I4, "pidx:1 p15i:1 gpi:1 wti:2 thi:1 lfi:16 raw:80 r12:80 ss:256 bi:80 ww:256 hh:256 qq:16 q16:1 ri:16 rn:16 jm:128 jn:128"),
                (U2, "li:256 lo:16 nl:16 rl:32 cl:32 rt:32")):
     for _x in _l.split():
         SCRATCH[_x.split(":")[0]] = ("sbuf", [128, int(_x.split(":")[1])], _d)
@@ -32,7 +41,7 @@ for _t in range(5):
     SCRATCH["add%d" % _t] = ("sbuf", [128, 4, 2, 4], F4)
 SCRATCH["fw"] = ("sbuf", [128, 4, 4, 2, 4], F4)
 SEMAPHORES = ["qv", "qt", "qs", "qg", "ls", "wp", "h1", "h2"] + ["za%d" % t for t in range(1, 5)] + \
-    ["fa%d" % t for t in range(1, 5)] + ["d%d" % k for k in range(16)]
+    ["fa%d" % t for t in range(1, 5)] + ["d%d" % k for k in range(18)]
 
 
 def state(g, T):
@@ -106,15 +115,14 @@ def arrival(S, sem, val, writes):
     note(S, [], writes, (sem, val, {}))
 
 
-def weave(main, fill, first=0, each=1):
-    for _ in range(first):
-        if fill:
-            fill.pop(0)()
-    for f in main:
-        f()
-        for _ in range(each):
-            if fill:
-                fill.pop(0)()
+def play(order, calls, rows):
+    for name in order.split():
+        if name[0] in rows:
+            row = rows[name[0]]
+            for _ in range(len(row) if name[1:] == "*" else min(1, len(row))):
+                row.pop(0)()
+        else:
+            calls[name]()
 
 
 def rank_program(g, core, T, topo):
@@ -172,89 +180,120 @@ def rank_program(g, core, T, topo):
         g.remote_dma(out, src, T.sem[sem], T.sem.ls, pid, rid, topo.mask(core, dst))
         S["count"]["ls"] = S["count"].get("ls", 0) + len(topo.engines(core, dst))
 
+    def slot(buf, a):
+        if a in (0, 15):
+            return buf[:, 16 * a:16 * a + 16]
+        first = 16 + 32 * ((a - 1) // 2)
+        return buf[:, first + (a - 1) % 2:first + 32:2]
+
     def lane_w(name, i):
         return T[name][:, 128 * i:128 * i + 128]
 
     dma(S, "y", lambda: g.sync.dma_start(T.wti[:], T.wt[:]), [], ["wti"])
     dma(S, "s", lambda: C.dma_start(T.lfi[:], T.leaf[:]), [], ["lfi"])
     dma(S, "y", lambda: g.sync.dma_start(T.zi0[:], T.z0[:]), [], ["zi0"])
-    dma(S, "y", lambda: g.sync.dma_start(T.win[:, 16:NW], T.x0[:]), [], [("win", 16, NW)])
+    dma(S, "s", lambda: C.dma_start(T.z1[:], T.z0[:]), [], ["z1"])
+    dma(S, "y", lambda: g.sync.dma_start(T.win[:, C0:NW], T.x0[:, 0:CUT]), [], [("win", C0, NW)])
+    dma(S, "y", lambda: g.sync.dma_start(T.win[:, 16:C0], T.x0[:, CUT:8192]), [], [("win", 16, C0)])
     iota("pidx", [[0, 1]], 0, 1)
-    for n, x in [("ones", 1.0), ("thi", 0), ("wd", 0.0), ("lh", 0.0), ("add0", 64.0)]:
+    for n, x in [("ones", 1.0), ("m120", -120.0), ("thi", 0), ("wd", 0.0), ("lh", 0.0), ("add0", 64.0)]:
         fill(T[n][:], x, n)
     dma(S, "s", lambda: C.dma_start(T.thi[0:128:16, :], T.th[:]), [], ["thi"])
 
-    def zeros(a):
-        s(lambda: C.activation(T.cw[:, a:a + 2048], T.wd[:], F.Sigmoid, bias=T.m120[:, 0:1], scale=0.0), ["wd", "m120"], [("cw", a, a + 2048)])
+    def zeros(a, n, src="wd"):
+        s(lambda: C.activation(T.cw[:, a:a + n], T[src][:, 0:n], F.Sigmoid, bias=T.m120[:, 0:1], scale=0.0), [src, "m120"],
+          [("cw", a, a + n)])
 
-    fill(T.m120[:], -120.0, "m120")
-    select(T.blk1[:], T.ones[:], [[-16, 8], [0, 16]], A.is_ge, 0.0, 0, 1, ["ones"], ["blk1"])
+    zeros(0, 128, "ones")
+    select(T.blk1[:], T.ones[:, 0:128], [[-16, 8], [0, 16]], A.is_ge, 0.0, 0, 1, ["ones"], ["blk1"])
     select(T.blk[:], T.blk1[:], [[16, 8], [0, 16]], A.is_ge, 0.0, 15, -1, ["blk1"], ["blk"])
-    select(T.eye[:], T.ones[:], [[-1, 128]], A.is_equal, 0.0, 0, 1, ["ones"], ["eye"])
+    select(T.eye[:], T.ones[:, 0:128], [[-1, 128]], A.is_equal, 0.0, 0, 1, ["ones"], ["eye"])
     vs(T.p15i[:], T.pidx[:], 15, None, A.bitwise_and, None, ["pidx"], ["p15i"])
     vs(T.gpi[:], T.pidx[:], 4, 1, A.arith_shift_right, A.bitwise_and, ["pidx"], ["gpi"])
     for n, pattern, base, cm in [("jm", [[1, 128]], 128, -1), ("k8", [[1, 8]], 1, 0), ("k16", [[-1, 8]], 15, 0), ("t6", [[1, 6]], 0, 0),
-                                 ("e16", [[-1, 16]], 15, 0), ("e240", [[-1, 240]], 255, 0)]:
+                                 ("e16", [[-1, 16]], 15, 0)]:
         iota(n, pattern, base, cm)
+
     for gr in range(8):
         copy(T.wd[:, 16 * gr::129], T.blk[:, 16 * gr:16 * gr + 16], ["blk"], ["wd"] if gr == 0 else [("wd", gr, gr + 1)])
     vc(T.gp1[:], T.gpi[:], ["gpi"], ["gp1"])
     vs(T.gp0[:], T.gpi[:], -1.0, 1.0, A.mult, A.add, ["gpi"], ["gp0"])
     vs(T.wa[:], T.wti[:, 0:1], 128.0, None, A.mult, None, ["wti"], ["wa"])
     vc(T.wf[:], T.wti[:], ["wti"], ["wf"])
-    vs(T.neye[:], T.eye[:], -1.0, None, A.mult, None, ["eye"], ["neye"])
     for q in range(8):
-        copy(T.lh[:, q, q % 4::32], T.blk[:, 16 * (q // 4)::32], ["blk", "wa"], [("lh", 2 * q, 2 * q + 1)], scale=T.wa[:, 0:1])
+        if q % 2:
+            copy(T.lh[:, q, q % 4::32], T.blk[:, 16 * (q // 4)::32], ["blk", "wa"], [("lh", 2 * q, 2 * q + 1)], scale=T.wa[:, 0:1])
+        else:
+            vs(T.lh[:, q, q % 4::32], T.blk[:, 16 * (q // 4)::32], T.wa[:, 0:1], None, A.mult, None, ["blk", "wa"],
+               [("lh", 2 * q, 2 * q + 1)])
     vs(T.lu[:, 0:16], T.lfi[:], T.gp0[:, 0:1], None, A.mult, None, ["lfi", "gp0"], [("lu", 0, 16)])
     vs(T.lu[:, 16:32], T.lfi[:], T.gp1[:, 0:1], None, A.mult, None, ["lfi", "gp1"], [("lu", 16, 32)])
     v(lambda: V.transpose(T.lt[:], T.lu[:]), ["lu"], ["lt"])
     vt(T.add0[:, :, 1, :], T.lt[:, 0:16], T.lt[:, 16:32], A.add, ["lt"], ["add0"])
+    fill(T.ck[:], 0.0, "ck")
+    vs(T.ey4[:], T.eye[:], 0.25, None, A.mult, None, ["eye"], ["ey4"])
+    for row, x in ((0, 37.0), (32, 0.125), (64, 2.0 ** -17)):
+        fill(T.ck[row:row + 1, :], x, ("ck", row, row + 1))
+    zeros(128, 896)
+    for a, b, step, base, by in ((17, 240, 2, 239, -2), (48, 240, 2, 238, -2), (16, 48, 2, 255, -1), (240, 256, 1, 46, -2)):
+        op(S, "g", lambda: g.iota(T.plc[:, a:b:step], [[by, len(range(a, b, step))]], base, 0, allow_small_or_imprecise_dtypes=True),
+           [], [("plc", a, a + 1)])
+    op(S, "g", lambda: g.iota(T.cw[:, 5120:7168], [[0, 2048]], 0, 0, allow_small_or_imprecise_dtypes=True), [], [("cw", 5120, 7168)])
     send(nxt, T.wp[:], T.wf[:], "wp", ["wf"])
     arrival(S, "wp", E, ["wp"])
-    for k in range(1, 9):
-        select(T.sh[:, k - 1, :, k:16], T.neye[:, :, k:16], [[-16, 8], [-1, 16 - k]], A.not_equal, 1.0, k - k, 1,
-               ["neye"], [("sh", 2 * k, 2 * k + 1)])
-        select(T.sh[:, k - 1, :, 0:k], T.neye[:, :, 0:k], [[-16, 8], [-1, k]], A.not_equal, 1.0, k - 16, 1,
-               ["neye"], [("sh", 2 * k + 1, 2 * k + 2)])
+
+    def rotations():
+        for h, b in enumerate(("pa", "pb")):
+            for k in range(4):
+                mm(T[b][:, 128 * k:128 * k + 128], T.eye[:], T.eye[:], True, False, ["eye"], [b])
+                mm(T[b][:, 128 * k:128 * k + 128], T.neye[:], T.ey2[:, :, 4 * h + k + 1:4 * h + k + 17], False, True, ["neye", "ey2"], [b])
+            copy(T.sh[:, 4 * h:4 * h + 4, :, :], T[b][:], [b], [("sh", 8 * h + 2, 8 * h + 10)])
 
     rest = [lambda: vc(T.p15[:], T.p15i[:], ["p15i"], ["p15"]),
+            lambda: vs(T.neye[:], T.eye[:], -1.0, None, A.mult, None, ["eye"], ["neye"]),
+            lambda: vc(T.ey2[:, :, 0:16], T.eye[:], ["eye"], [("ey2", 0, 1)]),
+            lambda: vc(T.ey2[:, :, 16:32], T.eye[:], ["eye"], [("ey2", 1, 2)]),
+            lambda: fill(T.ss[:, 0:16], 2453, ("ss", 0, 16)),
             lambda: vs(T.jn[:], T.jm[:], 15, None, A.bitwise_and, None, ["jm"], ["jn"]),
-            lambda: vs(T.tk[:], T.k8[:], T.p15[:, 0:1], None, A.is_gt, None, ["k8", "p15"], ["tk"]),
+            lambda: vs(T.tk[:], T.k16[:], T.p15[:, 0:1], None, A.is_gt, None, ["k16", "p15"], ["tk"]),
             lambda: vs(T.dm[:], T.jn[:], 1.0, None, A.add, None, ["jn"], ["dm"]),
-            lambda: vt(T.tl[:], T.tk[:], T.k16[:], A.mult, ["tk", "k16"], ["tl"]),
+            lambda: vt(T.tl[:], T.tk[:], T.k8[:], A.mult, ["tk", "k8"], ["tl"]),
             lambda: vs(T.oh[:], T.t6[:], T.p15[:, 0:1], None, A.is_equal, None, ["t6", "p15"], ["oh"]),
             lambda: vt(T.dm1[:], T.dm[:], T.blk[:], A.mult, ["dm", "blk"], ["dm1"]),
             lambda: vs(T.tk[:], T.tl[:], 1.0, None, A.add, None, ["tl"], ["tk"]),
             lambda: vs(T.bm[:], T.oh[:], 240.0, -120.0, A.mult, A.add, ["oh"], ["bm"]),
-            lambda: vs(T.sb[:], T.oh[:, 1:6], T.oh[:, 0:1], -BIG, A.subtract, A.mult, ["oh"], ["sb"]),
             lambda: vs(T.sm[:], T.oh[:, 0:1], 240.0, None, A.mult, None, ["oh"], ["sm"]),
-            lambda: vs(T.sf[:], T.oh[:, 0:1], -240.0, None, A.mult, None, ["oh"], ["sf"]),
-            lambda: vs(T.nb[:], T.oh[:, 0:1], 0.25 - BIG, None, A.mult, None, ["oh"], ["nb"]),
-            lambda: vs(T.lane[:], T.p15[:], 4080.0, None, A.add, None, ["p15"], ["lane"]),
-            lambda: vs(T.eye2[:], T.eye[:], 2.0, None, A.mult, None, ["eye"], ["eye2"]),
             lambda: fill(T.win[:, 0:16], 0.0, ("win", 0, 16)),
-            lambda: fill(T.hd[:], 0.0, "hd"), lambda: fill(T.fw[:], 64.0, "fw")]
+            lambda: vs(T.eye2[:], T.eye[:], 2.0, None, A.mult, None, ["eye"], ["eye2"]),
+            lambda: fill(T.hd[:, 0::17], 0.0, ("hd", 0, 1)),
+            lambda: fill(T.pd[:, :, 0], 0.0, "pd"),
+            lambda: fill(T.n128[:], -128.0, "n128"),
+            lambda: fill(T.pd[:, :, 16], 1000.0, "pd")]
 
     def last_constants():
-        zeros(4112)
-        zeros(6160)
-        op(S, "g", lambda: g.iota(T.cw[:, 0:1536], [[0, 1536]], 0, 0, allow_small_or_imprecise_dtypes=True), [], [("cw", 0, 1536)])
-        fill(T.cw[:, 1536:4112], 0.0, ("cw", 1536, 4112))
-        dma(S, "g", lambda: g.dma_start(T.cw[0:128:16, 16:NW], T.c0[:]), [], ["cw"])
-        vs(T.ph[:, 256:496], T.e240[:], BIG, 16.0, A.mult, A.add, ["e240"], ["ph"])
+        fill(T.cw[:, 7168:NW], 0.0, ("cw", 7168, NW))
+        dma(S, "g", lambda: g.dma_start(T.cw[0:128:16, 16:C0], T.c0[:, CUT:8192]), [], [("cw", 16, C0)])
+        dma(S, "g", lambda: g.dma_start(T.cw[0:128:16, C0:NW], T.c0[:, 0:CUT]), [], [("cw", C0, NW)])
+        rotations()
+        vs(T.ph[:, 272:512], T.plc[:, 16:256], BIG, 16.0, A.mult, A.add, ["plc"], ["ph"])
+
+    def routes():
         for k in range(8):
             vs(T.ro[:, k, :], T.dm1[:], T.tk[:, k:k + 1], -BIG, A.is_equal, A.mult, ["dm1", "tk"], [("ro", k, k + 1)])
+        fill(T.fw[:], 64.0, "fw")
 
-    def under_first_gathers():
-        fill(T.n128[:], -128.0, "n128")
-        fill(T.jb[:], 0.5 - 240 * BIG, "jb")
-        fill(T.pd[:, :, 0], 0.0, "pd")
-        fill(T.pd[:, :, 16], 1000.0, "pd")
+    def thresholds():
         vc(T.thb[:], T.thi[:], ["thi"], ["thb"])
         mm(T.px[:, 0:1], T.blk[:], T.thb[:], True, True, ["blk", "thb"], ["px"])
-        vs(T.hd[:, 16::17], T.e16[:], BIG, T.p15[:, 0:1], A.mult, A.add, ["e16", "p15"], [("hd", 16, 17)])
-        vc(T.thc[:], T.px[:, 0:1], ["px"], ["thc"])
-        vs(T.th2[:], T.px[:, 0:1], 1024.0, None, A.add, None, ["px"], ["th2"])
+
+    first_answer = [lambda: vs(T.hd[:, 16::17], T.e16[:], BIG, T.p15[:, 0:1], A.mult, A.add, ["e16", "p15"], [("hd", 16, 17)]),
+                    lambda: vc(T.mc[:], T.px[:, 0:1], ["px"], ["mc"]),
+                    lambda: vs(T.lane[:], T.p15[:], 4080.0, None, A.add, None, ["p15"], ["lane"]),
+                    lambda: vs(T.th2[:], T.px[:, 0:1], 1024.0, None, A.add, None, ["px"], ["th2"]),
+                    lambda: vs(T.sb[:], T.oh[:, 1:6], T.oh[:, 0:1], -BIG, A.subtract, A.mult, ["oh"], ["sb"]),
+                    lambda: vs(T.nb[:], T.oh[:, 0:1], 0.25 - BIG, None, A.mult, None, ["oh"], ["nb"]),
+                    lambda: vs(T.sf[:], T.oh[:, 0:1], -240.0, None, A.mult, None, ["oh"], ["sf"]),
+                    lambda: fill(T.jb[:], 0.5 - 240 * BIG, "jb")]
 
     def sums(t):
         zi = "zi%d" % t
@@ -265,99 +304,114 @@ def rank_program(g, core, T, topo):
     def chain(t):
         ad = "add%d" % t
 
-        def down(a, n, src, name, has):
+        def down(a, w, n, src, name, has):
             c = 2452.0 - has * 2452.0 / 2 ** n - 0.5 + 0.5 / 2 ** n
-            return lambda: vs(T.ss[:, a:a + 64], src, 1.0 / 2 ** n, c, A.mult, A.add, [name], [("ss", a, a + 64)])
+            return lambda: vs(T.ss[:, a:a + w], src, 1.0 / 2 ** n, c, A.mult, A.add, [name], [("ss", a, a + w)])
 
-        def rr0():
-            vs(T.ph[:, 0:16], T.oa[:, :, 0, :], 1.0 / 64, 296.0, A.mult, A.add, ["oa"], ["ph"])
-            for n in (16, 32, 64, 128):
-                copy(T.ph[:, n:2 * n], T.ph[:, 0:n], [], ["ph"])
-            copy(T.pp[:], T.ph[:, 0:16], ["ph"], ["pp"], bias=-148.5, scale=0.5)
+        def pages():
+            mm(T.ph[:, 0:256], T.ck[:], T.ones[:], True, False, ["ck", "ones"], ["ph"])
+            vs(T.pp[:], T.oa[:, :, 0, :], 1.0 / 128, -0.5, A.mult, A.add, ["oa"], ["pp"])
+            for a in range(16):
+                mm(slot(T.ph, a), T.ey4[:], T.pp[:], False, a == 15, ["ey4", "pp"], ["ph"])
 
-        return [lambda: v(lambda: V.transpose(T.ts[:], T.pg[:, :, 0:2, :]), ["pg"], ["ts"]),
-                lambda: vt(T.oi[:], T.ts[:, :, :, 0, :], T[ad][:], A.add, ["ts", ad], ["oi"]),
-                lambda: vs(T.oa[:], T.oi[:], 32767, None, A.bitwise_and, None, ["oi"], ["oa"]),
-                rr0,
-                lambda: vs(T.raw[:, 48:64], T.oa[:, :, 1, :], 32768.0, None, A.add, None, ["oa"], [("raw", 48, 64)]),
-                lambda: vs(T.raw[:, 32:48], T.raw[:, 48:64], 1, None, A.arith_shift_right, None, [("raw", 48, 64)], [("raw", 32, 48)]),
-                lambda: vs(T.raw[:, 0:32], T.raw[:, 32:64], 2, None, A.arith_shift_right, None, [("raw", 32, 64)], [("raw", 0, 32)]),
-                down(128, 4, T.raw[:], "raw", 0),
-                lambda: vs(T.r12[:], T.raw[:], 4095, None, A.bitwise_and, None, ["raw"], ["r12"]),
-                down(64, 8, T.raw[:], "raw", 0),
-                down(0, 8, T.ss[:, 128:192], ("ss", 128, 192), 1),
-                lambda: vs(T.ss[:, 192:256], T.r12[:], 2452.0, None, A.add, None, ["r12"], [("ss", 192, 256)]),
-                lambda: vs(T.bi[:], T.raw[:], 4096, None, A.bitwise_and, None, ["raw"], ["bi"]),
-                lambda: vt(T.aa[:], T.ss[:], T.ph[:, 0:256], A.mult, ["ss", "ph"], ["aa"]),
-                lambda: vs(T.ww[:], T.aa[:], 0.125, -91030.9375, A.mult, A.add, ["aa"], ["ww"]),
-                lambda: vt(T.ww[:, 192:256], T.ww[:, 192:256], T.bi[:], A.add, ["ww", "bi"], [("ww", 192, 256)]),
-                lambda: vs(T.hh[:], T.ww[:], 8191, None, A.bitwise_and, None, ["ww"], ["hh"]),
-                lambda: vs(T.li[:], T.hh[:], 16.0, None, A.add, None, ["hh"], ["li"])]
+        def shift(o, i, k, reads, writes):
+            return lambda: vs(o, i, k, None, A.arith_shift_right, None, reads, writes)
+
+        def forward():
+            if t < 4:
+                fw, to = ("fw", t, t + 1), "add%d" % (t + 1)
+                vs(T.fw[:, t, :, 1, :], T.oa[:, :, 1, :], 8.0, None, A.mult, None, ["oa"], [fw])
+                send(nxt, T[to][:], T.fw[:, t, :, :, :], "fa%d" % (t + 1), [fw])
+                arrival(S, "fa%d" % (t + 1), E, [to])
+
+        def root_pairs():
+            for k in range(8):
+                mm(T.pq[:, 8 + k, :], T.sh[:, k, :, :], T.pp[:], True, True, ["sh", "pp"], ["pq"])
+
+        def equal_roots():
+            vs(T.er[:], T.pq[:, 8:16, :], 0.0, None, A.is_equal, None, ["pq"], ["er"])
+            for k in range(8):
+                mm(T.pa[:, 0:16], T.ro[:, k, :], T.er[:, k, :], k == 0, k == 7, ["ro", "er"], ["pa"])
+
+        return {"turn": lambda: v(lambda: V.transpose(T.ts[:], T.pg[:, :, 0:2, :]), ["pg"], ["ts"]),
+                "oi": lambda: vt(T.oi[:], T.ts[:, :, :, 0, :], T[ad][:], A.add, ["ts", ad], ["oi"]),
+                "oa": lambda: vs(T.oa[:], T.oi[:], 32767, None, A.bitwise_and, None, ["oi"], ["oa"]),
+                "pages": pages, "pairs": root_pairs, "er": equal_roots, "fw": forward,
+                "l0": lambda: vs(T.raw[:, 64:80], T.oa[:, :, 1, :], 32768.0, None, A.add, None, ["oa"], [("raw", 64, 80)]),
+                "l1": shift(T.raw[:, 33:64:2], T.raw[:, 64:80], 1, [("raw", 64, 80)], [("raw", 33, 34)]),
+                "l2": shift(T.raw[:, 32:64:2], T.raw[:, 64:80], 2, [("raw", 64, 80)], [("raw", 32, 33)]),
+                "l34": shift(T.raw[:, 0:32], T.raw[:, 32:64], 2, [("raw", 32, 34)], [("raw", 0, 32)]),
+                "d4": down(112, 64, 4, T.raw[:, 0:64], "raw", 0),
+                "low": lambda: vs(T.r12[:], T.raw[:], 4095, None, A.bitwise_and, None, ["raw"], ["r12"]),
+                "d8": down(48, 64, 8, T.raw[:, 0:64], "raw", 0),
+                "d12": down(16, 32, 8, T.ss[:, 144:176], ("ss", 112, 176), 1),
+                "d0": lambda: vs(T.ss[:, 176:256], T.r12[:], 2452.0, None, A.add, None, ["r12"], [("ss", 176, 256)]),
+                "bit": lambda: vs(T.bi[:], T.raw[:], 4096, None, A.bitwise_and, None, ["raw"], ["bi"]),
+                "ww": lambda: vt(T.ww[:], T.ss[:], T.ph[:, 0:256], A.mult, ["ss", "ph"], ["ww"]),
+                "wb": lambda: vt(T.ww[:, 176:256], T.ww[:, 176:256], T.bi[:], A.add, ["ww", "bi"], [("ww", 176, 256)]),
+                "hh": lambda: vs(T.hh[:], T.ww[:], 8191, None, A.bitwise_and, None, ["ww"], ["hh"]),
+                "li": lambda: vs(T.li[:], T.hh[:], 16.0, None, A.add, None, ["hh"], ["li"]),
+                "nr": lambda: vt(T.nr[:], T.hh[:, 0:16], T.pa[:, 0:16], A.add, ["hh", "pa"], ["nr"]),
+                "rt": lambda: vs(T.rt[:, 0::2], T.nr[:], 16.0, T.p15[:, 0:1], A.add, A.max, ["nr", "p15"], ["rt"])}
 
     def twice(t):
+        zi = "zi%d" % t
         for h in range(2):
-            copy(T.z2[:, 256 * h:256 * h + 256], T["zi%d" % t][:], ["zi%d" % t], [("z2", h, h + 1)])
+            if t:
+                select(T.zr[:, :, h, :], T[zi][:], [[0, 256]], A.is_gt, 0.0, 1, 0, [zi], [("zr", h, h + 1)])
+            else:
+                vc(T.zr[:, :, h, :], T[zi][:], [zi], [("zr", h, h + 1)])
+        copy(T.z2[:], T.zr[:], ["zr"], ["z2"])
+        if t:
+            select(T.z1[:], T[zi][:], [[0, 256]], A.is_gt, 0.0, 1, 0, [zi], ["z1"])
 
     def sigmoids(vals, lst):
         return [lambda c=c: s(lambda: C.activation(T.cw[:, 0:NW].indirect(T[lst][:, 2 * c:2 * c + 1]), T[vals][:, 16 * c:16 * c + 16],
                                                    F.Sigmoid), [lst, vals], ["cw"]) for c in range(16)]
 
-    def gather(t, late):
+    def gather(t, late, ch):
         marks = sigmoids("mv", "rt")
-        for k in range(8):
-            mm(T.pq[:, 8 + k, :], T.sh[:, k, :, :], T.pp[:], True, True, [("sh", 2 * k + 2, 2 * k + 4), "pp"], ["pq"])
+
+        def root_counters():
+            copy(T.mv[:], T.cw[:, 0:NW].indirect(T.li[:, 0:16]), ["cw", "li", "sm", "bm"], ["mv"], bias=T.bm[:, t + 1:t + 2],
+                 scale=T.sm[:, 0:1])
+
+        if t in (2, 3):
+            send(cores[(rank - t + 1) % N], T["zh%d" % (t - 1)][:], T["zn%d" % (t - 1)][:], "h%d" % (t - 1), ["zn%d" % (t - 1)])
         while late:
             late.pop(0)()
-        for a, b in [(0, 2), (2, 4), (4, 6), (6, 8), (8, 10), (10, 12), (12, 14), (14, 15), (15, 16)]:
-            vt(T.diff[:, 256 * a:256 * b], T.win[:, 0:NW].indirect(T.li[:, 16 * a:16 * b]), T.z2[:, 0:256 * (b - a)], A.subtract,
-               ["win", "li", "z2"], [("diff", a, b)])
-            for k in range(max(a, 1), b):
-                s(lambda: C.activation(T.ad[:, :, k], T.diff[:, 256 * k:256 * k + 256], F.Abs), [("diff", k, k + 1)], [("ad", k, k + 1)])
-                if k in (4, 8, 12, 15):
-                    k0 = k - 3 + k // 15
-                    for i in range(16):
-                        mm(T.pd[:, :, k0:k + 1], lane_w("wd", i), T.ad[:, i::16, k0:k + 1], i == 0, i == 15,
-                           ["wd", ("ad", k0, k + 1)], ["pd"])
-            if a == (0 if t else 6):
-                copy(T.mv[:], T.cw[:, 0:NW].indirect(T.li[:, 0:16]), ["cw", "li", "sm", "bm"], ["mv"], bias=T.bm[:, t + 1:t + 2],
-                     scale=T.sm[:, 0:1])
+        if t:
+            root_counters()
+        for a, b in [(0, 1), (1, 3), (3, 5), (5, 7), (7, 9), (9, 11), (11, 13), (13, 15), (15, 16)]:
+            z = "z1" if b - a == 1 else "z2"
+            vt(T.diff[:, 256 * a:256 * b], T.win[:, 0:NW].indirect(T.li[:, 16 * a:16 * b]), T[z][:], A.subtract,
+               ["win", "li", z], [("diff", a, b)])
             if a == 0:
-                mm(T.pr[:, 0:256], T.eye2[:], T.z2[:, 0:256], True, False, ["eye2", "z2"], ["pr"])
+                mm(T.pr[:, 0:256], T.eye2[:], T.z1[:], True, False, ["eye2", "z1"], ["pr"])
                 mm(T.pr[:, 0:256], T.eye[:], T.diff[:, 0:256], False, True, ["eye", ("diff", 0, 1)], ["pr"])
-                vs(T.er[:], T.pq[:, 8:16, :], 0.0, None, A.is_equal, None, ["pq"], ["er"])
-                for k in range(8):
-                    mm(T.pa[:, 0:16], T.ro[:, k, :], T.er[:, k, :], k == 0, k == 7, ["ro", "er"], ["pa"])
-                vt(T.hf[:], T.hh[:, 16:256], T.ph[:, 256:496], A.add, ["hh", "ph"], ["hf"])
-                for m in range(1, 16):
-                    select(T.hd[:, m::17], T.hf[:, 16 * m - 16:16 * m], [[0, 16]], A.is_gt, 0.0, 1, 0, ["hf"], [("hd", m, m + 1)])
-                if t == 0:
-                    under_first_gathers()
-            if a == 2:
                 copy(T.rw[:], T.pr[:, 0:256], ["pr"], ["rw"], bias=127.8, scale=0.5)
-                vt(T.nr[:], T.hh[:, 0:16], T.pa[:, 0:16], A.add, ["hh", "pa"], ["nr"])
-                if t < 4:
-                    fw, to = ("fw", t, t + 1), "add%d" % (t + 1)
-                    vs(T.fw[:, t, :, 1, :], T.oa[:, :, 1, :], 8.0, None, A.mult, None, ["oa"], [fw])
-                    send(nxt, T[to][:], T.fw[:, t, :, :, :], "fa%d" % (t + 1), [fw])
-                    arrival(S, "fa%d" % (t + 1), E, [to])
-                if t in (2, 3):
-                    send(cores[(rank - t + 1) % N], T["zh%d" % (t - 1)][:], T["zn%d" % (t - 1)][:], "h%d" % (t - 1), ["zn%d" % (t - 1)])
-                vs(T.rt[:, 0::2], T.nr[:], 16.0, T.p15[:, 0:1], A.add, A.max, ["nr", "p15"], ["rt"])
-            if a == 4 and t:
-                vs(T.q16[:], T.ac[:], 1.0 / 32, 63.53125, A.mult, A.add, ["ac"], ["q16"])
-            if a == 6 and t:
-                vs(T.mc[:], T.q16[:], -16.0, T.at[:, 0:1], A.mult, A.add, ["q16", "at"], ["mc"])
-            if (4 if t else 8) <= a < 14:
-                marks.pop(0)()
-        while marks:
-            marks.pop(0)()
+            else:
+                s(lambda: C.activation(T.ad[:, :, a:b, :], T.diff[:, 256 * a:256 * b], F.Abs), [("diff", a, b)], [("ad", a, b)])
+            if b in (5, 9, 13, 16):
+                a0 = b - 4 + b // 16
+                for i in range(16):
+                    mm(T.pd[:, :, a0:b], lane_w("wd", i), T.ad[:, :, a0:b, i], i == 0, i == 15, ["wd", ("ad", a0, b)], ["pd"])
+            if a == 1:
+                vt(T.hf[:, 16:256], T.hh[:, 16:256], T.ph[:, 272:512], A.add, ["hh", "ph"], ["hf"])
+                for m in range(1, 16):
+                    select(T.hd[:, m::17], slot(T.hf, m), [[0, 16]], A.is_gt, 0.0, 1, 0, ["hf"], [("hd", m, m + 1)])
+            if t == 0 and a == 5:
+                root_counters()
+                thresholds()
+            play((AFTER if t else AFTER0).get(a, ""), ch, {"M": marks})
+        return marks
 
     def roots():
         return [lambda c=c: vt(T.win[:, 0:NW].indirect(T.rt[:, 2 * c:2 * c + 1]), T.rw[:, 16 * c:16 * c + 16], T.n128[:], A.add,
                                ["rt", "rw", "n128"], ["win"]) for c in range(15, -1, -1)]
 
-    def answer(t, rs):
-        zn, mc = "zn%d" % t, "mc" if t else "thc"
+    def answer(t, rs, marks):
+        zn, zi = "zn%d" % t, "zi%d" % t
 
         def new_z():
             vs(T.lo[:], T.qq[:], -16.0, T.lane[:, 0:1], A.mult, A.add, ["qq", "lane"], ["lo"])
@@ -368,83 +422,101 @@ def rank_program(g, core, T, topo):
             if t in (0, 4):
                 dma(S, "y", lambda: g.sync.dma_start(T.zs[:, 256 * t:256 * t + 256], T[zn][:]), [zn], [])
 
-        weave([lambda: vs(T.ms[:], T.pd[:, :, 0:17], T[mc][:, 0:1], None, A.is_gt, None, ["pd", mc], ["ms"]),
-               lambda: v(lambda: V.tensor_tensor_scan(T.sn[:], T.hd[:], T.ms[:], 0.0, A.max, A.mult), ["hd", "ms"], ["sn"]),
-               lambda: vs(T.qq[:], T.sn[:, 16::17], 1.0 / BIG, -0.25, A.mult, A.add, ["sn"], ["qq"])], rs, 9, 0)
-        vc(T.ri[:], T.sn[:, 16::17], ["sn"], ["ri"])
-        new_z()
+        def signs():
+            if t < 4:
+                s(lambda: C.activation(T.j15[:], T.sn[:, 16::17], F.Sign, bias=T.jb[:, 0:1]), ["sn", "jb"], ["j15"])
+                mm(T.px[:, 0:16], T.ones[:, 0:128], T.j15[:], True, True, ["ones", "j15"], ["px"])
 
-    def update(t, rs):
-        zi = "zi%d" % t
-        vs(T.rn[:], T.ri[:], 16383, None, A.bitwise_and, None, ["ri"], ["rn"])
-        weave([lambda: vc(T.hl[:, 0:16], T.rn[:], ["rn"], [("hl", 0, 16)]),
-               lambda: vc(T.nl[:], T.rn[:], ["rn"], ["nl"]),
-               lambda: vt(T.hl[:, 16:32], T.rn[:], T.hl[:, 0:16], A.subtract, ["rn", ("hl", 0, 16)], [("hl", 16, 32)])], rs, 1, 0)
-        copy(T.nc[:], T.cw[:, 0:NW].indirect(T.nl[:]), ["cw", "nl", "sb", "nb"], ["nc"], bias=T.nb[:, 0:1], scale=T.sb[:, t:t + 1])
-        for k in range(8):
-            for h in range(2):
-                mm(T.pq[:, k, :], T.sh[:, k, :, :], T.hl[:, 16 * h:16 * h + 16], h == 0, h == 1,
-                   ["sh", ("hl", 16 * h, 16 * h + 16)], ["pq"])
-        copy(T.ys[:], T.diff[:, 0:4096].indirect(T.lo[:]), ["diff", "lo"], ["ys"])
-        copy(T.nf[:], T.cw[:, 0:NW].indirect(T.nl[:]), ["cw", "nl", "sf", "bm"], ["nf"], bias=T.bm[:, 0:1], scale=T.sf[:, 0:1])
-        if t < 4:
-            s(lambda: C.activation(T.j15[:], T.sn[:, 16::17], F.Sign, bias=T.jb[:, 0:1]), ["sn", "jb"], ["j15"])
-        while rs:
-            rs.pop(0)()
-        vs(T.eq[:], T.pq[:, 0:8, :], 0.0, None, A.is_equal, None, ["pq"], ["eq"])
-        for b in ("pa", "pb"):
-            for h in range(2):
-                mm(T[b][:, 0:16], T.eye[:], T.hl[:, 16 * h:16 * h + 16], h == 0, False, ["eye", "hl"], [b])
-            for i in range(16 if b == "pa" else 0):
-                mm(T.pa[:, 0:16], lane_w("wd", i), T.nc[:, i::16], False, False, ["wd", "nc"], ["pa"])
+        def count():
+            if t < 4:
+                s(lambda: C.activation(T.junk[:], T.px[:, 0:16], F.Copy, accum_out=T.ac[:]), ["px"], ["junk", "ac"])
+
+        def low_part():
+            vt(T.hl[:, 16:32], T.rn[:], T.hl[:, 0:16], A.subtract, ["rn", ("hl", 0, 16)], [("hl", 16, 32)])
             for k in range(8):
-                mm(T[b][:, 0:16], T.ro[:, k, :], T.eq[:, k, :], False, k == 7, ["ro", "eq"], [b])
-        if t == 0:
-            for q in range(8):
-                copy(T.lh[:, q, 16 + q % 4::32], T.blk[:, 16 * (q // 4)::32], ["blk", "wp"], [("lh", 2 * q + 1, 2 * q + 2)],
-                     scale=T.wp[:, 1:2])
-        if t < 4:
-            mm(T.px[:, 0:16], T.ones[:], T.j15[:], True, True, ["ones", "j15"], ["px"])
-            s(lambda: C.activation(T.junk[:], T.px[:, 0:16], F.Copy, accum_out=T.ac[:]), ["px"], ["junk", "ac"])
-            copy(T.at[:], T.ac[:], ["ac", "th2"], ["at"], bias=T.th2[:, 0:1], scale=0.5)
-        else:
-            vs(T.xa[:], T.wd[:], T.wf[:, 0:1], None, A.mult, None, ["wd", "wf"], ["xa"])
-        vs(T.rl[:, 0::2], T.pa[:, 0:16], T.p15[:, 0:1], None, A.max, None, ["pa", "p15"], ["rl"])
+                for h in range(2):
+                    mm(T.pq[:, k, :], T.sh[:, k, :, :], T.hl[:, 16 * h:16 * h + 16], h == 0, h == 1,
+                       ["sh", ("hl", 16 * h, 16 * h + 16)], ["pq"])
+
+        def equal_names():
+            vs(T.eq[:], T.pq[:, 0:8, :], 0.0, None, A.is_equal, None, ["pq"], ["eq"])
+            for b in ("pa", "pb"):
+                for h in range(2):
+                    mm(T[b][:, 0:16], T.eye[:], T.hl[:, 16 * h:16 * h + 16], h == 0, False, ["eye", "hl"], [b])
+                for i in range(16 if b == "pa" else 0):
+                    mm(T.pa[:, 0:16], lane_w("wd", i), T.nc[:, i::16], False, False, ["wd", "nc"], ["pa"])
+                for k in range(8):
+                    mm(T[b][:, 0:16], T.ro[:, k, :], T.eq[:, k, :], False, k == 7, ["ro", "eq"], [b])
+
+        def once():
+            if t == 0:
+                for q in range(8):
+                    copy(T.lh[:, q, 16 + q % 4::32], T.blk[:, 16 * (q // 4)::32], ["blk", "wp"], [("lh", 2 * q + 1, 2 * q + 2)],
+                         scale=T.wp[:, 1:2])
+            if t == 4:
+                vs(T.xa[:], T.wd[:], T.wf[:, 0:1], None, A.mult, None, ["wd", "wf"], ["xa"])
+
+        def unless_last(f):
+            return f if t < 4 else lambda: None
+
         named = [lambda c=c: vt(T.win[:, 0:NW].indirect(T.rl[:, 2 * c:2 * c + 1]), T.ys[:, 16 * c:16 * c + 16], T[zi][:, c // 4, c % 4, :],
                                 A.add, ["rl", "ys", zi], ["win"]) for c in range(15, -1, -1)]
-        named.pop(0)()
-        named.pop(0)()
-        named.pop(0)()
-        vs(T.cl[:, 0::2], T.pb[:, 0:16], T.p15[:, 0:1], None, A.max, None, ["pb", "p15"], ["cl"])
+        play(ANSWER, {
+            "ms": lambda: vs(T.ms[:], T.pd[:, :, 0:17], T.mc[:, 0:1], None, A.is_gt, None, ["pd", "mc"], ["ms"]),
+            "sn": lambda: v(lambda: V.tensor_tensor_scan(T.sn[:], T.hd[:], T.ms[:], 0.0, A.max, A.mult), ["hd", "ms"], ["sn"]),
+            "qq": lambda: vs(T.qq[:], T.sn[:, 16::17], 1.0 / BIG, -0.25, A.mult, A.add, ["sn"], ["qq"]),
+            "ri": lambda: vc(T.ri[:], T.sn[:, 16::17], ["sn"], ["ri"]),
+            "signs": signs, "z": new_z, "count": count, "low": low_part, "eq": equal_names, "once": once,
+            "rn": lambda: vs(T.rn[:], T.ri[:], 16383, None, A.bitwise_and, None, ["ri"], ["rn"]),
+            "high": lambda: vc(T.hl[:, 0:16], T.rn[:], ["rn"], [("hl", 0, 16)]),
+            "nl": lambda: vc(T.nl[:], T.rn[:], ["rn"], ["nl"]),
+            "nc": lambda: copy(T.nc[:], T.cw[:, 0:NW].indirect(T.nl[:]), ["cw", "nl", "sb", "nb"], ["nc"], bias=T.nb[:, 0:1],
+                               scale=T.sb[:, t:t + 1]),
+            "ys": lambda: copy(T.ys[:], T.diff[:, 0:4096].indirect(T.lo[:]), ["diff", "lo"], ["ys"]),
+            "nf": lambda: copy(T.nf[:], T.cw[:, 0:NW].indirect(T.nl[:]), ["cw", "nl", "sf", "bm"], ["nf"], bias=T.bm[:, 0:1],
+                               scale=T.sf[:, 0:1]),
+            "at": unless_last(lambda: copy(T.at[:], T.ac[:], ["ac", "th2"], ["at"], bias=T.th2[:, 0:1], scale=0.5)),
+            "q16": unless_last(lambda: vs(T.q16[:], T.ac[:], 1.0 / 32, 63.53125, A.mult, A.add, ["ac"], ["q16"])),
+            "mc": unless_last(lambda: vs(T.mc[:], T.q16[:], -16.0, T.at[:, 0:1], A.mult, A.add, ["q16", "at"], ["mc"])),
+            "rl": lambda: vs(T.rl[:, 0::2], T.pa[:, 0:16], T.p15[:, 0:1], None, A.max, None, ["pa", "p15"], ["rl"]),
+            "cl": lambda: vs(T.cl[:, 0::2], T.pb[:, 0:16], T.p15[:, 0:1], None, A.max, None, ["pb", "p15"], ["cl"])},
+            {"R": rs, "M": marks, "N": named, "K": first_answer})
         return named, sigmoids("nf", "cl")
 
-    twice(0)
     sums(0)
-    weave(chain(0), rest)
+    twice(0)
+    zeros(1024, 2048)
+    zeros(3072, 2048)
+    ch = chain(0)
+    play(CHAIN0, ch, {"K": rest})
     last_constants()
+    routes()
     late = []
     for t in range(5):
-        gather(t, late)
-        rs = roots()
-        answer(t, rs)
-        named, late = update(t, rs)
+        marks = gather(t, late, ch)
+        if t == 4:
+            for u, b, sem in ((1, "zh1", "h1"), (2, "zh2", "h2")):
+                arrival(S, sem, len(topo.engines(cores[(rank + u) % N], core)), [b])
+                dma(S, "y", lambda: g.sync.dma_start(T.zs[:, 256 * u:256 * u + 256], T[b][:]), [b], [])
+            dma(S, "y", lambda: g.sync.dma_start(T.zs[:, 768:1024], T.zi4[:]), ["zi4"], [])
+        named, late = answer(t, roots(), marks)
         if t < 4:
-            weave([], late, 4)
-            twice(t + 1)
-            sums(t + 1)
-            weave(chain(t + 1), named)
-    weave(late, named)
-    for q in range(16):
-        mm(T.px[:], lane_w("xa", q), T.win[:, 16 + 512 * q:528 + 512 * q], q == 0, q == 15, ["xa", "win"], ["px"])
-    dma(S, "y", lambda: g.sync.dma_start(T.co[:], T.cw[0:128:16, 16:NW]), ["cw"], ["co"])
-    for t, b, sem in ((1, "zh1", "h1"), (2, "zh2", "h2")):
-        arrival(S, sem, len(topo.engines(cores[(rank + t) % N], core)), [b])
-        dma(S, "y", lambda: g.sync.dma_start(T.zs[:, 256 * t:256 * t + 256], T[b][:]), [b], [])
-    dma(S, "y", lambda: g.sync.dma_start(T.zs[:, 768:1024], T.zi4[:]), ["zi4"], [])
-    vs(T.c2[:], T.co[:], 0.5, None, A.is_gt, None, ["co"], ["c2"])
-    dma(S, "y", lambda: g.sync.dma_start(T.cs[:], T.c2[:]), ["c2"], [])
-    vc(T.xo[:], T.px[:], ["px"], ["xo"])
-    dma(S, "y", lambda: g.sync.dma_start(T.xs[:], T.xo[:]), ["xo"], [])
+            ch = chain(t + 1)
+            ch["twice"], ch["sums"] = lambda: twice(t + 1), lambda: sums(t + 1)
+            play(CHAIN, ch, {"N": named, "C": late})
+    play("N* C*", {}, {"N": named, "C": late})
+    dma(S, "s", lambda: C.dma_start(T.cs[:, 0:CUT], T.cw[0:128:16, C0:NW]), ["cw"], [])
+    dma(S, "s", lambda: C.dma_start(T.cs[:, CUT:8192], T.cw[0:128:16, 16:C0]), ["cw"], [])
+    for b, n, first in (("px", 384, 0), ("pr", 128, 384)):
+        for q in range(16):
+            v0 = 16 * first + n * q
+            cut = min(max(CUT, v0), v0 + n)
+            for lo, hi in ((v0, cut), (cut, v0 + n)):
+                if lo < hi:
+                    col = 16 + (lo + TURN) % 8192
+                    mm(T[b][:, lo - v0:hi - v0], lane_w("xa", q), T.win[:, col:col + hi - lo], q == 0, q == 15, ["xa", "win"], [b])
+        vc(T.xo[:, first:first + n], T[b][:, 0:n], [b], [("xo", first, first + n)])
+        dma(S, "y", lambda: g.sync.dma_start(T.xs[:, 16 * first:16 * (first + n)], T.xo[:, first:first + n]), [("xo", first, first + n)], [])
     for sem in SEMAPHORES:
         if S["count"].get(sem, 0):
             need(S, "g", (sem, S["count"][sem], {}))

@@ -1,14 +1,16 @@
 from concourse.mybir import AluOpType, ActivationFunctionType
 
-NW = 8208
+WASTE = 32
+NW = WASTE + 8192
 TURN = 919
-C0, CUT = 16 + TURN, 8192 - TURN
-CHAIN = ("C C C C twice sums turn N oi N oa N pages pairs l0 N l1 l2 N l34 fw N d4 low N d8 bit N d12 d0 N ww N wb er N hh N li N* nr")
-CHAIN0 = "turn K oi K oa K pages l0 K K l1 l2 K K l34 K K d4 low K d8 bit K d12 d0 K K ww K K wb K K hh K K li K*"
-AFTER = {0: "rt", 1: "M M", 3: "M M", 5: "M", 7: "M", 9: "M", 15: "M M M M M M M M M"}
-AFTER0 = {0: "pairs", 1: "er fw", 3: "nr", 5: "rt", 7: "M", 9: "M", 11: "M", 15: "M M M M M M M M M"}
-ANSWER = ("R K R K R K R K R K R K ms R K sn R K qq ri signs z rn R M* high nl low nc R ys R nf R count R eq at once R R R* q16 rl mc "
-          "N cl N N N")
+C0, CUT = WASTE + TURN, 8192 - TURN
+CHAIN = ("pb N cl N q16 N mc N C C C C twice sums turn N oi N oa N pages pairs l4 l3 N l2 l1 l0 N d10 d8 d4 N low bit fw N wwa d0 N "
+         "hha wwb N lia wb N er N hhb N N* lib hf")
+CHAIN0 = ("turn K K oi K K oa K K pages l4 l3 l2 l1 l0 K K d10 d8 d4 low bit K K wwa d0 K K hha wwb K K lia wb K K K hhb K K K "
+          "lib K*")
+AFTER = {0: "rw", 1: "nr", 3: "rt", 5: "M", 7: "M", 9: "M", 15: "M M M M M"}
+AFTER0 = {0: "pairs hf", 1: "er fw", 3: "nr rw", 5: "rt", 7: "M", 9: "M", 15: "M M M M M M"}
+ANSWER = "R K K K R K K K R K K K ms R sn R qq ri signs z h7 l7 rn R M* low nl nc R ys nf R count eq at once R* rl"
 BIG = 16384.0
 B2, F4, I4, U2 = "bfloat16", "float32", "int32", "uint16"
 SCRATCH = {"win": ("sbuf", [128, NW], B2), "cw": ("sbuf", [128, NW], F4),
@@ -16,23 +18,24 @@ SCRATCH = {"win": ("sbuf", [128, NW], B2), "cw": ("sbuf", [128, NW], F4),
            "ro": ("sbuf", [128, 8, 128], B2),
            "diff": ("sbuf", [128, 4096], B2),
            "ad": ("sbuf", [128, 16, 16, 16], B2),
+           "rot": ("sbuf", [128, 16, 128], B2),
            "ey2": ("sbuf", [128, 8, 32], B2), "zr": ("sbuf", [128, 16, 2, 16], B2),
            "eye": ("sbuf", [128, 8, 16], B2), "neye": ("sbuf", [128, 8, 16], B2), "lh": ("sbuf", [128, 8, 128], B2),
            "wd": ("sbuf", [128, 2048], B2),
            "xa": ("sbuf", [128, 2048], B2),
-           "eq": ("sbuf", [128, 8, 16], B2), "er": ("sbuf", [128, 8, 16], B2),
+           "eq": ("sbuf", [128, 8, 16], B2), "er": ("sbuf", [128, 16, 16], B2),
            "ts": ("sbuf", [128, 4, 2, 4, 4], F4), "oi": ("sbuf", [128, 4, 2, 4], I4), "oa": ("sbuf", [128, 4, 2, 4], I4)}
 PSUM = {"pg": [128, 4, 8, 16], "pd": [128, 16, 32], "pq": [128, 32, 16], "pa": [128, 512], "pb": [128, 512], "pr": [128, 512],
         "ph": [128, 512], "px": [128, 512]}
 for _n in PSUM:
     SCRATCH[_n] = ("psum", PSUM[_n], F4)
-for _d, _l in ((B2, "ones:256 blk1:128 blk:128 eye2:128 ey4:128 ck:128 z1:256 dm:128 dm1:128 n128:16 thb:1 j15:16 hl:32 pp:16 rw:256 zh1:256 zh2:256 z2:512 "
+for _d, _l in ((B2, "ones:256 blk1:128 blk:128 eye2:128 ey4:128 ck:128 z1:256 dm:128 dm1:128 nbe:128 n128:32 thb:1 j15:16 hl:32 pp:16 rw:256 zh1:256 zh2:256 z2:512 "
                     "ys:256 nc:256 junk:16"),
-               (F4, "p15:1 lane:1 gp1:1 gp0:1 wf:2 wa:1 wp:2 th2:1 mc:1 lu:32 lt:32 e16:16 plc:256 hf:256 "
+               (F4, "p15:1 p31:1 lane:1 gp1:1 gp0:1 wf:2 wa:1 wp:2 th2:1 mc:1 lu:32 lt:32 e16:16 plc:256 hf:256 "
                     "hd:272 ms:272 sn:272 ac:1 at:1 nr:16 mv:256 nf:256 xo:512 k8:8 k16:8 tk:8 tl:8 t6:6 oh:6 bm:6 sb:5 "
-                    "sm:1 sf:1 nb:1 jb:1 m120:1"),
-               (I4, "pidx:1 p15i:1 gpi:1 wti:2 thi:1 lfi:16 raw:80 r12:80 ss:256 bi:80 ww:256 hh:256 qq:16 q16:1 ri:16 rn:16 jm:128 jn:128"),
-               (U2, "li:256 lo:16 nl:16 rl:32 cl:32 rt:32")):
+                    "sm:1 so:1 sf:1 nb:1 jb:1 m120:1"),
+               (I4, "pidx:1 p15i:1 gpi:1 wti:2 thi:1 lfi:16 raw:80 r12:80 ss:256 bi:80 ww:256 hh:256 qq:16 q16:1 ri:16 rn:16 hi:32 jm:128 jn:128"),
+               (U2, "li:256 lo:16 nl:16 rl:32 cl:32 rt:16")):
     for _x in _l.split():
         SCRATCH[_x.split(":")[0]] = ("sbuf", [128, int(_x.split(":")[1])], _d)
 for _t in range(5):
@@ -46,7 +49,7 @@ SEMAPHORES = ["qv", "qt", "qs", "qg", "ls", "wp", "h1", "h2"] + ["za%d" % t for 
 
 def state(g, T):
     return {"g": g, "T": T, "q": {"v": g.vector, "t": g.tensor, "s": g.scalar, "g": g, "y": g.sync},
-            "known": {k: {} for k in "vtsgy"}, "count": {}, "w": {}, "r": {}, "nd": 0}
+            "known": {k: {} for k in "vtsgy"}, "count": {}, "w": {}, "r": {}, "bank": {}, "nd": 0}
 
 
 def norm(x):
@@ -89,8 +92,11 @@ def note(S, reads, writes, ev):
 
 
 def op(S, q, fn, reads, writes):
-    writes = writes + [x for x in reads if x in PSUM]
-    reads = [x for x in reads if x not in PSUM]
+    banks = [x for x in reads + writes if x in PSUM]
+    for x in banks:
+        for other, ev in S["bank"].setdefault(x, {}).items():
+            if other != q:
+                need(S, q, ev)
     deps(S, q, reads, writes)
     sem = "q" + q
     S["count"][sem] = S["count"].get(sem, 0) + 1
@@ -98,6 +104,8 @@ def op(S, q, fn, reads, writes):
     clock = dict(S["known"][q])
     clock[sem] = S["count"][sem]
     note(S, reads, writes, (sem, S["count"][sem], clock))
+    for x in banks:
+        S["bank"][x][q] = (sem, S["count"][sem], clock)
 
 
 def dma(S, q, fn, reads, writes):
@@ -194,7 +202,7 @@ def rank_program(g, core, T, topo):
     dma(S, "y", lambda: g.sync.dma_start(T.zi0[:], T.z0[:]), [], ["zi0"])
     dma(S, "s", lambda: C.dma_start(T.z1[:], T.z0[:]), [], ["z1"])
     dma(S, "y", lambda: g.sync.dma_start(T.win[:, C0:NW], T.x0[:, 0:CUT]), [], [("win", C0, NW)])
-    dma(S, "y", lambda: g.sync.dma_start(T.win[:, 16:C0], T.x0[:, CUT:8192]), [], [("win", 16, C0)])
+    dma(S, "y", lambda: g.sync.dma_start(T.win[:, WASTE:C0], T.x0[:, CUT:8192]), [], [("win", WASTE, C0)])
     iota("pidx", [[0, 1]], 0, 1)
     for n, x in [("ones", 1.0), ("m120", -120.0), ("thi", 0), ("wd", 0.0), ("lh", 0.0), ("add0", 64.0)]:
         fill(T[n][:], x, n)
@@ -263,7 +271,9 @@ def rank_program(g, core, T, topo):
             lambda: vs(T.tk[:], T.tl[:], 1.0, None, A.add, None, ["tl"], ["tk"]),
             lambda: vs(T.bm[:], T.oh[:], 240.0, -120.0, A.mult, A.add, ["oh"], ["bm"]),
             lambda: vs(T.sm[:], T.oh[:, 0:1], 240.0, None, A.mult, None, ["oh"], ["sm"]),
-            lambda: fill(T.win[:, 0:16], 0.0, ("win", 0, 16)),
+            lambda: fill(T.win[:, 0:WASTE], 0.0, ("win", 0, WASTE)),
+            lambda: vs(T.p31[:], T.p15[:], 16.0, None, A.add, None, ["p15"], ["p31"]),
+            lambda: vs(T.nbe[:], T.eye[:], -BIG, None, A.mult, None, ["eye"], ["nbe"]),
             lambda: vs(T.eye2[:], T.eye[:], 2.0, None, A.mult, None, ["eye"], ["eye2"]),
             lambda: fill(T.hd[:, 0::17], 0.0, ("hd", 0, 1)),
             lambda: fill(T.pd[:, :, 0], 0.0, "pd"),
@@ -272,12 +282,14 @@ def rank_program(g, core, T, topo):
 
     def last_constants():
         fill(T.cw[:, 7168:NW], 0.0, ("cw", 7168, NW))
-        dma(S, "g", lambda: g.dma_start(T.cw[0:128:16, 16:C0], T.c0[:, CUT:8192]), [], [("cw", 16, C0)])
+        dma(S, "g", lambda: g.dma_start(T.cw[0:128:16, WASTE:C0], T.c0[:, CUT:8192]), [], [("cw", WASTE, C0)])
         dma(S, "g", lambda: g.dma_start(T.cw[0:128:16, C0:NW], T.c0[:, 0:CUT]), [], [("cw", C0, NW)])
         rotations()
-        vs(T.ph[:, 272:512], T.plc[:, 16:256], BIG, 16.0, A.mult, A.add, ["plc"], ["ph"])
+        vs(T.ph[:, 272:512], T.plc[:, 16:256], BIG, float(WASTE), A.mult, A.add, ["plc"], ["ph"])
 
     def routes():
+        for k in range(16):
+            vc(T.rot[:, k, :], T.ey2[:, :, k:k + 16], ["ey2"], [("rot", k, k + 1)])
         for k in range(8):
             vs(T.ro[:, k, :], T.dm1[:], T.tk[:, k:k + 1], -BIG, A.is_equal, A.mult, ["dm1", "tk"], [("ro", k, k + 1)])
         fill(T.fw[:], 64.0, "fw")
@@ -293,7 +305,8 @@ def rank_program(g, core, T, topo):
                     lambda: vs(T.sb[:], T.oh[:, 1:6], T.oh[:, 0:1], -BIG, A.subtract, A.mult, ["oh"], ["sb"]),
                     lambda: vs(T.nb[:], T.oh[:, 0:1], 0.25 - BIG, None, A.mult, None, ["oh"], ["nb"]),
                     lambda: vs(T.sf[:], T.oh[:, 0:1], -240.0, None, A.mult, None, ["oh"], ["sf"]),
-                    lambda: fill(T.jb[:], 0.5 - 240 * BIG, "jb")]
+                    lambda: fill(T.jb[:], 0.5 - 240 * BIG, "jb"),
+                    lambda: vs(T.so[:], T.oh[:, 0:1], -1.0, None, A.mult, None, ["oh"], ["so"])]
 
     def sums(t):
         zi = "zi%d" % t
@@ -304,18 +317,29 @@ def rank_program(g, core, T, topo):
     def chain(t):
         ad = "add%d" % t
 
-        def down(a, w, n, src, name, has):
-            c = 2452.0 - has * 2452.0 / 2 ** n - 0.5 + 0.5 / 2 ** n
-            return lambda: vs(T.ss[:, a:a + w], src, 1.0 / 2 ** n, c, A.mult, A.add, [name], [("ss", a, a + w)])
+        def down(a, w, n):
+            return lambda: vs(T.ss[:, a:a + w], T.raw[:, 0:w], 0.5 ** n, 2451.5 + 0.5 ** (n + 1), A.mult, A.add, [("raw", 1, 5)],
+                              [("ss", a, a + w)])
+
+        def level(k, o):
+            c = 2.0 ** (15 - k) - (0.5 - 0.5 ** (k + 1))
+            return lambda: vs(o, T.oa[:, :, 1, :], 0.5 ** k, c, A.mult, A.add, ["oa"], [("raw", k, k + 1)])
+
+        def wide(a, b, part):
+            return {"ww" + part: lambda: vt(T.ww[:, a:b], T.ss[:, a:b], T.ph[:, a:b], A.mult, [("ss", a, b), "ph"], [("ww", a, b)]),
+                    "hh" + part: lambda: vs(T.hh[:, a:b], T.ww[:, a:b], 8191, None, A.bitwise_and, None, [("ww", a, b)], [("hh", a, b)]),
+                    "li" + part: lambda: vs(T.li[:, a:b], T.hh[:, a:b], float(WASTE), None, A.add, None, [("hh", a, b)], [("li", a, b)])}
+
+        def named_cells():
+            vt(T.hf[:, 16:256], T.hh[:, 16:256], T.ph[:, 272:512], A.add, ["hh", "ph"], ["hf"])
+            for m in range(1, 16):
+                select(T.hd[:, m::17], slot(T.hf, m), [[0, 16]], A.is_gt, 0.0, 1, 0, ["hf"], [("hd", m, m + 1)])
 
         def pages():
             mm(T.ph[:, 0:256], T.ck[:], T.ones[:], True, False, ["ck", "ones"], ["ph"])
             vs(T.pp[:], T.oa[:, :, 0, :], 1.0 / 128, -0.5, A.mult, A.add, ["oa"], ["pp"])
             for a in range(16):
                 mm(slot(T.ph, a), T.ey4[:], T.pp[:], False, a == 15, ["ey4", "pp"], ["ph"])
-
-        def shift(o, i, k, reads, writes):
-            return lambda: vs(o, i, k, None, A.arith_shift_right, None, reads, writes)
 
         def forward():
             if t < 4:
@@ -327,32 +351,36 @@ def rank_program(g, core, T, topo):
         def root_pairs():
             for k in range(8):
                 mm(T.pq[:, 8 + k, :], T.sh[:, k, :, :], T.pp[:], True, True, ["sh", "pp"], ["pq"])
+            for k in range(16):
+                out = T.pq[:, 16 + k // 2, 8 * (k % 2):8 * (k % 2) + 8]
+                mm(out, T.rot[:, k, :], T.pp[:, 0::2], True, False, ["rot", "pp"], ["pq"])
+                mm(out, T.neye[:], T.pp[:, 1::2], False, True, ["neye", "pp"], ["pq"])
 
         def equal_roots():
-            vs(T.er[:], T.pq[:, 8:16, :], 0.0, None, A.is_equal, None, ["pq"], ["er"])
+            vs(T.er[:], T.pq[:, 8:24, :], 0.0, None, A.is_equal, None, ["pq"], ["er"])
             for k in range(8):
-                mm(T.pa[:, 0:16], T.ro[:, k, :], T.er[:, k, :], k == 0, k == 7, ["ro", "er"], ["pa"])
+                mm(T.pa[:, 0:16], T.ro[:, k, :], T.er[:, k, :], k == 0, False, ["ro", "er"], ["pa"])
+            for k in range(16):
+                mm(T.pa[:, 1:16:2], T.nbe[:], T.er[:, 8 + k // 2, 8 * (k % 2):8 * (k % 2) + 8], False, k == 15, ["nbe", "er"], ["pa"])
 
-        return {"turn": lambda: v(lambda: V.transpose(T.ts[:], T.pg[:, :, 0:2, :]), ["pg"], ["ts"]),
+        def root_list():
+            for h, w in enumerate(("p15", "p31")):
+                vs(T.rt[:, h::2], T.nr[:, h::2], float(WASTE), T[w][:, 0:1], A.add, A.max, ["nr", w], [("rt", h, h + 1)])
+
+        return {**wide(0, 176, "a"), **wide(176, 256, "b"), "hf": named_cells, "rt": root_list,
+                "rw": lambda: copy(T.rw[:], T.pr[:, 0:256], ["pr"], ["rw"], bias=127.8, scale=0.5),
+                "turn": lambda: v(lambda: V.transpose(T.ts[:], T.pg[:, :, 0:2, :]), ["pg"], ["ts"]),
                 "oi": lambda: vt(T.oi[:], T.ts[:, :, :, 0, :], T[ad][:], A.add, ["ts", ad], ["oi"]),
                 "oa": lambda: vs(T.oa[:], T.oi[:], 32767, None, A.bitwise_and, None, ["oi"], ["oa"]),
                 "pages": pages, "pairs": root_pairs, "er": equal_roots, "fw": forward,
-                "l0": lambda: vs(T.raw[:, 64:80], T.oa[:, :, 1, :], 32768.0, None, A.add, None, ["oa"], [("raw", 64, 80)]),
-                "l1": shift(T.raw[:, 33:64:2], T.raw[:, 64:80], 1, [("raw", 64, 80)], [("raw", 33, 34)]),
-                "l2": shift(T.raw[:, 32:64:2], T.raw[:, 64:80], 2, [("raw", 64, 80)], [("raw", 32, 33)]),
-                "l34": shift(T.raw[:, 0:32], T.raw[:, 32:64], 2, [("raw", 32, 34)], [("raw", 0, 32)]),
-                "d4": down(112, 64, 4, T.raw[:, 0:64], "raw", 0),
+                "l0": level(0, T.raw[:, 64:80]), "l1": level(1, T.raw[:, 33:64:2]), "l2": level(2, T.raw[:, 32:64:2]),
+                "l3": level(3, T.raw[:, 1:32:2]), "l4": level(4, T.raw[:, 0:32:2]),
+                "d4": down(112, 64, 4), "d8": down(48, 64, 8), "d10": down(16, 32, 10),
                 "low": lambda: vs(T.r12[:], T.raw[:], 4095, None, A.bitwise_and, None, ["raw"], ["r12"]),
-                "d8": down(48, 64, 8, T.raw[:, 0:64], "raw", 0),
-                "d12": down(16, 32, 8, T.ss[:, 144:176], ("ss", 112, 176), 1),
                 "d0": lambda: vs(T.ss[:, 176:256], T.r12[:], 2452.0, None, A.add, None, ["r12"], [("ss", 176, 256)]),
                 "bit": lambda: vs(T.bi[:], T.raw[:], 4096, None, A.bitwise_and, None, ["raw"], ["bi"]),
-                "ww": lambda: vt(T.ww[:], T.ss[:], T.ph[:, 0:256], A.mult, ["ss", "ph"], ["ww"]),
-                "wb": lambda: vt(T.ww[:, 176:256], T.ww[:, 176:256], T.bi[:], A.add, ["ww", "bi"], [("ww", 176, 256)]),
-                "hh": lambda: vs(T.hh[:], T.ww[:], 8191, None, A.bitwise_and, None, ["ww"], ["hh"]),
-                "li": lambda: vs(T.li[:], T.hh[:], 16.0, None, A.add, None, ["hh"], ["li"]),
-                "nr": lambda: vt(T.nr[:], T.hh[:, 0:16], T.pa[:, 0:16], A.add, ["hh", "pa"], ["nr"]),
-                "rt": lambda: vs(T.rt[:, 0::2], T.nr[:], 16.0, T.p15[:, 0:1], A.add, A.max, ["nr", "p15"], ["rt"])}
+                "wb": lambda: vt(T.ww[:, 176:256], T.ww[:, 176:256], T.bi[:], A.add, [("ww", 176, 256), "bi"], [("ww", 176, 256)]),
+                "nr": lambda: vt(T.nr[:], T.hh[:, 0:16], T.pa[:, 0:16], A.add, [("hh", 0, 16), "pa"], ["nr"])}
 
     def twice(t):
         zi = "zi%d" % t
@@ -365,15 +393,16 @@ def rank_program(g, core, T, topo):
         if t:
             select(T.z1[:], T[zi][:], [[0, 256]], A.is_gt, 0.0, 1, 0, [zi], ["z1"])
 
-    def sigmoids(vals, lst):
-        return [lambda c=c: s(lambda: C.activation(T.cw[:, 0:NW].indirect(T[lst][:, 2 * c:2 * c + 1]), T[vals][:, 16 * c:16 * c + 16],
-                                                   F.Sigmoid), [lst, vals], ["cw"]) for c in range(16)]
+    def sigmoids(vals, lst, n):
+        return [lambda c=c: s(lambda: C.activation(T.cw[:, 0:NW].indirect(T[lst][:, 2 * c:2 * c + n]),
+                                                   T[vals][:, 16 * n * c:16 * n * (c + 1)], F.Sigmoid), [lst, vals], ["cw"])
+                for c in range(16 // n)]
 
     def gather(t, late, ch):
-        marks = sigmoids("mv", "rt")
+        marks = sigmoids("mv", "rt", 2)
 
         def root_counters():
-            copy(T.mv[:], T.cw[:, 0:NW].indirect(T.li[:, 0:16]), ["cw", "li", "sm", "bm"], ["mv"], bias=T.bm[:, t + 1:t + 2],
+            copy(T.mv[:], T.cw[:, 0:NW].indirect(T.li[:, 0:16]), ["cw", ("li", 0, 16), "sm", "bm"], ["mv"], bias=T.bm[:, t + 1:t + 2],
                  scale=T.sm[:, 0:1])
 
         if t in (2, 3):
@@ -385,21 +414,16 @@ def rank_program(g, core, T, topo):
         for a, b in [(0, 1), (1, 3), (3, 5), (5, 7), (7, 9), (9, 11), (11, 13), (13, 15), (15, 16)]:
             z = "z1" if b - a == 1 else "z2"
             vt(T.diff[:, 256 * a:256 * b], T.win[:, 0:NW].indirect(T.li[:, 16 * a:16 * b]), T[z][:], A.subtract,
-               ["win", "li", z], [("diff", a, b)])
+               ["win", ("li", 16 * a, 16 * b), z], [("diff", a, b)])
             if a == 0:
                 mm(T.pr[:, 0:256], T.eye2[:], T.z1[:], True, False, ["eye2", "z1"], ["pr"])
                 mm(T.pr[:, 0:256], T.eye[:], T.diff[:, 0:256], False, True, ["eye", ("diff", 0, 1)], ["pr"])
-                copy(T.rw[:], T.pr[:, 0:256], ["pr"], ["rw"], bias=127.8, scale=0.5)
             else:
                 s(lambda: C.activation(T.ad[:, :, a:b, :], T.diff[:, 256 * a:256 * b], F.Abs), [("diff", a, b)], [("ad", a, b)])
             if b in (5, 9, 13, 16):
                 a0 = b - 4 + b // 16
                 for i in range(16):
                     mm(T.pd[:, :, a0:b], lane_w("wd", i), T.ad[:, :, a0:b, i], i == 0, i == 15, ["wd", ("ad", a0, b)], ["pd"])
-            if a == 1:
-                vt(T.hf[:, 16:256], T.hh[:, 16:256], T.ph[:, 272:512], A.add, ["hh", "ph"], ["hf"])
-                for m in range(1, 16):
-                    select(T.hd[:, m::17], slot(T.hf, m), [[0, 16]], A.is_gt, 0.0, 1, 0, ["hf"], [("hd", m, m + 1)])
             if t == 0 and a == 5:
                 root_counters()
                 thresholds()
@@ -407,8 +431,8 @@ def rank_program(g, core, T, topo):
         return marks
 
     def roots():
-        return [lambda c=c: vt(T.win[:, 0:NW].indirect(T.rt[:, 2 * c:2 * c + 1]), T.rw[:, 16 * c:16 * c + 16], T.n128[:], A.add,
-                               ["rt", "rw", "n128"], ["win"]) for c in range(15, -1, -1)]
+        return [lambda c=c: vt(T.win[:, 0:NW].indirect(T.rt[:, 2 * c:2 * c + 2]), T.rw[:, 32 * c:32 * c + 32], T.n128[:], A.add,
+                               ["rt", "rw", "n128"], ["win"]) for c in range(7, -1, -1)]
 
     def answer(t, rs, marks):
         zn, zi = "zn%d" % t, "zi%d" % t
@@ -432,21 +456,26 @@ def rank_program(g, core, T, topo):
                 s(lambda: C.activation(T.junk[:], T.px[:, 0:16], F.Copy, accum_out=T.ac[:]), ["px"], ["junk", "ac"])
 
         def low_part():
-            vt(T.hl[:, 16:32], T.rn[:], T.hl[:, 0:16], A.subtract, ["rn", ("hl", 0, 16)], [("hl", 16, 32)])
+            vc(T.hl[:], T.hi[:], ["hi"], ["hl"])
             for k in range(8):
                 for h in range(2):
-                    mm(T.pq[:, k, :], T.sh[:, k, :, :], T.hl[:, 16 * h:16 * h + 16], h == 0, h == 1,
-                       ["sh", ("hl", 16 * h, 16 * h + 16)], ["pq"])
+                    mm(T.pq[:, k, :], T.sh[:, k, :, :], T.hl[:, 16 * h:16 * h + 16], h == 0, h == 1, ["sh", "hl"], ["pq"])
 
         def equal_names():
             vs(T.eq[:], T.pq[:, 0:8, :], 0.0, None, A.is_equal, None, ["pq"], ["eq"])
-            for b in ("pa", "pb"):
-                for h in range(2):
-                    mm(T[b][:, 0:16], T.eye[:], T.hl[:, 16 * h:16 * h + 16], h == 0, False, ["eye", "hl"], [b])
-                for i in range(16 if b == "pa" else 0):
-                    mm(T.pa[:, 0:16], lane_w("wd", i), T.nc[:, i::16], False, False, ["wd", "nc"], ["pa"])
-                for k in range(8):
-                    mm(T[b][:, 0:16], T.ro[:, k, :], T.eq[:, k, :], False, k == 7, ["ro", "eq"], [b])
+            sum_list("pa")
+
+        def sum_list(b):
+            for h in range(2):
+                mm(T[b][:, 0:16], T.eye[:], T.hl[:, 16 * h:16 * h + 16], h == 0, False, ["eye", "hl"], [b])
+            for i in range(16 if b == "pa" else 0):
+                mm(T.pa[:, 0:16], lane_w("wd", i), T.nc[:, i::16], False, False, ["wd", "nc"], ["pa"])
+            for k in range(8):
+                mm(T[b][:, 0:16], T.ro[:, k, :], T.eq[:, k, :], False, k == 7, ["ro", "eq"], [b])
+
+        def new_counters():
+            bias, scale = ("bm", "sf") if t < 4 else ("oh", "so")
+            copy(T.nf[:], T.cw[:, 0:NW].indirect(T.nl[:]), ["cw", "nl", scale, bias], ["nf"], bias=T[bias][:, 0:1], scale=T[scale][:, 0:1])
 
         def once():
             if t == 0:
@@ -468,20 +497,24 @@ def rank_program(g, core, T, topo):
             "ri": lambda: vc(T.ri[:], T.sn[:, 16::17], ["sn"], ["ri"]),
             "signs": signs, "z": new_z, "count": count, "low": low_part, "eq": equal_names, "once": once,
             "rn": lambda: vs(T.rn[:], T.ri[:], 16383, None, A.bitwise_and, None, ["ri"], ["rn"]),
-            "high": lambda: vc(T.hl[:, 0:16], T.rn[:], ["rn"], [("hl", 0, 16)]),
+            "h7": lambda: vs(T.hi[:, 0:16], T.ri[:], 16256, None, A.bitwise_and, None, ["ri"], [("hi", 0, 16)]),
+            "l7": lambda: vs(T.hi[:, 16:32], T.ri[:], 127, None, A.bitwise_and, None, ["ri"], [("hi", 16, 32)]),
             "nl": lambda: vc(T.nl[:], T.rn[:], ["rn"], ["nl"]),
             "nc": lambda: copy(T.nc[:], T.cw[:, 0:NW].indirect(T.nl[:]), ["cw", "nl", "sb", "nb"], ["nc"], bias=T.nb[:, 0:1],
                                scale=T.sb[:, t:t + 1]),
             "ys": lambda: copy(T.ys[:], T.diff[:, 0:4096].indirect(T.lo[:]), ["diff", "lo"], ["ys"]),
-            "nf": lambda: copy(T.nf[:], T.cw[:, 0:NW].indirect(T.nl[:]), ["cw", "nl", "sf", "bm"], ["nf"], bias=T.bm[:, 0:1],
-                               scale=T.sf[:, 0:1]),
+            "nf": new_counters,
             "at": unless_last(lambda: copy(T.at[:], T.ac[:], ["ac", "th2"], ["at"], bias=T.th2[:, 0:1], scale=0.5)),
-            "q16": unless_last(lambda: vs(T.q16[:], T.ac[:], 1.0 / 32, 63.53125, A.mult, A.add, ["ac"], ["q16"])),
-            "mc": unless_last(lambda: vs(T.mc[:], T.q16[:], -16.0, T.at[:, 0:1], A.mult, A.add, ["q16", "at"], ["mc"])),
-            "rl": lambda: vs(T.rl[:, 0::2], T.pa[:, 0:16], T.p15[:, 0:1], None, A.max, None, ["pa", "p15"], ["rl"]),
-            "cl": lambda: vs(T.cl[:, 0::2], T.pb[:, 0:16], T.p15[:, 0:1], None, A.max, None, ["pb", "p15"], ["cl"])},
+            "rl": lambda: vs(T.rl[:, 0::2], T.pa[:, 0:16], T.p15[:, 0:1], None, A.max, None, ["pa", "p15"], ["rl"])},
             {"R": rs, "M": marks, "N": named, "K": first_answer})
-        return named, sigmoids("nf", "cl")
+        counters = sigmoids("nf", "cl", 1) if t < 4 else [
+            lambda c=c: vc(T.cw[:, 0:NW].indirect(T.cl[:, 2 * c:2 * c + 1]), T.nf[:, 16 * c:16 * c + 16], ["cl", "nf"], ["cw"])
+            for c in range(16)]
+        return named, counters, {
+            "pb": lambda: sum_list("pb"),
+            "q16": lambda: vs(T.q16[:], T.ac[:], 1.0 / 32, 63.53125, A.mult, A.add, ["ac"], ["q16"]),
+            "mc": lambda: vs(T.mc[:], T.q16[:], -16.0, T.at[:, 0:1], A.mult, A.add, ["q16", "at"], ["mc"]),
+            "cl": lambda: vs(T.cl[:, 0::2], T.pb[:, 0:16], T.p15[:, 0:1], None, A.max, None, ["pb", "p15"], ["cl"])}
 
     sums(0)
     twice(0)
@@ -499,21 +532,21 @@ def rank_program(g, core, T, topo):
                 arrival(S, sem, len(topo.engines(cores[(rank + u) % N], core)), [b])
                 dma(S, "y", lambda: g.sync.dma_start(T.zs[:, 256 * u:256 * u + 256], T[b][:]), [b], [])
             dma(S, "y", lambda: g.sync.dma_start(T.zs[:, 768:1024], T.zi4[:]), ["zi4"], [])
-        named, late = answer(t, roots(), marks)
+        named, late, lists = answer(t, roots(), marks)
         if t < 4:
             ch = chain(t + 1)
-            ch["twice"], ch["sums"] = lambda: twice(t + 1), lambda: sums(t + 1)
+            ch.update(lists, twice=lambda: twice(t + 1), sums=lambda: sums(t + 1))
             play(CHAIN, ch, {"N": named, "C": late})
-    play("N* C*", {}, {"N": named, "C": late})
+    play("pb N N cl" + " N C" * 14 + " C*", lists, {"N": named, "C": late})
     dma(S, "s", lambda: C.dma_start(T.cs[:, 0:CUT], T.cw[0:128:16, C0:NW]), ["cw"], [])
-    dma(S, "s", lambda: C.dma_start(T.cs[:, CUT:8192], T.cw[0:128:16, 16:C0]), ["cw"], [])
+    dma(S, "s", lambda: C.dma_start(T.cs[:, CUT:8192], T.cw[0:128:16, WASTE:C0]), ["cw"], [])
     for b, n, first in (("px", 384, 0), ("pr", 128, 384)):
         for q in range(16):
             v0 = 16 * first + n * q
             cut = min(max(CUT, v0), v0 + n)
             for lo, hi in ((v0, cut), (cut, v0 + n)):
                 if lo < hi:
-                    col = 16 + (lo + TURN) % 8192
+                    col = WASTE + (lo + TURN) % 8192
                     mm(T[b][:, lo - v0:hi - v0], lane_w("xa", q), T.win[:, col:col + hi - lo], q == 0, q == 15, ["xa", "win"], [b])
         vc(T.xo[:, first:first + n], T[b][:, 0:n], [b], [("xo", first, first + n)])
         dma(S, "y", lambda: g.sync.dma_start(T.xs[:, 16 * first:16 * (first + n)], T.xo[:, first:first + n]), [("xo", first, first + n)], [])

@@ -4,13 +4,14 @@ WASTE = 32
 NW = WASTE + 8192
 TURN = 919
 C0, CUT = WASTE + TURN, 8192 - TURN
-CHAIN = ("pb N cl N q16 N mc N C C C C twice sums turn N oi N oa N pages pairs l4 l3 N l2 l1 l0 N d10 d8 d4 N low bit fw N wwa d0 N "
-         "hha wwb N lia wb N er N hhb N N* lib hf")
+CHAIN = ("sums pb twice N turn N oi q16 N oa cl N C C pages pairs l4 l3 l2 l1 N l0 mc d10 d8 d4 low N wwa bit d0 N hha wwb fw N* "
+         "lia wb er")
 CHAIN0 = ("turn K K oi K K oa K K pages l4 l3 l2 l1 l0 K K d10 d8 d4 low bit K K wwa d0 K K hha wwb K K lia wb K K K hhb K K K "
           "lib K*")
-AFTER = {0: "rw", 1: "nr", 3: "rt", 5: "M", 7: "M", 9: "M", 15: "M M M M M"}
-AFTER0 = {0: "pairs hf", 1: "er fw", 3: "nr rw", 5: "rt", 7: "M", 9: "M", 15: "M M M M M M"}
-ANSWER = "R K K K R K K K R K K K ms R sn R qq ri signs z h7 l7 rn R M* low nl nc R ys nf R count eq at once R* rl"
+AFTER = {0: "hhb", 1: "lib hf rw nr", 3: "rt dr", 5: "M", 7: "M", 9: "M", 15: "M M M M M"}
+AFTER0 = {0: "pairs hf", 1: "er fw", 3: "nr rw", 5: "rt dr", 7: "M", 9: "M", 15: "M M M M M M"}
+ANSWER = ("R K K K R K K K R K K ms R sn R qq ri signs z h7 l7 rn R M* low nl odd1 nc pn R ys odd2 nf eq R count R* eq2 pa at once "
+          "rl")
 BIG = 16384.0
 B2, F4, I4, U2 = "bfloat16", "float32", "int32", "uint16"
 SCRATCH = {"win": ("sbuf", [128, NW], B2), "cw": ("sbuf", [128, NW], F4),
@@ -23,19 +24,19 @@ SCRATCH = {"win": ("sbuf", [128, NW], B2), "cw": ("sbuf", [128, NW], F4),
            "eye": ("sbuf", [128, 8, 16], B2), "neye": ("sbuf", [128, 8, 16], B2), "lh": ("sbuf", [128, 8, 128], B2),
            "wd": ("sbuf", [128, 2048], B2),
            "xa": ("sbuf", [128, 2048], B2),
-           "eq": ("sbuf", [128, 8, 16], B2), "er": ("sbuf", [128, 16, 16], B2),
+           "z1": ("sbuf", [128, 2, 256], B2), "eq": ("sbuf", [128, 16, 16], B2), "er": ("sbuf", [128, 16, 16], B2),
            "ts": ("sbuf", [128, 4, 2, 4, 4], F4), "oi": ("sbuf", [128, 4, 2, 4], I4), "oa": ("sbuf", [128, 4, 2, 4], I4)}
-PSUM = {"pg": [128, 4, 8, 16], "pd": [128, 16, 32], "pq": [128, 32, 16], "pa": [128, 512], "pb": [128, 512], "pr": [128, 512],
-        "ph": [128, 512], "px": [128, 512]}
+PSUM = {"pg": [128, 4, 8, 16], "pq": [128, 32, 16], "pa": [128, 512], "pb": [128, 512], "pr": [128, 512],
+        "ph": [128, 512], "px": [128, 512], "pd": [128, 16, 32]}
 for _n in PSUM:
     SCRATCH[_n] = ("psum", PSUM[_n], F4)
-for _d, _l in ((B2, "ones:256 blk1:128 blk:128 eye2:128 ey4:128 ck:128 z1:256 dm:128 dm1:128 nbe:128 n128:32 thb:1 j15:16 hl:32 pp:16 rw:256 zh1:256 zh2:256 z2:512 "
+for _d, _l in ((B2, "ones:256 blk1:128 blk:128 xr:256 ey4:128 ck:128 dm:128 dm1:128 nbe:128 n128:32 thb:1 j15:16 hl:32 pp:16 rw:256 zh1:256 zh2:256 z2:512 "
                     "ys:256 nc:256 junk:16"),
                (F4, "p15:1 p31:1 lane:1 gp1:1 gp0:1 wf:2 wa:1 wp:2 th2:1 mc:1 lu:32 lt:32 e16:16 plc:256 hf:256 "
                     "hd:272 ms:272 sn:272 ac:1 at:1 nr:16 mv:256 nf:256 xo:512 k8:8 k16:8 tk:8 tl:8 t6:6 oh:6 bm:6 sb:5 "
-                    "sm:1 so:1 sf:1 nb:1 jb:1 m120:1"),
+                    "rp:128 sm:1 sf:1 nb:1 jb:1 m120:1"),
                (I4, "pidx:1 p15i:1 gpi:1 wti:2 thi:1 lfi:16 raw:80 r12:80 ss:256 bi:80 ww:256 hh:256 qq:16 q16:1 ri:16 rn:16 hi:32 jm:128 jn:128"),
-               (U2, "li:256 lo:16 nl:16 rl:32 cl:32 rt:16")):
+               (U2, "li:256 lo:16 nl:16 rl:16 cl:16 rt:16")):
     for _x in _l.split():
         SCRATCH[_x.split(":")[0]] = ("sbuf", [128, int(_x.split(":")[1])], _d)
 for _t in range(5):
@@ -200,7 +201,7 @@ def rank_program(g, core, T, topo):
     dma(S, "y", lambda: g.sync.dma_start(T.wti[:], T.wt[:]), [], ["wti"])
     dma(S, "s", lambda: C.dma_start(T.lfi[:], T.leaf[:]), [], ["lfi"])
     dma(S, "y", lambda: g.sync.dma_start(T.zi0[:], T.z0[:]), [], ["zi0"])
-    dma(S, "s", lambda: C.dma_start(T.z1[:], T.z0[:]), [], ["z1"])
+    dma(S, "s", lambda: C.dma_start(T.z1[:, 0, :], T.z0[:]), [], [("z1", 0, 1)])
     dma(S, "y", lambda: g.sync.dma_start(T.win[:, C0:NW], T.x0[:, 0:CUT]), [], [("win", C0, NW)])
     dma(S, "y", lambda: g.sync.dma_start(T.win[:, WASTE:C0], T.x0[:, CUT:8192]), [], [("win", WASTE, C0)])
     iota("pidx", [[0, 1]], 0, 1)
@@ -274,7 +275,6 @@ def rank_program(g, core, T, topo):
             lambda: fill(T.win[:, 0:WASTE], 0.0, ("win", 0, WASTE)),
             lambda: vs(T.p31[:], T.p15[:], 16.0, None, A.add, None, ["p15"], ["p31"]),
             lambda: vs(T.nbe[:], T.eye[:], -BIG, None, A.mult, None, ["eye"], ["nbe"]),
-            lambda: vs(T.eye2[:], T.eye[:], 2.0, None, A.mult, None, ["eye"], ["eye2"]),
             lambda: fill(T.hd[:, 0::17], 0.0, ("hd", 0, 1)),
             lambda: fill(T.pd[:, :, 0], 0.0, "pd"),
             lambda: fill(T.n128[:], -128.0, "n128"),
@@ -299,14 +299,13 @@ def rank_program(g, core, T, topo):
         mm(T.px[:, 0:1], T.blk[:], T.thb[:], True, True, ["blk", "thb"], ["px"])
 
     first_answer = [lambda: vs(T.hd[:, 16::17], T.e16[:], BIG, T.p15[:, 0:1], A.mult, A.add, ["e16", "p15"], [("hd", 16, 17)]),
-                    lambda: vc(T.mc[:], T.px[:, 0:1], ["px"], ["mc"]),
                     lambda: vs(T.lane[:], T.p15[:], 4080.0, None, A.add, None, ["p15"], ["lane"]),
+                    lambda: vc(T.mc[:], T.px[:, 0:1], ["px"], ["mc"]),
                     lambda: vs(T.th2[:], T.px[:, 0:1], 1024.0, None, A.add, None, ["px"], ["th2"]),
                     lambda: vs(T.sb[:], T.oh[:, 1:6], T.oh[:, 0:1], -BIG, A.subtract, A.mult, ["oh"], ["sb"]),
-                    lambda: vs(T.nb[:], T.oh[:, 0:1], 0.25 - BIG, None, A.mult, None, ["oh"], ["nb"]),
+                    lambda: vs(T.nb[:], T.oh[:, 0:1], -BIG, None, A.mult, None, ["oh"], ["nb"]),
                     lambda: vs(T.sf[:], T.oh[:, 0:1], -240.0, None, A.mult, None, ["oh"], ["sf"]),
-                    lambda: fill(T.jb[:], 0.5 - 240 * BIG, "jb"),
-                    lambda: vs(T.so[:], T.oh[:, 0:1], -1.0, None, A.mult, None, ["oh"], ["so"])]
+                    lambda: fill(T.jb[:], 0.5 - 240 * BIG, "jb")]
 
     def sums(t):
         zi = "zi%d" % t
@@ -368,6 +367,7 @@ def rank_program(g, core, T, topo):
                 vs(T.rt[:, h::2], T.nr[:, h::2], float(WASTE), T[w][:, 0:1], A.add, A.max, ["nr", w], [("rt", h, h + 1)])
 
         return {**wide(0, 176, "a"), **wide(176, 256, "b"), "hf": named_cells, "rt": root_list,
+                "dr": lambda: copy(T.diff[:, 0:256], T.pr[:, 256:512], ["pr"], [("diff", 0, 1)]),
                 "rw": lambda: copy(T.rw[:], T.pr[:, 0:256], ["pr"], ["rw"], bias=127.8, scale=0.5),
                 "turn": lambda: v(lambda: V.transpose(T.ts[:], T.pg[:, :, 0:2, :]), ["pg"], ["ts"]),
                 "oi": lambda: vt(T.oi[:], T.ts[:, :, :, 0, :], T[ad][:], A.add, ["ts", ad], ["oi"]),
@@ -391,7 +391,7 @@ def rank_program(g, core, T, topo):
                 vc(T.zr[:, :, h, :], T[zi][:], [zi], [("zr", h, h + 1)])
         copy(T.z2[:], T.zr[:], ["zr"], ["z2"])
         if t:
-            select(T.z1[:], T[zi][:], [[0, 256]], A.is_gt, 0.0, 1, 0, [zi], ["z1"])
+            select(T.z1[:, t % 2, :], T[zi][:], [[0, 256]], A.is_gt, 0.0, 1, 0, [zi], [("z1", t % 2, t % 2 + 1)])
 
     def sigmoids(vals, lst, n):
         return [lambda c=c: s(lambda: C.activation(T.cw[:, 0:NW].indirect(T[lst][:, 2 * c:2 * c + n]),
@@ -409,24 +409,25 @@ def rank_program(g, core, T, topo):
             send(cores[(rank - t + 1) % N], T["zh%d" % (t - 1)][:], T["zn%d" % (t - 1)][:], "h%d" % (t - 1), ["zn%d" % (t - 1)])
         while late:
             late.pop(0)()
+        one = ("z1", t % 2, t % 2 + 1)
+        copy(T.xr[:], T.win[:, 0:NW].indirect(T.li[:, 0:16]), ["win", ("li", 0, 16)], ["xr"])
         if t:
             root_counters()
-        for a, b in [(0, 1), (1, 3), (3, 5), (5, 7), (7, 9), (9, 11), (11, 13), (13, 15), (15, 16)]:
-            z = "z1" if b - a == 1 else "z2"
-            vt(T.diff[:, 256 * a:256 * b], T.win[:, 0:NW].indirect(T.li[:, 16 * a:16 * b]), T[z][:], A.subtract,
+        for h, w in enumerate(("eye", "neye")):
+            mm(T.pr[:, 256 * h:256 * h + 256], T[w][:], T.z1[:, t % 2, :], True, False, [w, one], ["pr"])
+            mm(T.pr[:, 256 * h:256 * h + 256], T.eye[:], T.xr[:], False, True, ["eye", "xr"], ["pr"])
+        play((AFTER if t else AFTER0).get(0, ""), ch, {"M": marks})
+        for a, b in [(1, 3), (3, 5), (5, 7), (7, 9), (9, 11), (11, 13), (13, 15), (15, 16)]:
+            z, zz = (one, T.z1[:, t % 2, :]) if b - a == 1 else ("z2", T.z2[:])
+            vt(T.diff[:, 256 * a:256 * b], T.win[:, 0:NW].indirect(T.li[:, 16 * a:16 * b]), zz, A.subtract,
                ["win", ("li", 16 * a, 16 * b), z], [("diff", a, b)])
-            if a == 0:
-                mm(T.pr[:, 0:256], T.eye2[:], T.z1[:], True, False, ["eye2", "z1"], ["pr"])
-                mm(T.pr[:, 0:256], T.eye[:], T.diff[:, 0:256], False, True, ["eye", ("diff", 0, 1)], ["pr"])
-            else:
-                s(lambda: C.activation(T.ad[:, :, a:b, :], T.diff[:, 256 * a:256 * b], F.Abs), [("diff", a, b)], [("ad", a, b)])
+            s(lambda: C.activation(T.ad[:, :, a:b, :], T.diff[:, 256 * a:256 * b], F.Abs), [("diff", a, b)], [("ad", a, b)])
             if b in (5, 9, 13, 16):
                 a0 = b - 4 + b // 16
                 for i in range(16):
                     mm(T.pd[:, :, a0:b], lane_w("wd", i), T.ad[:, :, a0:b, i], i == 0, i == 15, ["wd", ("ad", a0, b)], ["pd"])
             if t == 0 and a == 5:
                 root_counters()
-                thresholds()
             play((AFTER if t else AFTER0).get(a, ""), ch, {"M": marks})
         return marks
 
@@ -460,22 +461,35 @@ def rank_program(g, core, T, topo):
             for k in range(8):
                 for h in range(2):
                     mm(T.pq[:, k, :], T.sh[:, k, :, :], T.hl[:, 16 * h:16 * h + 16], h == 0, h == 1, ["sh", "hl"], ["pq"])
+            for k in range(16):
+                for h in range(2):
+                    mm(T.pg[:, 0, k // 2, 8 * (k % 2):8 * (k % 2) + 8], T.rot[:, k, :], T.hl[:, 16 * h:16 * h + 16:2], h == 0, h == 1,
+                       ["rot", "hl"], ["pg"])
 
-        def equal_names():
-            vs(T.eq[:], T.pq[:, 0:8, :], 0.0, None, A.is_equal, None, ["pq"], ["eq"])
-            sum_list("pa")
+        def odd(first):
+            for n in range(4 if first else 3):
+                if first:
+                    vc(T.rp[:, 8 * n:8 * n + 8], T.rn[:, 1::2], ["rn"], [("rp", 8 * n, 8 * n + 8)])
+                else:
+                    vc(T.rp[:, 32 * n + 32:32 * n + 64], T.rp[:, 0:32], [("rp", 0, 32)], [("rp", 32 * n + 32, 32 * n + 64)])
 
-        def sum_list(b):
-            for h in range(2):
+        def sum_list(b, parts):
+            for h in range(2 if 0 in parts else 0):
                 mm(T[b][:, 0:16], T.eye[:], T.hl[:, 16 * h:16 * h + 16], h == 0, False, ["eye", "hl"], [b])
-            for i in range(16 if b == "pa" else 0):
-                mm(T.pa[:, 0:16], lane_w("wd", i), T.nc[:, i::16], False, False, ["wd", "nc"], ["pa"])
-            for k in range(8):
-                mm(T[b][:, 0:16], T.ro[:, k, :], T.eq[:, k, :], False, k == 7, ["ro", "eq"], [b])
+            for i in range(16 if 1 in parts else 0):
+                mm(T[b][:, 0:16], lane_w("wd", i), T.nc[:, i::16], False, False, ["wd", "nc"], [b])
+            for k in range(8 if 2 in parts else 0):
+                mm(T[b][:, 0:16], T.ro[:, k, :], T.eq[:, k, :], False, False, ["ro", ("eq", 0, 8)], [b])
+            for k in range(16 if 3 in parts else 0):
+                mm(T[b][:, 1:16:2], T.nbe[:], T.eq[:, 8 + k // 2, 8 * (k % 2):8 * (k % 2) + 8], False, k == 15,
+                   ["nbe", ("eq", 8, 16)], [b])
+
+        def to_list(name, b):
+            for h, w in enumerate(("p15", "p31")):
+                vs(T[name][:, h::2], T[b][:, h:16:2], T[w][:, 0:1], None, A.max, None, [b, w], [(name, h, h + 1)])
 
         def new_counters():
-            bias, scale = ("bm", "sf") if t < 4 else ("oh", "so")
-            copy(T.nf[:], T.cw[:, 0:NW].indirect(T.nl[:]), ["cw", "nl", scale, bias], ["nf"], bias=T[bias][:, 0:1], scale=T[scale][:, 0:1])
+            copy(T.nf[:], T.cw[:, 0:NW].indirect(T.nl[:]), ["cw", "nl", "sf", "bm"], ["nf"], bias=T.bm[:, 0:1], scale=T.sf[:, 0:1])
 
         def once():
             if t == 0:
@@ -488,14 +502,19 @@ def rank_program(g, core, T, topo):
         def unless_last(f):
             return f if t < 4 else lambda: None
 
-        named = [lambda c=c: vt(T.win[:, 0:NW].indirect(T.rl[:, 2 * c:2 * c + 1]), T.ys[:, 16 * c:16 * c + 16], T[zi][:, c // 4, c % 4, :],
-                                A.add, ["rl", "ys", zi], ["win"]) for c in range(15, -1, -1)]
+        named = [lambda c=c: vt(T.win[:, 0:NW].indirect(T.rl[:, 2 * c:2 * c + 2]), T.ys[:, 32 * c:32 * c + 32],
+                                T.z1[:, t % 2, 32 * c:32 * c + 32], A.add, ["rl", "ys", ("z1", t % 2, t % 2 + 1)], ["win"])
+                 for c in range(7, -1, -1)]
         play(ANSWER, {
             "ms": lambda: vs(T.ms[:], T.pd[:, :, 0:17], T.mc[:, 0:1], None, A.is_gt, None, ["pd", "mc"], ["ms"]),
             "sn": lambda: v(lambda: V.tensor_tensor_scan(T.sn[:], T.hd[:], T.ms[:], 0.0, A.max, A.mult), ["hd", "ms"], ["sn"]),
             "qq": lambda: vs(T.qq[:], T.sn[:, 16::17], 1.0 / BIG, -0.25, A.mult, A.add, ["sn"], ["qq"]),
             "ri": lambda: vc(T.ri[:], T.sn[:, 16::17], ["sn"], ["ri"]),
-            "signs": signs, "z": new_z, "count": count, "low": low_part, "eq": equal_names, "once": once,
+            "signs": signs, "z": new_z, "count": count, "low": low_part, "once": once,
+            "odd1": lambda: odd(True), "odd2": lambda: odd(False),
+            "eq": lambda: vs(T.eq[:, 0:8, :], T.pq[:, 0:8, :], 0.0, None, A.is_equal, None, ["pq"], [("eq", 0, 8)]),
+            "eq2": lambda: vt(T.eq[:, 8:16, :], T.pg[:, 0, :, :], T.rp[:], A.is_equal, ["pg", "rp"], [("eq", 8, 16)]),
+            "pn": lambda: sum_list("pa", (0, 1)), "pa": lambda: sum_list("pa", (2, 3)),
             "rn": lambda: vs(T.rn[:], T.ri[:], 16383, None, A.bitwise_and, None, ["ri"], ["rn"]),
             "h7": lambda: vs(T.hi[:, 0:16], T.ri[:], 16256, None, A.bitwise_and, None, ["ri"], [("hi", 0, 16)]),
             "l7": lambda: vs(T.hi[:, 16:32], T.ri[:], 127, None, A.bitwise_and, None, ["ri"], [("hi", 16, 32)]),
@@ -505,16 +524,13 @@ def rank_program(g, core, T, topo):
             "ys": lambda: copy(T.ys[:], T.diff[:, 0:4096].indirect(T.lo[:]), ["diff", "lo"], ["ys"]),
             "nf": new_counters,
             "at": unless_last(lambda: copy(T.at[:], T.ac[:], ["ac", "th2"], ["at"], bias=T.th2[:, 0:1], scale=0.5)),
-            "rl": lambda: vs(T.rl[:, 0::2], T.pa[:, 0:16], T.p15[:, 0:1], None, A.max, None, ["pa", "p15"], ["rl"])},
+            "rl": lambda: to_list("rl", "pa")},
             {"R": rs, "M": marks, "N": named, "K": first_answer})
-        counters = sigmoids("nf", "cl", 1) if t < 4 else [
-            lambda c=c: vc(T.cw[:, 0:NW].indirect(T.cl[:, 2 * c:2 * c + 1]), T.nf[:, 16 * c:16 * c + 16], ["cl", "nf"], ["cw"])
-            for c in range(16)]
-        return named, counters, {
-            "pb": lambda: sum_list("pb"),
+        return named, sigmoids("nf", "cl", 2), {
+            "pb": lambda: sum_list("pb", (0, 2, 3)),
             "q16": lambda: vs(T.q16[:], T.ac[:], 1.0 / 32, 63.53125, A.mult, A.add, ["ac"], ["q16"]),
             "mc": lambda: vs(T.mc[:], T.q16[:], -16.0, T.at[:, 0:1], A.mult, A.add, ["q16", "at"], ["mc"]),
-            "cl": lambda: vs(T.cl[:, 0::2], T.pb[:, 0:16], T.p15[:, 0:1], None, A.max, None, ["pb", "p15"], ["cl"])}
+            "cl": lambda: to_list("cl", "pb")}
 
     sums(0)
     twice(0)
@@ -523,6 +539,7 @@ def rank_program(g, core, T, topo):
     ch = chain(0)
     play(CHAIN0, ch, {"K": rest})
     last_constants()
+    thresholds()
     routes()
     late = []
     for t in range(5):
@@ -537,7 +554,7 @@ def rank_program(g, core, T, topo):
             ch = chain(t + 1)
             ch.update(lists, twice=lambda: twice(t + 1), sums=lambda: sums(t + 1))
             play(CHAIN, ch, {"N": named, "C": late})
-    play("pb N N cl" + " N C" * 14 + " C*", lists, {"N": named, "C": late})
+    play("pb N N cl N* C*", lists, {"N": named, "C": late})
     dma(S, "s", lambda: C.dma_start(T.cs[:, 0:CUT], T.cw[0:128:16, C0:NW]), ["cw"], [])
     dma(S, "s", lambda: C.dma_start(T.cs[:, CUT:8192], T.cw[0:128:16, WASTE:C0]), ["cw"], [])
     for b, n, first in (("px", 384, 0), ("pr", 128, 384)):

@@ -4,14 +4,15 @@ WASTE = 32
 NW = WASTE + 8192
 TURN = 919
 C0, CUT = WASTE + TURN, 8192 - TURN
-CHAIN = ("sums pb twice N turn N oi q16 N oa cl N C C pages pairs l4 l3 l2 l1 N l0 mc d10 d8 d4 low N wwa bit d0 N hha wwb fw N* "
+CHAIN = ("sums pb N turn N oi N oa cl N C C twice home pages pairs l4 l3 l2 l1 N l0 d10 d8 d4 low N wwa bit d0 N hha wwb fw N* "
          "lia wb er")
 CHAIN0 = ("turn K K oi K K oa K K pages l4 l3 l2 l1 l0 K K d10 d8 d4 low bit K K wwa d0 K K hha wwb K K lia wb K K K hhb K K K "
           "lib K*")
-AFTER = {0: "hhb", 1: "lib hf rw nr", 3: "rt dr", 5: "M", 7: "M", 9: "M", 15: "M M M M M"}
-AFTER0 = {0: "pairs hf", 1: "er fw", 3: "nr rw", 5: "rt dr", 7: "M", 9: "M", 15: "M M M M M M"}
-ANSWER = ("R K K K R K K K R K K ms R sn R qq ri signs z h7 l7 rn R M* low nl odd1 nc pn R ys odd2 nf eq R count R* eq2 pa at once "
-          "rl")
+AFTER = {0: "hhb", 1: "lib hf rw nr xl", 3: "rt sends", 5: "al M", 7: "M", 13: "dr dl M M M M M"}
+AFTER0 = {0: "hf", 1: "fw xl", 3: "er rw sends", 5: "al", 7: "nr", 9: "rt", 11: "M", 13: "dr dl M M M M M M"}
+ANSWER = ("R q16 K K K R mc K K K R K K ms R sc sn z R h7 l7 rn signs M* parts nl odd1 nc once pn R ys odd2 nf R count eq2 R* eq pa "
+          "at xa rl")
+LAST = [(0, 16)]
 BIG = 16384.0
 B2, F4, I4, U2 = "bfloat16", "float32", "int32", "uint16"
 SCRATCH = {"win": ("sbuf", [128, NW], B2), "cw": ("sbuf", [128, NW], F4),
@@ -30,12 +31,12 @@ PSUM = {"pg": [128, 4, 8, 16], "pq": [128, 32, 16], "pa": [128, 512], "pb": [128
         "ph": [128, 512], "px": [128, 512], "pd": [128, 16, 32]}
 for _n in PSUM:
     SCRATCH[_n] = ("psum", PSUM[_n], F4)
-for _d, _l in ((B2, "ones:256 blk1:128 blk:128 xr:256 ey4:128 ck:128 dm:128 dm1:128 nbe:128 n128:32 thb:1 j15:16 hl:32 pp:16 rw:256 zh1:256 zh2:256 z2:512 "
-                    "ys:256 nc:256 junk:16"),
+for _d, _l in ((B2, "ones:256 blk1:128 blk:128 xr:256 xl:256 ey4:128 ck:128 dm:128 dm1:128 nbe:128 n128:32 thb:1 j15:16 hl:32 pp:16 rw:256 zh1:256 zh2:256 z2:512 "
+                    "ys:256 nc:256"),
                (F4, "p15:1 p31:1 lane:1 gp1:1 gp0:1 wf:2 wa:1 wp:2 th2:1 mc:1 lu:32 lt:32 e16:16 plc:256 hf:256 "
-                    "hd:272 ms:272 sn:272 ac:1 at:1 nr:16 mv:256 nf:256 xo:512 k8:8 k16:8 tk:8 tl:8 t6:6 oh:6 bm:6 sb:5 "
-                    "rp:128 sm:1 sf:1 nb:1 jb:1 m120:1"),
-               (I4, "pidx:1 p15i:1 gpi:1 wti:2 thi:1 lfi:16 raw:80 r12:80 ss:256 bi:80 ww:256 hh:256 qq:16 q16:1 ri:16 rn:16 hi:32 jm:128 jn:128"),
+                    "hd:272 ms:272 e3:272 sc:272 ac:1 at:1 nr:16 mv:256 nf:256 xo:512 k8:8 k16:8 tk:8 tl:8 t6:6 oh:6 bm:6 sb:5 "
+                    "rp:128 sm:1 sf:1 nb:1 m120:1"),
+               (I4, "pidx:1 p15i:1 gpi:1 wti:2 thi:1 lfi:16 raw:80 r12:80 ss:256 bi:80 ww:256 hh:256 q16:1 sn:272 rn:16 hi:32 jm:128 jn:128"),
                (U2, "li:256 lo:16 nl:16 rl:16 cl:16 rt:16")):
     for _x in _l.split():
         SCRATCH[_x.split(":")[0]] = ("sbuf", [128, int(_x.split(":")[1])], _d)
@@ -205,7 +206,7 @@ def rank_program(g, core, T, topo):
     dma(S, "y", lambda: g.sync.dma_start(T.win[:, C0:NW], T.x0[:, 0:CUT]), [], [("win", C0, NW)])
     dma(S, "y", lambda: g.sync.dma_start(T.win[:, WASTE:C0], T.x0[:, CUT:8192]), [], [("win", WASTE, C0)])
     iota("pidx", [[0, 1]], 0, 1)
-    for n, x in [("ones", 1.0), ("m120", -120.0), ("thi", 0), ("wd", 0.0), ("lh", 0.0), ("add0", 64.0)]:
+    for n, x in [("ones", 1.0), ("m120", -120.0), ("thi", 0), ("ck", 0.0), ("wd", 0.0), ("lh", 0.0), ("add0", 64.0)]:
         fill(T[n][:], x, n)
     dma(S, "s", lambda: C.dma_start(T.thi[0:128:16, :], T.th[:]), [], ["thi"])
 
@@ -217,8 +218,10 @@ def rank_program(g, core, T, topo):
     select(T.blk1[:], T.ones[:, 0:128], [[-16, 8], [0, 16]], A.is_ge, 0.0, 0, 1, ["ones"], ["blk1"])
     select(T.blk[:], T.blk1[:], [[16, 8], [0, 16]], A.is_ge, 0.0, 15, -1, ["blk1"], ["blk"])
     select(T.eye[:], T.ones[:, 0:128], [[-1, 128]], A.is_equal, 0.0, 0, 1, ["ones"], ["eye"])
-    vs(T.p15i[:], T.pidx[:], 15, None, A.bitwise_and, None, ["pidx"], ["p15i"])
     vs(T.gpi[:], T.pidx[:], 4, 1, A.arith_shift_right, A.bitwise_and, ["pidx"], ["gpi"])
+    vs(T.p15i[:], T.pidx[:], 15, None, A.bitwise_and, None, ["pidx"], ["p15i"])
+    for row, x in ((0, 37.0), (32, 0.125), (64, 2.0 ** -17)):
+        fill(T.ck[row:row + 1, :], x, ("ck", row, row + 1))
     for n, pattern, base, cm in [("jm", [[1, 128]], 128, -1), ("k8", [[1, 8]], 1, 0), ("k16", [[-1, 8]], 15, 0), ("t6", [[1, 6]], 0, 0),
                                  ("e16", [[-1, 16]], 15, 0)]:
         iota(n, pattern, base, cm)
@@ -228,6 +231,8 @@ def rank_program(g, core, T, topo):
     vc(T.gp1[:], T.gpi[:], ["gpi"], ["gp1"])
     vs(T.gp0[:], T.gpi[:], -1.0, 1.0, A.mult, A.add, ["gpi"], ["gp0"])
     vs(T.wa[:], T.wti[:, 0:1], 128.0, None, A.mult, None, ["wti"], ["wa"])
+    vs(T.lu[:, 0:16], T.lfi[:], T.gp0[:, 0:1], None, A.mult, None, ["lfi", "gp0"], [("lu", 0, 16)])
+    vs(T.lu[:, 16:32], T.lfi[:], T.gp1[:, 0:1], None, A.mult, None, ["lfi", "gp1"], [("lu", 16, 32)])
     vc(T.wf[:], T.wti[:], ["wti"], ["wf"])
     for q in range(8):
         if q % 2:
@@ -235,21 +240,15 @@ def rank_program(g, core, T, topo):
         else:
             vs(T.lh[:, q, q % 4::32], T.blk[:, 16 * (q // 4)::32], T.wa[:, 0:1], None, A.mult, None, ["blk", "wa"],
                [("lh", 2 * q, 2 * q + 1)])
-    vs(T.lu[:, 0:16], T.lfi[:], T.gp0[:, 0:1], None, A.mult, None, ["lfi", "gp0"], [("lu", 0, 16)])
-    vs(T.lu[:, 16:32], T.lfi[:], T.gp1[:, 0:1], None, A.mult, None, ["lfi", "gp1"], [("lu", 16, 32)])
     v(lambda: V.transpose(T.lt[:], T.lu[:]), ["lu"], ["lt"])
+    for h in range(2):
+        vc(T.zr[:, :, h, :], T.zi0[:], ["zi0"], [("zr", h, h + 1)])
     vt(T.add0[:, :, 1, :], T.lt[:, 0:16], T.lt[:, 16:32], A.add, ["lt"], ["add0"])
-    fill(T.ck[:], 0.0, "ck")
-    vs(T.ey4[:], T.eye[:], 0.25, None, A.mult, None, ["eye"], ["ey4"])
-    for row, x in ((0, 37.0), (32, 0.125), (64, 2.0 ** -17)):
-        fill(T.ck[row:row + 1, :], x, ("ck", row, row + 1))
     zeros(128, 896)
     for a, b, step, base, by in ((17, 240, 2, 239, -2), (48, 240, 2, 238, -2), (16, 48, 2, 255, -1), (240, 256, 1, 46, -2)):
         op(S, "g", lambda: g.iota(T.plc[:, a:b:step], [[by, len(range(a, b, step))]], base, 0, allow_small_or_imprecise_dtypes=True),
            [], [("plc", a, a + 1)])
-    op(S, "g", lambda: g.iota(T.cw[:, 5120:7168], [[0, 2048]], 0, 0, allow_small_or_imprecise_dtypes=True), [], [("cw", 5120, 7168)])
-    send(nxt, T.wp[:], T.wf[:], "wp", ["wf"])
-    arrival(S, "wp", E, ["wp"])
+    op(S, "g", lambda: g.iota(T.cw[:, 5120:NW], [[0, NW - 5120]], 0, 0, allow_small_or_imprecise_dtypes=True), [], [("cw", 5120, NW)])
 
     def rotations():
         for h, b in enumerate(("pa", "pb")):
@@ -258,7 +257,8 @@ def rank_program(g, core, T, topo):
                 mm(T[b][:, 128 * k:128 * k + 128], T.neye[:], T.ey2[:, :, 4 * h + k + 1:4 * h + k + 17], False, True, ["neye", "ey2"], [b])
             copy(T.sh[:, 4 * h:4 * h + 4, :, :], T[b][:], [b], [("sh", 8 * h + 2, 8 * h + 10)])
 
-    rest = [lambda: vc(T.p15[:], T.p15i[:], ["p15i"], ["p15"]),
+    rest = [lambda: vs(T.ey4[:], T.eye[:], 0.25, None, A.mult, None, ["eye"], ["ey4"]),
+            lambda: vc(T.p15[:], T.p15i[:], ["p15i"], ["p15"]),
             lambda: vs(T.neye[:], T.eye[:], -1.0, None, A.mult, None, ["eye"], ["neye"]),
             lambda: vc(T.ey2[:, :, 0:16], T.eye[:], ["eye"], [("ey2", 0, 1)]),
             lambda: vc(T.ey2[:, :, 16:32], T.eye[:], ["eye"], [("ey2", 1, 2)]),
@@ -280,16 +280,24 @@ def rank_program(g, core, T, topo):
             lambda: fill(T.n128[:], -128.0, "n128"),
             lambda: fill(T.pd[:, :, 16], 1000.0, "pd")]
 
+    later = []
+
     def last_constants():
-        fill(T.cw[:, 7168:NW], 0.0, ("cw", 7168, NW))
         dma(S, "g", lambda: g.dma_start(T.cw[0:128:16, WASTE:C0], T.c0[:, CUT:8192]), [], [("cw", WASTE, C0)])
         dma(S, "g", lambda: g.dma_start(T.cw[0:128:16, C0:NW], T.c0[:, 0:CUT]), [], [("cw", C0, NW)])
+        send(nxt, T.wp[:], T.wf[:], "wp", ["wf"])
+        arrival(S, "wp", E, ["wp"])
+        for a, base, by in [(None, -16, 0), (0, -256, -16), (14, -496, 16), (15, 0, 0)] + [(a, -496, 0) for a in range(2, 14, 2)]:
+            ap, n = (T.e3[:], 272) if a is None else (T.e3[:, a::17], 16)
+            later.append(lambda a=a, ap=ap, n=n, base=base, by=by: op(
+                S, "g", lambda: g.iota(ap, [[by, n]], base, 0, allow_small_or_imprecise_dtypes=True), [],
+                ["e3" if a is None else ("e3", a, a + 1)]))
         rotations()
         vs(T.ph[:, 272:512], T.plc[:, 16:256], BIG, float(WASTE), A.mult, A.add, ["plc"], ["ph"])
 
     def routes():
         for k in range(16):
-            vc(T.rot[:, k, :], T.ey2[:, :, k:k + 16], ["ey2"], [("rot", k, k + 1)])
+            (vc if k < 10 else copy)(T.rot[:, k, :], T.ey2[:, :, k:k + 16], ["ey2"], [("rot", k, k + 1)])
         for k in range(8):
             vs(T.ro[:, k, :], T.dm1[:], T.tk[:, k:k + 1], -BIG, A.is_equal, A.mult, ["dm1", "tk"], [("ro", k, k + 1)])
         fill(T.fw[:], 64.0, "fw")
@@ -301,11 +309,11 @@ def rank_program(g, core, T, topo):
     first_answer = [lambda: vs(T.hd[:, 16::17], T.e16[:], BIG, T.p15[:, 0:1], A.mult, A.add, ["e16", "p15"], [("hd", 16, 17)]),
                     lambda: vs(T.lane[:], T.p15[:], 4080.0, None, A.add, None, ["p15"], ["lane"]),
                     lambda: vc(T.mc[:], T.px[:, 0:1], ["px"], ["mc"]),
-                    lambda: vs(T.th2[:], T.px[:, 0:1], 1024.0, None, A.add, None, ["px"], ["th2"]),
+                    lambda: vs(T.e3[:, 16::17], T.e16[:], -16.0, T.lane[:, 0:1], A.mult, A.add, ["e16", "lane"], [("e3", 16, 17)]),
+                    lambda: vc(T.th2[:], T.px[:, 0:1], ["px"], ["th2"]),
                     lambda: vs(T.sb[:], T.oh[:, 1:6], T.oh[:, 0:1], -BIG, A.subtract, A.mult, ["oh"], ["sb"]),
                     lambda: vs(T.nb[:], T.oh[:, 0:1], -BIG, None, A.mult, None, ["oh"], ["nb"]),
-                    lambda: vs(T.sf[:], T.oh[:, 0:1], -240.0, None, A.mult, None, ["oh"], ["sf"]),
-                    lambda: fill(T.jb[:], 0.5 - 240 * BIG, "jb")]
+                    lambda: vs(T.sf[:], T.oh[:, 0:1], -240.0, None, A.mult, None, ["oh"], ["sf"])]
 
     def sums(t):
         zi = "zi%d" % t
@@ -342,10 +350,24 @@ def rank_program(g, core, T, topo):
 
         def forward():
             if t < 4:
-                fw, to = ("fw", t, t + 1), "add%d" % (t + 1)
-                vs(T.fw[:, t, :, 1, :], T.oa[:, :, 1, :], 8.0, None, A.mult, None, ["oa"], [fw])
-                send(nxt, T[to][:], T.fw[:, t, :, :, :], "fa%d" % (t + 1), [fw])
+                vs(T.fw[:, t, :, 1, :], T.oa[:, :, 1, :], 8.0, None, A.mult, None, ["oa"], [("fw", t, t + 1)])
+
+        def sends():
+            while later:
+                later.pop(0)()
+            if t < 4:
+                to = "add%d" % (t + 1)
+                send(nxt, T[to][:], T.fw[:, t, :, :, :], "fa%d" % (t + 1), [("fw", t, t + 1)])
                 arrival(S, "fa%d" % (t + 1), E, [to])
+
+        def home():
+            if t in (2, 3):
+                send(cores[(rank - t + 1) % N], T["zh%d" % (t - 1)][:], T["zn%d" % (t - 1)][:], "h%d" % (t - 1), ["zn%d" % (t - 1)])
+
+        def leaf():
+            copy(T.xl[:], T.win[:, 0:NW].indirect(T.li[:, 240:256]), ["win", ("li", 240, 256)], ["xl"])
+            mm(T.px[:, 256:512], T.neye[:], T.z1[:, t % 2, :], True, False, ["neye", ("z1", t % 2, t % 2 + 1)], ["px"])
+            mm(T.px[:, 256:512], T.eye[:], T.xl[:], False, True, ["eye", "xl"], ["px"])
 
         def root_pairs():
             for k in range(8):
@@ -367,12 +389,14 @@ def rank_program(g, core, T, topo):
                 vs(T.rt[:, h::2], T.nr[:, h::2], float(WASTE), T[w][:, 0:1], A.add, A.max, ["nr", w], [("rt", h, h + 1)])
 
         return {**wide(0, 176, "a"), **wide(176, 256, "b"), "hf": named_cells, "rt": root_list,
-                "dr": lambda: copy(T.diff[:, 0:256], T.pr[:, 256:512], ["pr"], [("diff", 0, 1)]),
+                "dr": lambda: vc(T.diff[:, 0:256], T.pr[:, 256:512], ["pr"], [("diff", 0, 1)]), "xl": leaf,
+                "al": lambda: s(lambda: C.activation(T.ad[:, :, 15, :], T.px[:, 256:512], F.Abs), ["px"], [("ad", 15, 16)]),
+                "dl": lambda: vc(T.diff[:, 3840:4096], T.px[:, 256:512], ["px"], [("diff", 15, 16)]),
                 "rw": lambda: copy(T.rw[:], T.pr[:, 0:256], ["pr"], ["rw"], bias=127.8, scale=0.5),
                 "turn": lambda: v(lambda: V.transpose(T.ts[:], T.pg[:, :, 0:2, :]), ["pg"], ["ts"]),
                 "oi": lambda: vt(T.oi[:], T.ts[:, :, :, 0, :], T[ad][:], A.add, ["ts", ad], ["oi"]),
                 "oa": lambda: vs(T.oa[:], T.oi[:], 32767, None, A.bitwise_and, None, ["oi"], ["oa"]),
-                "pages": pages, "pairs": root_pairs, "er": equal_roots, "fw": forward,
+                "pages": pages, "pairs": root_pairs, "er": equal_roots, "fw": forward, "sends": sends, "home": home,
                 "l0": level(0, T.raw[:, 64:80]), "l1": level(1, T.raw[:, 33:64:2]), "l2": level(2, T.raw[:, 32:64:2]),
                 "l3": level(3, T.raw[:, 1:32:2]), "l4": level(4, T.raw[:, 0:32:2]),
                 "d4": down(112, 64, 4), "d8": down(48, 64, 8), "d10": down(16, 32, 10),
@@ -384,13 +408,12 @@ def rank_program(g, core, T, topo):
 
     def twice(t):
         zi = "zi%d" % t
-        for h in range(2):
-            if t:
-                select(T.zr[:, :, h, :], T[zi][:], [[0, 256]], A.is_gt, 0.0, 1, 0, [zi], [("zr", h, h + 1)])
-            else:
-                vc(T.zr[:, :, h, :], T[zi][:], [zi], [("zr", h, h + 1)])
-        copy(T.z2[:], T.zr[:], ["zr"], ["z2"])
-        if t:
+        for h in range(2 if t else 0):
+            select(T.zr[:, :, h, :], T[zi][:], [[0, 256]], A.is_gt, 0.0, 1, 0, [zi], [("zr", h, h + 1)])
+        if t == 0:
+            copy(T.z2[:], T.zr[:], ["zr"], ["z2"])
+        else:
+            select(T.z2[:], T.zr[:], [[0, 512]], A.is_gt, 0.0, 1, 0, ["zr"], ["z2"])
             select(T.z1[:, t % 2, :], T[zi][:], [[0, 256]], A.is_gt, 0.0, 1, 0, [zi], [("z1", t % 2, t % 2 + 1)])
 
     def sigmoids(vals, lst, n):
@@ -405,11 +428,11 @@ def rank_program(g, core, T, topo):
             copy(T.mv[:], T.cw[:, 0:NW].indirect(T.li[:, 0:16]), ["cw", ("li", 0, 16), "sm", "bm"], ["mv"], bias=T.bm[:, t + 1:t + 2],
                  scale=T.sm[:, 0:1])
 
-        if t in (2, 3):
-            send(cores[(rank - t + 1) % N], T["zh%d" % (t - 1)][:], T["zn%d" % (t - 1)][:], "h%d" % (t - 1), ["zn%d" % (t - 1)])
         while late:
             late.pop(0)()
         one = ("z1", t % 2, t % 2 + 1)
+        if t == 0:
+            ch["pairs"]()
         copy(T.xr[:], T.win[:, 0:NW].indirect(T.li[:, 0:16]), ["win", ("li", 0, 16)], ["xr"])
         if t:
             root_counters()
@@ -417,17 +440,21 @@ def rank_program(g, core, T, topo):
             mm(T.pr[:, 256 * h:256 * h + 256], T[w][:], T.z1[:, t % 2, :], True, False, [w, one], ["pr"])
             mm(T.pr[:, 256 * h:256 * h + 256], T.eye[:], T.xr[:], False, True, ["eye", "xr"], ["pr"])
         play((AFTER if t else AFTER0).get(0, ""), ch, {"M": marks})
-        for a, b in [(1, 3), (3, 5), (5, 7), (7, 9), (9, 11), (11, 13), (13, 15), (15, 16)]:
-            z, zz = (one, T.z1[:, t % 2, :]) if b - a == 1 else ("z2", T.z2[:])
-            vt(T.diff[:, 256 * a:256 * b], T.win[:, 0:NW].indirect(T.li[:, 16 * a:16 * b]), zz, A.subtract,
-               ["win", ("li", 16 * a, 16 * b), z], [("diff", a, b)])
-            s(lambda: C.activation(T.ad[:, :, a:b, :], T.diff[:, 256 * a:256 * b], F.Abs), [("diff", a, b)], [("ad", a, b)])
-            if b in (5, 9, 13, 16):
-                a0 = b - 4 + b // 16
+        for a in range(1, 15, 2):
+            b = a + 2
+            for c0, c1 in LAST if a == 13 else [(0, 16)]:
+                first = 16 * a + 2 * c0
+                d, key = T.diff[:, 16 * first:16 * first + 32 * (c1 - c0)], (a + c0 / 8, a + c1 / 8)
+                vt(d, T.win[:, 0:NW].indirect(T.li[:, first:first + 2 * (c1 - c0)]), T.z2[:, 32 * c0:32 * c1], A.subtract,
+                   ["win", ("li", 16 * a, 16 * b), "z2"], [("diff",) + key])
+                s(lambda: C.activation(T.ad[:, c0:c1, a:b, :], d, F.Abs), [("diff",) + key], [("ad",) + key])
+            if b in (5, 9, 13, 15):
+                a0, b0 = (b - 4, b) if b < 15 else (13, 16)
                 for i in range(16):
-                    mm(T.pd[:, :, a0:b], lane_w("wd", i), T.ad[:, :, a0:b, i], i == 0, i == 15, ["wd", ("ad", a0, b)], ["pd"])
+                    mm(T.pd[:, :, a0:b0], lane_w("wd", i), T.ad[:, :, a0:b0, i], i == 0, i == 15, ["wd", ("ad", a0, b0)], ["pd"])
             if t == 0 and a == 5:
                 root_counters()
+                thresholds()
             play((AFTER if t else AFTER0).get(a, ""), ch, {"M": marks})
         return marks
 
@@ -439,7 +466,7 @@ def rank_program(g, core, T, topo):
         zn, zi = "zn%d" % t, "zi%d" % t
 
         def new_z():
-            vs(T.lo[:], T.qq[:], -16.0, T.lane[:, 0:1], A.mult, A.add, ["qq", "lane"], ["lo"])
+            vc(T.lo[:], T.sc[:, 16::17], ["sc"], ["lo"])
             s(lambda: C.activation(T[zn][:], T.diff[:, 0:4096].indirect(T.lo[:]), F.Abs), ["diff", "lo"], [zn])
             if t < 4:
                 send(nxt, T["zi%d" % (t + 1)][:], T[zn][:], "za%d" % (t + 1), [zn])
@@ -449,22 +476,21 @@ def rank_program(g, core, T, topo):
 
         def signs():
             if t < 4:
-                s(lambda: C.activation(T.j15[:], T.sn[:, 16::17], F.Sign, bias=T.jb[:, 0:1]), ["sn", "jb"], ["j15"])
+                vs(T.j15[:], T.sn[:, 16::17], 240 * BIG, 2.0, A.is_ge, A.mult, ["sn"], ["j15"])
                 mm(T.px[:, 0:16], T.ones[:, 0:128], T.j15[:], True, True, ["ones", "j15"], ["px"])
 
         def count():
             if t < 4:
-                s(lambda: C.activation(T.junk[:], T.px[:, 0:16], F.Copy, accum_out=T.ac[:]), ["px"], ["junk", "ac"])
+                s(lambda: C.activation(T.j15[:], T.px[:, 0:16], F.Copy, accum_out=T.ac[:]), ["px"], ["j15", "ac"])
 
         def low_part():
             vc(T.hl[:], T.hi[:], ["hi"], ["hl"])
+            for k in range(16):
+                for h in range(2):
+                    mm(T.pr[:, 8 * k:8 * k + 8], T.rot[:, k, :], T.hl[:, 16 * h:16 * h + 16:2], h == 0, h == 1, ["rot", "hl"], ["pr"])
             for k in range(8):
                 for h in range(2):
                     mm(T.pq[:, k, :], T.sh[:, k, :, :], T.hl[:, 16 * h:16 * h + 16], h == 0, h == 1, ["sh", "hl"], ["pq"])
-            for k in range(16):
-                for h in range(2):
-                    mm(T.pg[:, 0, k // 2, 8 * (k % 2):8 * (k % 2) + 8], T.rot[:, k, :], T.hl[:, 16 * h:16 * h + 16:2], h == 0, h == 1,
-                       ["rot", "hl"], ["pg"])
 
         def odd(first):
             for n in range(4 if first else 3):
@@ -478,11 +504,11 @@ def rank_program(g, core, T, topo):
                 mm(T[b][:, 0:16], T.eye[:], T.hl[:, 16 * h:16 * h + 16], h == 0, False, ["eye", "hl"], [b])
             for i in range(16 if 1 in parts else 0):
                 mm(T[b][:, 0:16], lane_w("wd", i), T.nc[:, i::16], False, False, ["wd", "nc"], [b])
-            for k in range(8 if 2 in parts else 0):
-                mm(T[b][:, 0:16], T.ro[:, k, :], T.eq[:, k, :], False, False, ["ro", ("eq", 0, 8)], [b])
             for k in range(16 if 3 in parts else 0):
-                mm(T[b][:, 1:16:2], T.nbe[:], T.eq[:, 8 + k // 2, 8 * (k % 2):8 * (k % 2) + 8], False, k == 15,
+                mm(T[b][:, 1:16:2], T.nbe[:], T.eq[:, 8 + k // 2, 8 * (k % 2):8 * (k % 2) + 8], False, False,
                    ["nbe", ("eq", 8, 16)], [b])
+            for k in range(8 if 2 in parts else 0):
+                mm(T[b][:, 0:16], T.ro[:, k, :], T.eq[:, k, :], False, k == 7, ["ro", ("eq", 0, 8)], [b])
 
         def to_list(name, b):
             for h, w in enumerate(("p15", "p31")):
@@ -496,8 +522,10 @@ def rank_program(g, core, T, topo):
                 for q in range(8):
                     copy(T.lh[:, q, 16 + q % 4::32], T.blk[:, 16 * (q // 4)::32], ["blk", "wp"], [("lh", 2 * q + 1, 2 * q + 2)],
                          scale=T.wp[:, 1:2])
-            if t == 4:
-                vs(T.xa[:], T.wd[:], T.wf[:, 0:1], None, A.mult, None, ["wd", "wf"], ["xa"])
+
+        def weights():
+            if t == 3:
+                copy(T.xa[:], T.wd[:], ["wd", "wf"], ["xa"], scale=T.wf[:, 0:1])
 
         def unless_last(f):
             return f if t < 4 else lambda: None
@@ -505,32 +533,27 @@ def rank_program(g, core, T, topo):
         named = [lambda c=c: vt(T.win[:, 0:NW].indirect(T.rl[:, 2 * c:2 * c + 2]), T.ys[:, 32 * c:32 * c + 32],
                                 T.z1[:, t % 2, 32 * c:32 * c + 32], A.add, ["rl", "ys", ("z1", t % 2, t % 2 + 1)], ["win"])
                  for c in range(7, -1, -1)]
-        play(ANSWER, {
+        return {"R": rs, "M": marks, "N": named, "K": first_answer, "C": sigmoids("nf", "cl", 2)}, {
             "ms": lambda: vs(T.ms[:], T.pd[:, :, 0:17], T.mc[:, 0:1], None, A.is_gt, None, ["pd", "mc"], ["ms"]),
             "sn": lambda: v(lambda: V.tensor_tensor_scan(T.sn[:], T.hd[:], T.ms[:], 0.0, A.max, A.mult), ["hd", "ms"], ["sn"]),
-            "qq": lambda: vs(T.qq[:], T.sn[:, 16::17], 1.0 / BIG, -0.25, A.mult, A.add, ["sn"], ["qq"]),
-            "ri": lambda: vc(T.ri[:], T.sn[:, 16::17], ["sn"], ["ri"]),
-            "signs": signs, "z": new_z, "count": count, "low": low_part, "once": once,
+            "sc": lambda: v(lambda: V.tensor_tensor_scan(T.sc[:], T.ms[:], T.e3[:], 0.0, A.mult, A.add), ["ms", "e3"], ["sc"]),
+            "signs": signs, "z": new_z, "count": count, "parts": low_part, "once": once, "xa": weights,
             "odd1": lambda: odd(True), "odd2": lambda: odd(False),
             "eq": lambda: vs(T.eq[:, 0:8, :], T.pq[:, 0:8, :], 0.0, None, A.is_equal, None, ["pq"], [("eq", 0, 8)]),
-            "eq2": lambda: vt(T.eq[:, 8:16, :], T.pg[:, 0, :, :], T.rp[:], A.is_equal, ["pg", "rp"], [("eq", 8, 16)]),
+            "eq2": lambda: vt(T.eq[:, 8:16, :], T.pr[:, 0:128], T.rp[:], A.is_equal, ["pr", "rp"], [("eq", 8, 16)]),
             "pn": lambda: sum_list("pa", (0, 1)), "pa": lambda: sum_list("pa", (2, 3)),
-            "rn": lambda: vs(T.rn[:], T.ri[:], 16383, None, A.bitwise_and, None, ["ri"], ["rn"]),
-            "h7": lambda: vs(T.hi[:, 0:16], T.ri[:], 16256, None, A.bitwise_and, None, ["ri"], [("hi", 0, 16)]),
-            "l7": lambda: vs(T.hi[:, 16:32], T.ri[:], 127, None, A.bitwise_and, None, ["ri"], [("hi", 16, 32)]),
+            "rn": lambda: vs(T.rn[:], T.sn[:, 16::17], 16383, None, A.bitwise_and, None, ["sn"], ["rn"]),
+            "h7": lambda: vs(T.hi[:, 0:16], T.sn[:, 16::17], 16256, None, A.bitwise_and, None, ["sn"], [("hi", 0, 16)]),
+            "l7": lambda: vs(T.hi[:, 16:32], T.sn[:, 16::17], 127, None, A.bitwise_and, None, ["sn"], [("hi", 16, 32)]),
             "nl": lambda: vc(T.nl[:], T.rn[:], ["rn"], ["nl"]),
             "nc": lambda: copy(T.nc[:], T.cw[:, 0:NW].indirect(T.nl[:]), ["cw", "nl", "sb", "nb"], ["nc"], bias=T.nb[:, 0:1],
                                scale=T.sb[:, t:t + 1]),
             "ys": lambda: copy(T.ys[:], T.diff[:, 0:4096].indirect(T.lo[:]), ["diff", "lo"], ["ys"]),
             "nf": new_counters,
             "at": unless_last(lambda: copy(T.at[:], T.ac[:], ["ac", "th2"], ["at"], bias=T.th2[:, 0:1], scale=0.5)),
-            "rl": lambda: to_list("rl", "pa")},
-            {"R": rs, "M": marks, "N": named, "K": first_answer})
-        return named, sigmoids("nf", "cl", 2), {
-            "pb": lambda: sum_list("pb", (0, 2, 3)),
-            "q16": lambda: vs(T.q16[:], T.ac[:], 1.0 / 32, 63.53125, A.mult, A.add, ["ac"], ["q16"]),
-            "mc": lambda: vs(T.mc[:], T.q16[:], -16.0, T.at[:, 0:1], A.mult, A.add, ["q16", "at"], ["mc"]),
-            "cl": lambda: to_list("cl", "pb")}
+            "rl": lambda: to_list("rl", "pa"), "pb": lambda: sum_list("pb", (0, 2, 3)), "cl": lambda: to_list("cl", "pb"),
+            "q16": lambda: t and vs(T.q16[:], T.ac[:], 1.0 / 32, -0.46875, A.mult, A.add, ["ac"], ["q16"]),
+            "mc": lambda: t and vs(T.mc[:], T.q16[:], -16.0, T.at[:, 0:1], A.mult, A.add, ["q16", "at"], ["mc"])}
 
     sums(0)
     twice(0)
@@ -539,7 +562,6 @@ def rank_program(g, core, T, topo):
     ch = chain(0)
     play(CHAIN0, ch, {"K": rest})
     last_constants()
-    thresholds()
     routes()
     late = []
     for t in range(5):
@@ -549,12 +571,14 @@ def rank_program(g, core, T, topo):
                 arrival(S, sem, len(topo.engines(cores[(rank + u) % N], core)), [b])
                 dma(S, "y", lambda: g.sync.dma_start(T.zs[:, 256 * u:256 * u + 256], T[b][:]), [b], [])
             dma(S, "y", lambda: g.sync.dma_start(T.zs[:, 768:1024], T.zi4[:]), ["zi4"], [])
-        named, late, lists = answer(t, roots(), marks)
-        if t < 4:
-            ch = chain(t + 1)
-            ch.update(lists, twice=lambda: twice(t + 1), sums=lambda: sums(t + 1))
-            play(CHAIN, ch, {"N": named, "C": late})
-    play("pb N N cl N* C*", lists, {"N": named, "C": late})
+        rows, calls = answer(t, roots(), marks)
+        ch = chain(t + 1)
+        ch.update(twice=lambda: twice(t + 1), sums=lambda: sums(t + 1))
+        if t == 4:
+            ch = {name: lambda: None for name in ch}
+        play(ANSWER + " " + CHAIN, {**ch, **calls}, rows)
+        late = rows["C"]
+    play("C*", {}, rows)
     dma(S, "s", lambda: C.dma_start(T.cs[:, 0:CUT], T.cw[0:128:16, C0:NW]), ["cw"], [])
     dma(S, "s", lambda: C.dma_start(T.cs[:, CUT:8192], T.cw[0:128:16, WASTE:C0]), ["cw"], [])
     for b, n, first in (("px", 384, 0), ("pr", 128, 384)):

@@ -4,49 +4,51 @@ WASTE = 32
 NW = WASTE + 8192
 TURN = 919
 C0, CUT = WASTE + TURN, 8192 - TURN
-CHAIN = ("sums pb N turn N oi N oa cl N C C twice home pages pairs l4 l3 l2 l1 N l0 d10 d8 d4 low N wwa bit d0 N hha wwb fw N* "
+FILL = (256, 768, 1536, 3072, 5120, 5632)
+ROT_V = 14
+CHAIN = ("sums N cl turn N C* oi N oa N twice home pages pairs l4 l3 l2 l1 N l0 d10 d8 d4 low N wwa bit d0 N hha wwb fw N "
          "lia wb er")
 CHAIN0 = ("turn K K oi K K oa K K pages l4 l3 l2 l1 l0 K K d10 d8 d4 low bit K K wwa d0 K K hha wwb K K lia wb K K K hhb K K K "
           "lib K*")
-AFTER = {0: "hhb", 1: "lib hf rw nr xl", 3: "rt sends", 5: "al M", 7: "M", 13: "dr dl M M M M M"}
-AFTER0 = {0: "hf", 1: "fw xl", 3: "er rw sends", 5: "al", 7: "nr", 9: "rt", 11: "M", 13: "dr dl M M M M M M"}
-ANSWER = ("R q16 K K K R mc K K K R K K ms R sc sn z R h7 l7 rn signs M* parts nl odd1 nc once pn R ys odd2 nf R count eq2 R* eq pa "
-          "at xa rl")
+AFTER = {0: "mv hhb", 1: "lib hf nr xl", 3: "rt sends", 5: "al M", 7: "M", 13: "rv dr dl M M M M M"}
+AFTER0 = {0: "hf", 1: "fw xl", 3: "er sends", 5: "mv al", 7: "nr", 9: "rt", 11: "M", 13: "rv dr dl M M M M M M"}
+AFTER4 = {0: "mv hhb X X X X", 1: "lib hf rw nr xl X X X X", 3: "rt X X X X", 5: "al xo M X*", 7: "M"}
+ANSWER = ("R q16 K K K R mc K K K R K* ms R sc sn z R h7 l7 rn signs M* parts nl odd1 nc once pn R odd2 ys R odd3 nf count eq2 R* eq "
+          "any pa pb at xa rl")
+ANSWER4 = ("xp q16 dr mc dl M M rx M M M ms sc sn z R h7 l7 rn M* parts nl odd1 nc pn nf R odd2 R odd3 ys R eq2 R eq any pb R cl nx pa "
+           "C R R C rl C N C N C N C N C N C N N N")
 LAST = [(0, 16)]
 BIG = 16384.0
 B2, F4, I4, U2 = "bfloat16", "float32", "int32", "uint16"
-SCRATCH = {"win": ("sbuf", [128, NW], B2), "cw": ("sbuf", [128, NW], F4),
+SCRATCH = {"win": ("sbuf", [128, NW], B2), "cw": ("sbuf", [128, NW], F4), "xw": ("sbuf", [128, NW], F4),
            "sh": ("sbuf", [128, 8, 8, 16], B2),
            "ro": ("sbuf", [128, 8, 128], B2),
            "diff": ("sbuf", [128, 4096], B2),
            "ad": ("sbuf", [128, 16, 16, 16], B2),
            "rot": ("sbuf", [128, 16, 128], B2),
            "ey2": ("sbuf", [128, 8, 32], B2), "zr": ("sbuf", [128, 16, 2, 16], B2),
-           "eye": ("sbuf", [128, 8, 16], B2), "neye": ("sbuf", [128, 8, 16], B2), "lh": ("sbuf", [128, 8, 128], B2),
-           "wd": ("sbuf", [128, 2048], B2),
-           "xa": ("sbuf", [128, 2048], B2),
-           "z1": ("sbuf", [128, 2, 256], B2), "eq": ("sbuf", [128, 16, 16], B2), "er": ("sbuf", [128, 16, 16], B2),
-           "ts": ("sbuf", [128, 4, 2, 4, 4], F4), "oi": ("sbuf", [128, 4, 2, 4], I4), "oa": ("sbuf", [128, 4, 2, 4], I4)}
+           "eye": ("sbuf", [128, 8, 16], B2), "neye": ("sbuf", [128, 8, 16], B2), "lh": ("sbuf", [128, 2, 132], B2),
+           "wd": ("sbuf", [128, 144], B2),
+           "xa": ("sbuf", [128, 144], B2),
+           "z1": ("sbuf", [128, 2, 256], B2), "eq": ("sbuf", [128, 8, 16], B2), "rp": ("sbuf", [128, 8, 16], F4), "er": ("sbuf", [128, 16, 16], B2),
+           "ts": ("sbuf", [128, 4, 2, 4, 4], F4), "oi": ("sbuf", [128, 4, 2, 4], I4), "oa": ("sbuf", [128, 4, 2, 4], I4),
+           "zi": ("sbuf", [128, 5, 4, 4, 16], B2), "zn": ("sbuf", [128, 5, 256], B2),
+           "fa": ("sbuf", [128, 5, 4, 2, 4], F4), "fw": ("sbuf", [128, 4, 4, 2, 4], F4), "xo": ("sbuf", [128, 2, 256], F4)}
 PSUM = {"pg": [128, 4, 8, 16], "pq": [128, 32, 16], "pa": [128, 512], "pb": [128, 512], "pr": [128, 512],
         "ph": [128, 512], "px": [128, 512], "pd": [128, 16, 32]}
 for _n in PSUM:
     SCRATCH[_n] = ("psum", PSUM[_n], F4)
-for _d, _l in ((B2, "ones:256 blk1:128 blk:128 xr:256 xl:256 ey4:128 ck:128 dm:128 dm1:128 nbe:128 n128:32 thb:1 j15:16 hl:32 pp:16 rw:256 zh1:256 zh2:256 z2:512 "
-                    "ys:256 nc:256"),
+for _d, _l in ((B2, "ones:256 blk1:128 blk:128 xb:128 xr:256 xl:256 ey4:128 ck:128 dm:128 dm1:128 nbe:128 n128:256 thb:1 j15:16 hl:32 "
+                    "pp:16 rw:256 zh1:256 zh2:256 z2:512 ys:256 nc:256 eb:128 mk:128 sa:128"),
                (F4, "p15:1 p31:1 lane:1 gp1:1 gp0:1 wf:2 wa:1 wp:2 th2:1 mc:1 lu:32 lt:32 e16:16 plc:256 hf:256 "
-                    "hd:272 ms:272 e3:272 sc:272 ac:1 at:1 nr:16 mv:256 nf:256 xo:512 k8:8 k16:8 tk:8 tl:8 t6:6 oh:6 bm:6 sb:5 "
-                    "rp:128 sm:1 sf:1 nb:1 m120:1"),
+                    "hd:272 ms:272 e3:272 sc:272 ac:1 at:1 nr:16 mv:256 nf:256 k8:8 k16:8 tk:8 tl:8 t6:6 oh:6 bm:6 sb:5 "
+                    "rx:256 nx:256 sm:1 sf:1 nb:1 m120:1"),
                (I4, "pidx:1 p15i:1 gpi:1 wti:2 thi:1 lfi:16 raw:80 r12:80 ss:256 bi:80 ww:256 hh:256 q16:1 sn:272 rn:16 hi:32 jm:128 jn:128"),
                (U2, "li:256 lo:16 nl:16 rl:16 cl:16 rt:16")):
     for _x in _l.split():
         SCRATCH[_x.split(":")[0]] = ("sbuf", [128, int(_x.split(":")[1])], _d)
-for _t in range(5):
-    SCRATCH["zi%d" % _t] = ("sbuf", [128, 4, 4, 16], B2)
-    SCRATCH["zn%d" % _t] = ("sbuf", [128, 256], B2)
-    SCRATCH["add%d" % _t] = ("sbuf", [128, 4, 2, 4], F4)
-SCRATCH["fw"] = ("sbuf", [128, 4, 4, 2, 4], F4)
 SEMAPHORES = ["qv", "qt", "qs", "qg", "ls", "wp", "h1", "h2"] + ["za%d" % t for t in range(1, 5)] + \
-    ["fa%d" % t for t in range(1, 5)] + ["d%d" % k for k in range(18)]
+    ["fa%d" % t for t in range(1, 5)] + ["d%d" % k for k in range(22)]
 
 
 def state(g, T):
@@ -197,24 +199,33 @@ def rank_program(g, core, T, topo):
         return buf[:, first + (a - 1) % 2:first + 32:2]
 
     def lane_w(name, i):
-        return T[name][:, 128 * i:128 * i + 128]
+        return T[name][:, 15 - i:143 - i]
+
+    def sum_weights(first, w, key, on):
+        for h in range(2):
+            o, i, at = T.lh[:, h, first:131:32], T.blk[:, 16 * h::32], ("lh", 2 * (first // 16) + h, 2 * (first // 16) + h + 1)
+            if on == "s":
+                copy(o, i, ["blk", key], [at], scale=w)
+            else:
+                vs(o, i, w, None, A.mult, None, ["blk", key], [at])
 
     dma(S, "y", lambda: g.sync.dma_start(T.wti[:], T.wt[:]), [], ["wti"])
     dma(S, "s", lambda: C.dma_start(T.lfi[:], T.leaf[:]), [], ["lfi"])
-    dma(S, "y", lambda: g.sync.dma_start(T.zi0[:], T.z0[:]), [], ["zi0"])
+    dma(S, "y", lambda: g.sync.dma_start(T.zi[:, 0, :, :, :], T.z0[:]), [], ["zi0"])
     dma(S, "s", lambda: C.dma_start(T.z1[:, 0, :], T.z0[:]), [], [("z1", 0, 1)])
     dma(S, "y", lambda: g.sync.dma_start(T.win[:, C0:NW], T.x0[:, 0:CUT]), [], [("win", C0, NW)])
     dma(S, "y", lambda: g.sync.dma_start(T.win[:, WASTE:C0], T.x0[:, CUT:8192]), [], [("win", WASTE, C0)])
     iota("pidx", [[0, 1]], 0, 1)
-    for n, x in [("ones", 1.0), ("m120", -120.0), ("thi", 0), ("ck", 0.0), ("wd", 0.0), ("lh", 0.0), ("add0", 64.0)]:
+    for n, x in [("ones", 1.0), ("m120", -120.0), ("thi", 0), ("ck", 0.0), ("wd", 0.0), ("lh", 0.0)]:
         fill(T[n][:], x, n)
+    fill(T.fa[:, 0, :, :, :], 64.0, "fa0")
     dma(S, "s", lambda: C.dma_start(T.thi[0:128:16, :], T.th[:]), [], ["thi"])
 
-    def zeros(a, n, src="wd"):
-        s(lambda: C.activation(T.cw[:, a:a + n], T[src][:, 0:n], F.Sigmoid, bias=T.m120[:, 0:1], scale=0.0), [src, "m120"],
-          [("cw", a, a + n)])
+    def zeros(a, b, src="cw"):
+        s(lambda: C.activation(T.cw[:, a:b], T[src][:, 0:b - a], F.Sigmoid, bias=T.m120[:, 0:1], scale=0.0),
+          [(src, 0, b - a), "m120"], [("cw", a, b)])
 
-    zeros(0, 128, "ones")
+    zeros(0, FILL[0], "ones")
     select(T.blk1[:], T.ones[:, 0:128], [[-16, 8], [0, 16]], A.is_ge, 0.0, 0, 1, ["ones"], ["blk1"])
     select(T.blk[:], T.blk1[:], [[16, 8], [0, 16]], A.is_ge, 0.0, 15, -1, ["blk1"], ["blk"])
     select(T.eye[:], T.ones[:, 0:128], [[-1, 128]], A.is_equal, 0.0, 0, 1, ["ones"], ["eye"])
@@ -226,29 +237,26 @@ def rank_program(g, core, T, topo):
                                  ("e16", [[-1, 16]], 15, 0)]:
         iota(n, pattern, base, cm)
 
-    for gr in range(8):
-        copy(T.wd[:, 16 * gr::129], T.blk[:, 16 * gr:16 * gr + 16], ["blk"], ["wd"] if gr == 0 else [("wd", gr, gr + 1)])
     vc(T.gp1[:], T.gpi[:], ["gpi"], ["gp1"])
     vs(T.gp0[:], T.gpi[:], -1.0, 1.0, A.mult, A.add, ["gpi"], ["gp0"])
+    fill(T.cw[:, FILL[0]:FILL[1]], 0.0, ("cw", FILL[0], FILL[1]))
+    zeros(FILL[1], FILL[2])
+    zeros(FILL[2], FILL[3])
+    vc(T.wd[:, 15:143:16], T.blk[:, 0::16], ["blk"], ["wd"])
     vs(T.wa[:], T.wti[:, 0:1], 128.0, None, A.mult, None, ["wti"], ["wa"])
     vs(T.lu[:, 0:16], T.lfi[:], T.gp0[:, 0:1], None, A.mult, None, ["lfi", "gp0"], [("lu", 0, 16)])
     vs(T.lu[:, 16:32], T.lfi[:], T.gp1[:, 0:1], None, A.mult, None, ["lfi", "gp1"], [("lu", 16, 32)])
     vc(T.wf[:], T.wti[:], ["wti"], ["wf"])
-    for q in range(8):
-        if q % 2:
-            copy(T.lh[:, q, q % 4::32], T.blk[:, 16 * (q // 4)::32], ["blk", "wa"], [("lh", 2 * q, 2 * q + 1)], scale=T.wa[:, 0:1])
-        else:
-            vs(T.lh[:, q, q % 4::32], T.blk[:, 16 * (q // 4)::32], T.wa[:, 0:1], None, A.mult, None, ["blk", "wa"],
-               [("lh", 2 * q, 2 * q + 1)])
+    sum_weights(3, T.wa[:, 0:1], "wa", "v")
     v(lambda: V.transpose(T.lt[:], T.lu[:]), ["lu"], ["lt"])
     for h in range(2):
-        vc(T.zr[:, :, h, :], T.zi0[:], ["zi0"], [("zr", h, h + 1)])
-    vt(T.add0[:, :, 1, :], T.lt[:, 0:16], T.lt[:, 16:32], A.add, ["lt"], ["add0"])
-    zeros(128, 896)
+        vc(T.zr[:, :, h, :], T.zi[:, 0, :, :, :], ["zi0"], [("zr", h, h + 1)])
+    vt(T.fa[:, 0, :, 1, :], T.lt[:, 0:16], T.lt[:, 16:32], A.add, ["lt"], ["fa0"])
     for a, b, step, base, by in ((17, 240, 2, 239, -2), (48, 240, 2, 238, -2), (16, 48, 2, 255, -1), (240, 256, 1, 46, -2)):
         op(S, "g", lambda: g.iota(T.plc[:, a:b:step], [[by, len(range(a, b, step))]], base, 0, allow_small_or_imprecise_dtypes=True),
            [], [("plc", a, a + 1)])
-    op(S, "g", lambda: g.iota(T.cw[:, 5120:NW], [[0, NW - 5120]], 0, 0, allow_small_or_imprecise_dtypes=True), [], [("cw", 5120, NW)])
+    op(S, "g", lambda: g.iota(T.cw[:, FILL[5]:NW], [[0, NW - FILL[5]]], 0, 0, allow_small_or_imprecise_dtypes=True), [],
+       [("cw", FILL[5], NW)])
 
     def rotations():
         for h, b in enumerate(("pa", "pb")):
@@ -277,10 +285,8 @@ def rank_program(g, core, T, topo):
             lambda: vs(T.nbe[:], T.eye[:], -BIG, None, A.mult, None, ["eye"], ["nbe"]),
             lambda: fill(T.hd[:, 0::17], 0.0, ("hd", 0, 1)),
             lambda: fill(T.pd[:, :, 0], 0.0, "pd"),
-            lambda: fill(T.n128[:], -128.0, "n128"),
+            lambda: fill(T.n128[:, 0:32], -128.0, "n128"),
             lambda: fill(T.pd[:, :, 16], 1000.0, "pd")]
-
-    later = []
 
     def last_constants():
         dma(S, "g", lambda: g.dma_start(T.cw[0:128:16, WASTE:C0], T.c0[:, CUT:8192]), [], [("cw", WASTE, C0)])
@@ -289,15 +295,14 @@ def rank_program(g, core, T, topo):
         arrival(S, "wp", E, ["wp"])
         for a, base, by in [(None, -16, 0), (0, -256, -16), (14, -496, 16), (15, 0, 0)] + [(a, -496, 0) for a in range(2, 14, 2)]:
             ap, n = (T.e3[:], 272) if a is None else (T.e3[:, a::17], 16)
-            later.append(lambda a=a, ap=ap, n=n, base=base, by=by: op(
-                S, "g", lambda: g.iota(ap, [[by, n]], base, 0, allow_small_or_imprecise_dtypes=True), [],
-                ["e3" if a is None else ("e3", a, a + 1)]))
+            op(S, "g", lambda: g.iota(ap, [[by, n]], base, 0, allow_small_or_imprecise_dtypes=True), [],
+               ["e3" if a is None else ("e3", a, a + 1)])
         rotations()
         vs(T.ph[:, 272:512], T.plc[:, 16:256], BIG, float(WASTE), A.mult, A.add, ["plc"], ["ph"])
 
     def routes():
         for k in range(16):
-            (vc if k < 10 else copy)(T.rot[:, k, :], T.ey2[:, :, k:k + 16], ["ey2"], [("rot", k, k + 1)])
+            (vc if k < ROT_V else copy)(T.rot[:, k, :], T.ey2[:, :, k:k + 16], ["ey2"], [("rot", k, k + 1)])
         for k in range(8):
             vs(T.ro[:, k, :], T.dm1[:], T.tk[:, k:k + 1], -BIG, A.is_equal, A.mult, ["dm1", "tk"], [("ro", k, k + 1)])
         fill(T.fw[:], 64.0, "fw")
@@ -309,21 +314,20 @@ def rank_program(g, core, T, topo):
     first_answer = [lambda: vs(T.hd[:, 16::17], T.e16[:], BIG, T.p15[:, 0:1], A.mult, A.add, ["e16", "p15"], [("hd", 16, 17)]),
                     lambda: vs(T.lane[:], T.p15[:], 4080.0, None, A.add, None, ["p15"], ["lane"]),
                     lambda: vc(T.mc[:], T.px[:, 0:1], ["px"], ["mc"]),
+                    lambda: fill(T.mk[:], 1.0, "mk"),
                     lambda: vs(T.e3[:, 16::17], T.e16[:], -16.0, T.lane[:, 0:1], A.mult, A.add, ["e16", "lane"], [("e3", 16, 17)]),
                     lambda: vc(T.th2[:], T.px[:, 0:1], ["px"], ["th2"]),
+                    lambda: fill(T.mk[:, 0::16], 0.0, "mk"),
                     lambda: vs(T.sb[:], T.oh[:, 1:6], T.oh[:, 0:1], -BIG, A.subtract, A.mult, ["oh"], ["sb"]),
                     lambda: vs(T.nb[:], T.oh[:, 0:1], -BIG, None, A.mult, None, ["oh"], ["nb"]),
                     lambda: vs(T.sf[:], T.oh[:, 0:1], -240.0, None, A.mult, None, ["oh"], ["sf"])]
 
     def sums(t):
-        zi = "zi%d" % t
         for q in range(8):
-            mm(T.pg[:, :, q // 4, :], T.lh[:, q, :], T[zi][:, :, q % 4, :], q % 4 == 0, q % 4 == 3,
-               [("lh", 2 * q, 2 * q + (2 if t else 1)), zi], ["pg"])
+            mm(T.pg[:, :, q // 4, :], T.lh[:, q // 4, 3 - q % 4:131 - q % 4], T.zi[:, t, :, q % 4, :], q % 4 == 0, q % 4 == 3,
+               ["lh", "zi%d" % t], ["pg"])
 
     def chain(t):
-        ad = "add%d" % t
-
         def down(a, w, n):
             return lambda: vs(T.ss[:, a:a + w], T.raw[:, 0:w], 0.5 ** n, 2451.5 + 0.5 ** (n + 1), A.mult, A.add, [("raw", 1, 5)],
                               [("ss", a, a + w)])
@@ -353,16 +357,13 @@ def rank_program(g, core, T, topo):
                 vs(T.fw[:, t, :, 1, :], T.oa[:, :, 1, :], 8.0, None, A.mult, None, ["oa"], [("fw", t, t + 1)])
 
         def sends():
-            while later:
-                later.pop(0)()
             if t < 4:
-                to = "add%d" % (t + 1)
-                send(nxt, T[to][:], T.fw[:, t, :, :, :], "fa%d" % (t + 1), [("fw", t, t + 1)])
-                arrival(S, "fa%d" % (t + 1), E, [to])
+                send(nxt, T.fa[:, t + 1, :, :, :], T.fw[:, t, :, :, :], "fa%d" % (t + 1), [("fw", t, t + 1)])
+                arrival(S, "fa%d" % (t + 1), E, ["fa%d" % (t + 1)])
 
         def home():
             if t in (2, 3):
-                send(cores[(rank - t + 1) % N], T["zh%d" % (t - 1)][:], T["zn%d" % (t - 1)][:], "h%d" % (t - 1), ["zn%d" % (t - 1)])
+                send(cores[(rank - t + 1) % N], T["zh%d" % (t - 1)][:], T.zn[:, t - 1, :], "h%d" % (t - 1), ["zn%d" % (t - 1)])
 
         def leaf():
             copy(T.xl[:], T.win[:, 0:NW].indirect(T.li[:, 240:256]), ["win", ("li", 240, 256)], ["xl"])
@@ -388,13 +389,28 @@ def rank_program(g, core, T, topo):
             for h, w in enumerate(("p15", "p31")):
                 vs(T.rt[:, h::2], T.nr[:, h::2], float(WASTE), T[w][:, 0:1], A.add, A.max, ["nr", w], [("rt", h, h + 1)])
 
-        return {**wide(0, 176, "a"), **wide(176, 256, "b"), "hf": named_cells, "rt": root_list,
+        def root_sums():
+            mm(T.pb[:, 0:256], T.xb[:], T.n128[:], True, False, ["xb", "n128"], ["pb"])
+            mm(T.pb[:, 0:256], T.xb[:], T.rw[:], False, True, ["xb", "rw"], ["pb"])
+            copy(T.rx[:], T.pb[:, 0:256], ["pb"], ["rx"])
+
+        def all_sums(h):
+            a, b = WASTE + 4096 * h, ("pg", "pb")[h]
+            (copy, vc)[h](T.xo[:, h, :], (T.pg[:, 0:2, :, :], T.pb[:, 256:512])[h], [b], [("xo", h, h + 1)])
+            dma(S, "y", lambda: g.sync.dma_start(T.xw[0:128:16, a:a + 4096], T.xo[:, h, :]), [("xo", h, h + 1)], [("xw", a, a + 4096)])
+
+        return {**wide(0, 176, "a"), **wide(176, 256, "b"), "hf": named_cells, "rt": root_list, "rx": root_sums,
+                "xo": lambda: all_sums(0), "xp": lambda: all_sums(1),
                 "dr": lambda: vc(T.diff[:, 0:256], T.pr[:, 256:512], ["pr"], [("diff", 0, 1)]), "xl": leaf,
                 "al": lambda: s(lambda: C.activation(T.ad[:, :, 15, :], T.px[:, 256:512], F.Abs), ["px"], [("ad", 15, 16)]),
                 "dl": lambda: vc(T.diff[:, 3840:4096], T.px[:, 256:512], ["px"], [("diff", 15, 16)]),
                 "rw": lambda: copy(T.rw[:], T.pr[:, 0:256], ["pr"], ["rw"], bias=127.8, scale=0.5),
+                "rv": lambda: vs(T.rw[:], T.pr[:, 0:256], 0.5, 127.8, A.mult, A.add, ["pr"], ["rw"]),
+                "lv": lambda: vt(T.diff[:, 3840:4096], T.win[:, 0:NW].indirect(T.li[:, 240:256]), T.z1[:, t % 2, :], A.subtract,
+                                 ["win", ("li", 240, 256), ("z1", t % 2, t % 2 + 1)], [("diff", 15, 16)]),
+                "av": lambda: s(lambda: C.activation(T.ad[:, :, 15, :], T.diff[:, 3840:4096], F.Abs), [("diff", 15, 16)], [("ad", 15, 16)]),
                 "turn": lambda: v(lambda: V.transpose(T.ts[:], T.pg[:, :, 0:2, :]), ["pg"], ["ts"]),
-                "oi": lambda: vt(T.oi[:], T.ts[:, :, :, 0, :], T[ad][:], A.add, ["ts", ad], ["oi"]),
+                "oi": lambda: vt(T.oi[:], T.ts[:, :, :, 0, :], T.fa[:, t, :, :, :], A.add, ["ts", "fa%d" % t], ["oi"]),
                 "oa": lambda: vs(T.oa[:], T.oi[:], 32767, None, A.bitwise_and, None, ["oi"], ["oa"]),
                 "pages": pages, "pairs": root_pairs, "er": equal_roots, "fw": forward, "sends": sends, "home": home,
                 "l0": level(0, T.raw[:, 64:80]), "l1": level(1, T.raw[:, 33:64:2]), "l2": level(2, T.raw[:, 32:64:2]),
@@ -407,14 +423,14 @@ def rank_program(g, core, T, topo):
                 "nr": lambda: vt(T.nr[:], T.hh[:, 0:16], T.pa[:, 0:16], A.add, [("hh", 0, 16), "pa"], ["nr"])}
 
     def twice(t):
-        zi = "zi%d" % t
+        zi, z = "zi%d" % t, T.zi[:, t, :, :, :]
         for h in range(2 if t else 0):
-            select(T.zr[:, :, h, :], T[zi][:], [[0, 256]], A.is_gt, 0.0, 1, 0, [zi], [("zr", h, h + 1)])
+            select(T.zr[:, :, h, :], z, [[0, 256]], A.is_gt, 0.0, 1, 0, [zi], [("zr", h, h + 1)])
         if t == 0:
             copy(T.z2[:], T.zr[:], ["zr"], ["z2"])
         else:
             select(T.z2[:], T.zr[:], [[0, 512]], A.is_gt, 0.0, 1, 0, ["zr"], ["z2"])
-            select(T.z1[:, t % 2, :], T[zi][:], [[0, 256]], A.is_gt, 0.0, 1, 0, [zi], [("z1", t % 2, t % 2 + 1)])
+            select(T.z1[:, t % 2, :], z, [[0, 256]], A.is_gt, 0.0, 1, 0, [zi], [("z1", t % 2, t % 2 + 1)])
 
     def sigmoids(vals, lst, n):
         return [lambda c=c: s(lambda: C.activation(T.cw[:, 0:NW].indirect(T[lst][:, 2 * c:2 * c + n]),
@@ -424,22 +440,27 @@ def rank_program(g, core, T, topo):
     def gather(t, late, ch):
         marks = sigmoids("mv", "rt", 2)
 
+        def two(n):
+            for q in (n, n + 1):
+                mm((T.pg[:, 0:2, :, :], T.pb[:, 256:512])[q // 16], lane_w("xa", q % 16), T.win[:, WASTE + 256 * q:WASTE + 256 * q + 256],
+                   q % 16 == 0, q % 16 == 15, ["xa", "win"], [("pg", "pb")[q // 16]])
+
+        rows = {"M": marks, "C": late, "X": [lambda n=n: two(n) for n in range(0, 32 if t == 4 else 0, 2)]}
+        after = {0: AFTER0, 4: AFTER4}.get(t, AFTER)
+
         def root_counters():
             copy(T.mv[:], T.cw[:, 0:NW].indirect(T.li[:, 0:16]), ["cw", ("li", 0, 16), "sm", "bm"], ["mv"], bias=T.bm[:, t + 1:t + 2],
                  scale=T.sm[:, 0:1])
 
-        while late:
-            late.pop(0)()
+        ch = {**ch, "mv": root_counters}
         one = ("z1", t % 2, t % 2 + 1)
         if t == 0:
             ch["pairs"]()
         copy(T.xr[:], T.win[:, 0:NW].indirect(T.li[:, 0:16]), ["win", ("li", 0, 16)], ["xr"])
-        if t:
-            root_counters()
         for h, w in enumerate(("eye", "neye")):
             mm(T.pr[:, 256 * h:256 * h + 256], T[w][:], T.z1[:, t % 2, :], True, False, [w, one], ["pr"])
             mm(T.pr[:, 256 * h:256 * h + 256], T.eye[:], T.xr[:], False, True, ["eye", "xr"], ["pr"])
-        play((AFTER if t else AFTER0).get(0, ""), ch, {"M": marks})
+        play(after.get(0, ""), ch, rows)
         for a in range(1, 15, 2):
             b = a + 2
             for c0, c1 in LAST if a == 13 else [(0, 16)]:
@@ -453,60 +474,59 @@ def rank_program(g, core, T, topo):
                 for i in range(16):
                     mm(T.pd[:, :, a0:b0], lane_w("wd", i), T.ad[:, :, a0:b0, i], i == 0, i == 15, ["wd", ("ad", a0, b0)], ["pd"])
             if t == 0 and a == 5:
-                root_counters()
                 thresholds()
-            play((AFTER if t else AFTER0).get(a, ""), ch, {"M": marks})
+            play(after.get(a, ""), ch, rows)
         return marks
 
-    def roots():
-        return [lambda c=c: vt(T.win[:, 0:NW].indirect(T.rt[:, 2 * c:2 * c + 2]), T.rw[:, 32 * c:32 * c + 32], T.n128[:], A.add,
-                               ["rt", "rw", "n128"], ["win"]) for c in range(7, -1, -1)]
+    def scatters(t, lst, x, y, sums_):
+        if t == 4:
+            return [lambda c=c: vc(T.xw[:, 0:NW].indirect(T[lst][:, 2 * c:2 * c + 2]), T[sums_][:, 32 * c:32 * c + 32], [lst, sums_], ["xw"])
+                    for c in range(7, -1, -1)]
+        return [lambda c=c: vt(T.win[:, 0:NW].indirect(T[lst][:, 2 * c:2 * c + 2]), T[x][:, 32 * c:32 * c + 32],
+                               T.n128[:, 0:32] if y == "n128" else T.z1[:, t % 2, 32 * c:32 * c + 32], A.add, [lst, x, y], ["win"])
+                for c in range(7, -1, -1)]
 
-    def answer(t, rs, marks):
-        zn, zi = "zn%d" % t, "zi%d" % t
+    def answer(t, marks):
+        zn, one = "zn%d" % t, ("z1", t % 2, t % 2 + 1)
 
         def new_z():
             vc(T.lo[:], T.sc[:, 16::17], ["sc"], ["lo"])
-            s(lambda: C.activation(T[zn][:], T.diff[:, 0:4096].indirect(T.lo[:]), F.Abs), ["diff", "lo"], [zn])
+            s(lambda: C.activation(T.zn[:, t, :], T.diff[:, 0:4096].indirect(T.lo[:]), F.Abs), ["diff", "lo"], [zn])
             if t < 4:
-                send(nxt, T["zi%d" % (t + 1)][:], T[zn][:], "za%d" % (t + 1), [zn])
+                send(nxt, T.zi[:, t + 1, :, :, :], T.zn[:, t, :], "za%d" % (t + 1), [zn])
                 arrival(S, "za%d" % (t + 1), E, ["zi%d" % (t + 1)])
             if t in (0, 4):
-                dma(S, "y", lambda: g.sync.dma_start(T.zs[:, 256 * t:256 * t + 256], T[zn][:]), [zn], [])
+                dma(S, "y", lambda: g.sync.dma_start(T.zs[:, 256 * t:256 * t + 256], T.zn[:, t, :]), [zn], [])
 
         def signs():
-            if t < 4:
-                vs(T.j15[:], T.sn[:, 16::17], 240 * BIG, 2.0, A.is_ge, A.mult, ["sn"], ["j15"])
-                mm(T.px[:, 0:16], T.ones[:, 0:128], T.j15[:], True, True, ["ones", "j15"], ["px"])
+            vs(T.j15[:], T.sn[:, 16::17], 240 * BIG, 2.0, A.is_ge, A.mult, ["sn"], ["j15"])
+            mm(T.px[:, 0:16], T.ones[:, 0:128], T.j15[:], True, True, ["ones", "j15"], ["px"])
 
         def count():
-            if t < 4:
-                s(lambda: C.activation(T.j15[:], T.px[:, 0:16], F.Copy, accum_out=T.ac[:]), ["px"], ["j15", "ac"])
+            s(lambda: C.activation(T.j15[:], T.px[:, 0:16], F.Copy, accum_out=T.ac[:]), ["px"], ["j15", "ac"])
 
         def low_part():
             vc(T.hl[:], T.hi[:], ["hi"], ["hl"])
             for k in range(16):
                 for h in range(2):
-                    mm(T.pr[:, 8 * k:8 * k + 8], T.rot[:, k, :], T.hl[:, 16 * h:16 * h + 16:2], h == 0, h == 1, ["rot", "hl"], ["pr"])
+                    mm(T.pr[:, k:128:16], T.rot[:, k, :], T.hl[:, 16 * h:16 * h + 16:2], h == 0, h == 1, ["rot", "hl"], ["pr"])
             for k in range(8):
                 for h in range(2):
                     mm(T.pq[:, k, :], T.sh[:, k, :, :], T.hl[:, 16 * h:16 * h + 16], h == 0, h == 1, ["sh", "hl"], ["pq"])
 
-        def odd(first):
-            for n in range(4 if first else 3):
-                if first:
-                    vc(T.rp[:, 8 * n:8 * n + 8], T.rn[:, 1::2], ["rn"], [("rp", 8 * n, 8 * n + 8)])
-                else:
-                    vc(T.rp[:, 32 * n + 32:32 * n + 64], T.rp[:, 0:32], [("rp", 0, 32)], [("rp", 32 * n + 32, 32 * n + 64)])
+        def odd(n):
+            for k in range(0 if n else 4):
+                vc(T.rp[:, :, k], T.rn[:, 1::2], ["rn"], [("rp", k, k + 1)])
+            if n:
+                vc(T.rp[:, :, n:2 * n], T.rp[:, :, 0:n], [("rp", 0, n)], [("rp", n, 2 * n)])
 
         def sum_list(b, parts):
             for h in range(2 if 0 in parts else 0):
                 mm(T[b][:, 0:16], T.eye[:], T.hl[:, 16 * h:16 * h + 16], h == 0, False, ["eye", "hl"], [b])
             for i in range(16 if 1 in parts else 0):
                 mm(T[b][:, 0:16], lane_w("wd", i), T.nc[:, i::16], False, False, ["wd", "nc"], [b])
-            for k in range(16 if 3 in parts else 0):
-                mm(T[b][:, 1:16:2], T.nbe[:], T.eq[:, 8 + k // 2, 8 * (k % 2):8 * (k % 2) + 8], False, False,
-                   ["nbe", ("eq", 8, 16)], [b])
+            if 3 in parts:
+                mm(T[b][:, 1:16:2], T.nbe[:], T.sa[:, 15::16], False, False, ["nbe", "sa"], [b])
             for k in range(8 if 2 in parts else 0):
                 mm(T[b][:, 0:16], T.ro[:, k, :], T.eq[:, k, :], False, k == 7, ["ro", ("eq", 0, 8)], [b])
 
@@ -519,28 +539,30 @@ def rank_program(g, core, T, topo):
 
         def once():
             if t == 0:
-                for q in range(8):
-                    copy(T.lh[:, q, 16 + q % 4::32], T.blk[:, 16 * (q // 4)::32], ["blk", "wp"], [("lh", 2 * q + 1, 2 * q + 2)],
-                         scale=T.wp[:, 1:2])
+                sum_weights(19, T.wp[:, 1:2], "wp", "s")
 
         def weights():
-            if t == 3:
+            if t == 1:
                 copy(T.xa[:], T.wd[:], ["wd", "wf"], ["xa"], scale=T.wf[:, 0:1])
+            if t == 2:
+                copy(T.xb[:], T.blk[:], ["blk", "wf"], ["xb"], scale=T.wf[:, 0:1])
+                copy(T.n128[:, 32:256], T.ones[:, 32:256], ["ones"], [("n128", 32, 256)], scale=-128.0)
 
-        def unless_last(f):
-            return f if t < 4 else lambda: None
+        def named_sums():
+            mm(T.px[:, 0:256], T.xb[:], T.z1[:, t % 2, :], True, False, ["xb", one], ["px"])
+            mm(T.px[:, 0:256], T.xb[:], T.ys[:], False, True, ["xb", "ys"], ["px"])
+            copy(T.nx[:], T.px[:, 0:256], ["px"], ["nx"])
 
-        named = [lambda c=c: vt(T.win[:, 0:NW].indirect(T.rl[:, 2 * c:2 * c + 2]), T.ys[:, 32 * c:32 * c + 32],
-                                T.z1[:, t % 2, 32 * c:32 * c + 32], A.add, ["rl", "ys", ("z1", t % 2, t % 2 + 1)], ["win"])
-                 for c in range(7, -1, -1)]
-        return {"R": rs, "M": marks, "N": named, "K": first_answer, "C": sigmoids("nf", "cl", 2)}, {
+        return {"R": scatters(t, "rt", "rw", "n128", "rx"), "M": marks, "N": scatters(t, "rl", "ys", one, "nx"), "K": first_answer,
+                "C": sigmoids("nf", "cl", 2)}, {
             "ms": lambda: vs(T.ms[:], T.pd[:, :, 0:17], T.mc[:, 0:1], None, A.is_gt, None, ["pd", "mc"], ["ms"]),
             "sn": lambda: v(lambda: V.tensor_tensor_scan(T.sn[:], T.hd[:], T.ms[:], 0.0, A.max, A.mult), ["hd", "ms"], ["sn"]),
             "sc": lambda: v(lambda: V.tensor_tensor_scan(T.sc[:], T.ms[:], T.e3[:], 0.0, A.mult, A.add), ["ms", "e3"], ["sc"]),
-            "signs": signs, "z": new_z, "count": count, "parts": low_part, "once": once, "xa": weights,
-            "odd1": lambda: odd(True), "odd2": lambda: odd(False),
+            "signs": signs, "z": new_z, "count": count, "parts": low_part, "once": once, "xa": weights, "nx": named_sums,
+            "odd1": lambda: odd(0), "odd2": lambda: odd(4), "odd3": lambda: odd(8),
+            "any": lambda: v(lambda: V.tensor_tensor_scan(T.sa[:], T.mk[:], T.eb[:], 0.0, A.mult, A.max), ["mk", "eb"], ["sa"]),
             "eq": lambda: vs(T.eq[:, 0:8, :], T.pq[:, 0:8, :], 0.0, None, A.is_equal, None, ["pq"], [("eq", 0, 8)]),
-            "eq2": lambda: vt(T.eq[:, 8:16, :], T.pr[:, 0:128], T.rp[:], A.is_equal, ["pr", "rp"], [("eq", 8, 16)]),
+            "eq2": lambda: vt(T.eb[:], T.pr[:, 0:128], T.rp[:], A.is_equal, ["pr", "rp"], ["eb"]),
             "pn": lambda: sum_list("pa", (0, 1)), "pa": lambda: sum_list("pa", (2, 3)),
             "rn": lambda: vs(T.rn[:], T.sn[:, 16::17], 16383, None, A.bitwise_and, None, ["sn"], ["rn"]),
             "h7": lambda: vs(T.hi[:, 0:16], T.sn[:, 16::17], 16256, None, A.bitwise_and, None, ["sn"], [("hi", 0, 16)]),
@@ -550,47 +572,37 @@ def rank_program(g, core, T, topo):
                                scale=T.sb[:, t:t + 1]),
             "ys": lambda: copy(T.ys[:], T.diff[:, 0:4096].indirect(T.lo[:]), ["diff", "lo"], ["ys"]),
             "nf": new_counters,
-            "at": unless_last(lambda: copy(T.at[:], T.ac[:], ["ac", "th2"], ["at"], bias=T.th2[:, 0:1], scale=0.5)),
+            "at": lambda: copy(T.at[:], T.ac[:], ["ac", "th2"], ["at"], bias=T.th2[:, 0:1], scale=0.5),
             "rl": lambda: to_list("rl", "pa"), "pb": lambda: sum_list("pb", (0, 2, 3)), "cl": lambda: to_list("cl", "pb"),
             "q16": lambda: t and vs(T.q16[:], T.ac[:], 1.0 / 32, -0.46875, A.mult, A.add, ["ac"], ["q16"]),
             "mc": lambda: t and vs(T.mc[:], T.q16[:], -16.0, T.at[:, 0:1], A.mult, A.add, ["q16", "at"], ["mc"])}
 
     sums(0)
+    zeros(FILL[3], FILL[4])
     twice(0)
-    zeros(1024, 2048)
-    zeros(3072, 2048)
+    zeros(FILL[4], FILL[5])
     ch = chain(0)
     play(CHAIN0, ch, {"K": rest})
     last_constants()
     routes()
     late = []
     for t in range(5):
-        marks = gather(t, late, ch)
         if t == 4:
             for u, b, sem in ((1, "zh1", "h1"), (2, "zh2", "h2")):
                 arrival(S, sem, len(topo.engines(cores[(rank + u) % N], core)), [b])
                 dma(S, "y", lambda: g.sync.dma_start(T.zs[:, 256 * u:256 * u + 256], T[b][:]), [b], [])
-            dma(S, "y", lambda: g.sync.dma_start(T.zs[:, 768:1024], T.zi4[:]), ["zi4"], [])
-        rows, calls = answer(t, roots(), marks)
-        ch = chain(t + 1)
-        ch.update(twice=lambda: twice(t + 1), sums=lambda: sums(t + 1))
-        if t == 4:
-            ch = {name: lambda: None for name in ch}
-        play(ANSWER + " " + CHAIN, {**ch, **calls}, rows)
+            dma(S, "y", lambda: g.sync.dma_start(T.zs[:, 768:1024], T.zi[:, 4, :, :, :]), ["zi4"], [])
+        marks = gather(t, late, ch)
+        rows, calls = answer(t, marks)
+        if t < 4:
+            ch = chain(t + 1)
+            ch.update(twice=lambda: twice(t + 1), sums=lambda: sums(t + 1))
+        play(ANSWER + " " + CHAIN if t < 4 else ANSWER4, {**ch, **calls}, rows)
         late = rows["C"]
-    play("C*", {}, rows)
     dma(S, "s", lambda: C.dma_start(T.cs[:, 0:CUT], T.cw[0:128:16, C0:NW]), ["cw"], [])
     dma(S, "s", lambda: C.dma_start(T.cs[:, CUT:8192], T.cw[0:128:16, WASTE:C0]), ["cw"], [])
-    for b, n, first in (("px", 384, 0), ("pr", 128, 384)):
-        for q in range(16):
-            v0 = 16 * first + n * q
-            cut = min(max(CUT, v0), v0 + n)
-            for lo, hi in ((v0, cut), (cut, v0 + n)):
-                if lo < hi:
-                    col = WASTE + (lo + TURN) % 8192
-                    mm(T[b][:, lo - v0:hi - v0], lane_w("xa", q), T.win[:, col:col + hi - lo], q == 0, q == 15, ["xa", "win"], [b])
-        vc(T.xo[:, first:first + n], T[b][:, 0:n], [b], [("xo", first, first + n)])
-        dma(S, "y", lambda: g.sync.dma_start(T.xs[:, 16 * first:16 * (first + n)], T.xo[:, first:first + n]), [("xo", first, first + n)], [])
+    dma(S, "y", lambda: g.sync.dma_start(T.xs[:, 0:CUT], T.xw[0:128:16, C0:NW]), ["xw"], [])
+    dma(S, "y", lambda: g.sync.dma_start(T.xs[:, CUT:8192], T.xw[0:128:16, WASTE:C0]), ["xw"], [])
     for sem in SEMAPHORES:
         if S["count"].get(sem, 0):
             need(S, "g", (sem, S["count"][sem], {}))

from concourse.mybir import AluOpType, ActivationFunctionType

WASTE = 32
NW = WASTE + 8192
TURN = 919
C0, CUT = WASTE + TURN, 8192 - TURN
FILL = (256, 768, 1536, 3072, 5120, 5632)
ROT_V = 14
CHAIN = ("sums N cl turn N C* oi N oa N twice home pages pairs l4 l3 l2 l1 N l0 d10 d8 d4 low N wwa bit d0 N hha wwb fw N "
         "lia wb er")
CHAIN0 = ("turn K K oi K K oa K K pages l4 l3 l2 l1 l0 K K d10 d8 d4 low bit K K wwa d0 K K hha wwb K K lia wb K K K hhb K K K "
          "lib K*")
AFTER = {0: "mv hhb", 1: "lib hf nr xl", 3: "rt sends", 5: "al M", 7: "M", 13: "rv dr dl M M M M M"}
AFTER0 = {0: "hf", 1: "fw xl", 3: "er sends", 5: "mv al", 7: "nr", 9: "rt", 11: "M", 13: "rv dr dl M M M M M M"}
AFTER4 = {0: "mv hhb X X X X", 1: "lib hf rw nr xl X X X X", 3: "rt X X X X", 5: "al xo M X*", 7: "M"}
ANSWER = ("R q16 K K K R mc K K K R K* ms R sc sn z R h7 l7 rn signs M* parts nl odd1 nc once pn R odd2 ys R odd3 nf count eq2 R* eq "
          "any pa pb at xa rl")
ANSWER4 = ("xp q16 dr mc dl M M rx M M M ms sc sn z R h7 l7 rn M* parts nl odd1 nc pn nf R odd2 R odd3 ys R eq2 R eq any pb R cl nx pa "
           "C R R C rl C N C N C N C N C N C N N N")
LAST = [(0, 16)]
BIG = 16384.0
B2, F4, I4, U2 = "bfloat16", "float32", "int32", "uint16"
SCRATCH = {"win": ("sbuf", [128, NW], B2), "cw": ("sbuf", [128, NW], F4), "xw": ("sbuf", [128, NW], F4),
           "sh": ("sbuf", [128, 8, 8, 16], B2),
           "ro": ("sbuf", [128, 8, 128], B2),
           "diff": ("sbuf", [128, 4096], B2),
           "ad": ("sbuf", [128, 16, 16, 16], B2),
           "rot": ("sbuf", [128, 16, 128], B2),
           "ey2": ("sbuf", [128, 8, 32], B2), "zr": ("sbuf", [128, 16, 2, 16], B2),
           "eye": ("sbuf", [128, 8, 16], B2), "neye": ("sbuf", [128, 8, 16], B2), "lh": ("sbuf", [128, 2, 132], B2),
           "wd": ("sbuf", [128, 144], B2),
           "xa": ("sbuf", [128, 144], B2),
           "z1": ("sbuf", [128, 2, 256], B2), "eq": ("sbuf", [128, 8, 16], B2), "rp": ("sbuf", [128, 8, 16], F4), "er": ("sbuf", [128, 16, 16], B2),
           "ts": ("sbuf", [128, 4, 2, 4, 4], F4), "oi": ("sbuf", [128, 4, 2, 4], I4), "oa": ("sbuf", [128, 4, 2, 4], I4),
           "zi": ("sbuf", [128, 5, 4, 4, 16], B2), "zn": ("sbuf", [128, 5, 256], B2),
           "fa": ("sbuf", [128, 5, 4, 2, 4], F4), "fw": ("sbuf", [128, 4, 4, 2, 4], F4), "xo": ("sbuf", [128, 2, 256], F4)}
PSUM = {"pg": [128, 4, 8, 16], "pq": [128, 32, 16], "pa": [128, 512], "pb": [128, 512], "pr": [128, 512],
        "ph": [128, 512], "px": [128, 512], "pd": [128, 16, 32]}
for _n in PSUM:
    SCRATCH[_n] = ("psum", PSUM[_n], F4)
for _d, _l in ((B2, "ones:256 blk1:128 blk:128 xb:128 xr:256 xl:256 ey4:128 ck:128 dm:128 dm1:128 nbe:128 n128:256 thb:1 j15:16 hl:32 "
                    "pp:16 rw:256 zh1:256 zh2:256 z2:512 ys:256 nc:256 eb:128 mk:128 sa:128"),
               (F4, "p15:1 p31:1 lane:1 gp1:1 gp0:1 wf:2 wa:1 wp:2 th2:1 mc:1 lu:32 lt:32 e16:16 plc:256 hf:256 "
                    "hd:272 ms:272 e3:272 sc:272 ac:1 at:1 nr:16 mv:256 nf:256 k8:8 k16:8 tk:8 tl:8 t6:6 oh:6 bm:6 sb:5 "
                    "rx:256 nx:256 sm:1 sf:1 nb:1 m120:1"),
               (I4, "pidx:1 p15i:1 gpi:1 wti:2 thi:1 lfi:16 raw:80 r12:80 ss:256 bi:80 ww:256 hh:256 q16:1 sn:272 rn:16 hi:32 jm:128 jn:128"),
               (U2, "li:256 lo:16 nl:16 rl:16 cl:16 rt:16")):
    for _x in _l.split():
        SCRATCH[_x.split(":")[0]] = ("sbuf", [128, int(_x.split(":")[1])], _d)
SEMAPHORES = ["qv", "qt", "qs", "qg", "ls", "wp", "h1", "h2"] + ["za%d" % t for t in range(1, 5)] + \
    ["fa%d" % t for t in range(1, 5)] + ["d%d" % k for k in range(22)]


def state(g, T):
    return {"g": g, "T": T, "q": {"v": g.vector, "t": g.tensor, "s": g.scalar, "g": g, "y": g.sync},
            "known": {k: {} for k in "vtsgy"}, "count": {}, "w": {}, "r": {}, "bank": {}, "nd": 0}


def norm(x):
    return (x, 0, 1 << 30) if isinstance(x, str) else x


def need(S, q, ev):
    kn = S["known"][q]
    sem, val, clock = ev
    if kn.get(sem, 0) >= val:
        return
    S["q"][q].wait_ge(S["T"].sem[sem], val)
    for k in clock:
        kn[k] = max(kn.get(k, 0), clock[k])
    kn[sem] = max(kn.get(sem, 0), val)


def deps(S, q, reads, writes):
    todo = []
    for x, old in [(x, S["w"]) for x in reads] + [(x, S["w"]) for x in writes] + [(x, S["r"]) for x in writes]:
        n, lo, hi = norm(x)
        for (a, b, ev) in old.get(n, []):
            if lo < b and a < hi and not (q == "t" and ev[0] == "qt"):
                todo.append(ev)
    for ev in sorted(todo, key=lambda e: -e[1]):
        need(S, q, ev)


def note(S, reads, writes, ev):
    for x in reads:
        n, lo, hi = norm(x)
        l = S["r"].setdefault(n, [])
        l[:] = [e for e in l if not (e[2][0] == ev[0] and lo <= e[0] and e[1] <= hi)] + [(lo, hi, ev)]
    for x in writes:
        n, lo, hi = norm(x)
        for key in ("w", "r"):
            l = S[key].setdefault(n, [])
            l[:] = [e for e in l if not (lo <= e[0] and e[1] <= hi)]
        S["w"][n].append((lo, hi, ev))


def op(S, q, fn, reads, writes):
    banks = [x for x in reads + writes if x in PSUM]
    for x in banks:
        for other, ev in S["bank"].setdefault(x, {}).items():
            if other != q:
                need(S, q, ev)
    deps(S, q, reads, writes)
    sem = "q" + q
    S["count"][sem] = S["count"].get(sem, 0) + 1
    fn().then_inc(S["T"].sem[sem], 1)
    clock = dict(S["known"][q])
    clock[sem] = S["count"][sem]
    note(S, reads, writes, (sem, S["count"][sem], clock))
    for x in banks:
        S["bank"][x][q] = (sem, S["count"][sem], clock)


def dma(S, q, fn, reads, writes):
    deps(S, q, reads, writes)
    sem = "d%d" % S["nd"]
    S["nd"] += 1
    fn().then_inc(S["T"].sem[sem], 16)
    clock = dict(S["known"][q])
    clock[sem] = S["count"][sem] = 16
    note(S, reads, writes, (sem, 16, clock))


def arrival(S, sem, val, writes):
    S["count"][sem] = val
    note(S, [], writes, (sem, val, {}))


def play(order, calls, rows):
    for name in order.split():
        if name[0] in rows:
            row = rows[name[0]]
            for _ in range(len(row) if name[1:] == "*" else min(1, len(row))):
                row.pop(0)()
        else:
            calls[name]()


def rank_program(g, core, T, topo):
    rank = T.rank_of(core)
    if rank is None:
        return
    A, F = AluOpType, ActivationFunctionType
    S = state(g, T)
    V, P, C = g.vector, g.tensor, g.scalar
    cores = list(T.cores)
    N = len(cores)
    nxt, prv = cores[(rank + 1) % N], cores[(rank - 1) % N]
    E = len(topo.engines(prv, core))

    def v(fn, reads, writes):
        op(S, "v", fn, reads, writes)

    def s(fn, reads, writes):
        op(S, "s", fn, reads, writes)

    def vs(o, i, a, b, p, q, reads, writes):
        if q is None:
            v(lambda: V.tensor_scalar(o, i, a, b, p), reads, writes)
        else:
            v(lambda: V.tensor_scalar(o, i, a, b, p, q), reads, writes)

    def vt(o, x, y, p, reads, writes):
        v(lambda: V.tensor_tensor(o, x, y, p), reads, writes)

    def vc(o, i, reads, writes):
        v(lambda: V.tensor_copy(o, i), reads, writes)

    def fill(ap, x, name):
        v(lambda: V.memset(ap, x), [], [name])

    def copy(o, i, reads, writes, bias=0.0, scale=1.0):
        f = F.Copy if isinstance(bias, float) else F.Identity
        s(lambda: C.activation(o, i, f, bias=bias, scale=scale), reads, writes)

    def mm(out, lhsT, rhs, start, stop, reads, writes):
        op(S, "t", lambda: P.matmul(out, lhsT, rhs, start=start, stop=stop), reads, writes)

    def iota(name, pattern, base, cm=0):
        if SCRATCH[name][2] == I4:
            op(S, "g", lambda: g.iota(T[name][:], pattern, base, cm), [], [name])
        else:
            op(S, "g", lambda: g.iota(T[name][:], pattern, base, cm, allow_small_or_imprecise_dtypes=True), [], [name])

    def select(o, i, pattern, cmp, x, base, cm, reads, writes):
        op(S, "g", lambda: g.affine_select(o, i, pattern, cmp, x, base, cm), reads, writes)

    def send(dst, out, src, sem, reads):
        deps(S, "g", reads, [])
        rid, pid, _ = topo.addr(dst)
        g.remote_dma(out, src, T.sem[sem], T.sem.ls, pid, rid, topo.mask(core, dst))
        S["count"]["ls"] = S["count"].get("ls", 0) + len(topo.engines(core, dst))

    def slot(buf, a):
        if a in (0, 15):
            return buf[:, 16 * a:16 * a + 16]
        first = 16 + 32 * ((a - 1) // 2)
        return buf[:, first + (a - 1) % 2:first + 32:2]

    def lane_w(name, i):
        return T[name][:, 15 - i:143 - i]

    def sum_weights(first, w, key, on):
        for h in range(2):
            o, i, at = T.lh[:, h, first:131:32], T.blk[:, 16 * h::32], ("lh", 2 * (first // 16) + h, 2 * (first // 16) + h + 1)
            if on == "s":
                copy(o, i, ["blk", key], [at], scale=w)
            else:
                vs(o, i, w, None, A.mult, None, ["blk", key], [at])

    dma(S, "y", lambda: g.sync.dma_start(T.wti[:], T.wt[:]), [], ["wti"])
    dma(S, "s", lambda: C.dma_start(T.lfi[:], T.leaf[:]), [], ["lfi"])
    dma(S, "y", lambda: g.sync.dma_start(T.zi[:, 0, :, :, :], T.z0[:]), [], ["zi0"])
    dma(S, "s", lambda: C.dma_start(T.z1[:, 0, :], T.z0[:]), [], [("z1", 0, 1)])
    dma(S, "y", lambda: g.sync.dma_start(T.win[:, C0:NW], T.x0[:, 0:CUT]), [], [("win", C0, NW)])
    dma(S, "y", lambda: g.sync.dma_start(T.win[:, WASTE:C0], T.x0[:, CUT:8192]), [], [("win", WASTE, C0)])
    iota("pidx", [[0, 1]], 0, 1)
    for n, x in [("ones", 1.0), ("m120", -120.0), ("thi", 0), ("ck", 0.0), ("wd", 0.0), ("lh", 0.0)]:
        fill(T[n][:], x, n)
    fill(T.fa[:, 0, :, :, :], 64.0, "fa0")
    dma(S, "s", lambda: C.dma_start(T.thi[0:128:16, :], T.th[:]), [], ["thi"])

    def zeros(a, b, src="cw"):
        s(lambda: C.activation(T.cw[:, a:b], T[src][:, 0:b - a], F.Sigmoid, bias=T.m120[:, 0:1], scale=0.0),
          [(src, 0, b - a), "m120"], [("cw", a, b)])

    zeros(0, FILL[0], "ones")
    select(T.blk1[:], T.ones[:, 0:128], [[-16, 8], [0, 16]], A.is_ge, 0.0, 0, 1, ["ones"], ["blk1"])
    select(T.blk[:], T.blk1[:], [[16, 8], [0, 16]], A.is_ge, 0.0, 15, -1, ["blk1"], ["blk"])
    select(T.eye[:], T.ones[:, 0:128], [[-1, 128]], A.is_equal, 0.0, 0, 1, ["ones"], ["eye"])
    vs(T.gpi[:], T.pidx[:], 4, 1, A.arith_shift_right, A.bitwise_and, ["pidx"], ["gpi"])
    vs(T.p15i[:], T.pidx[:], 15, None, A.bitwise_and, None, ["pidx"], ["p15i"])
    for row, x in ((0, 37.0), (32, 0.125), (64, 2.0 ** -17)):
        fill(T.ck[row:row + 1, :], x, ("ck", row, row + 1))
    for n, pattern, base, cm in [("jm", [[1, 128]], 128, -1), ("k8", [[1, 8]], 1, 0), ("k16", [[-1, 8]], 15, 0), ("t6", [[1, 6]], 0, 0),
                                 ("e16", [[-1, 16]], 15, 0)]:
        iota(n, pattern, base, cm)

    vc(T.gp1[:], T.gpi[:], ["gpi"], ["gp1"])
    vs(T.gp0[:], T.gpi[:], -1.0, 1.0, A.mult, A.add, ["gpi"], ["gp0"])
    fill(T.cw[:, FILL[0]:FILL[1]], 0.0, ("cw", FILL[0], FILL[1]))
    zeros(FILL[1], FILL[2])
    zeros(FILL[2], FILL[3])
    vc(T.wd[:, 15:143:16], T.blk[:, 0::16], ["blk"], ["wd"])
    vs(T.wa[:], T.wti[:, 0:1], 128.0, None, A.mult, None, ["wti"], ["wa"])
    vs(T.lu[:, 0:16], T.lfi[:], T.gp0[:, 0:1], None, A.mult, None, ["lfi", "gp0"], [("lu", 0, 16)])
    vs(T.lu[:, 16:32], T.lfi[:], T.gp1[:, 0:1], None, A.mult, None, ["lfi", "gp1"], [("lu", 16, 32)])
    vc(T.wf[:], T.wti[:], ["wti"], ["wf"])
    sum_weights(3, T.wa[:, 0:1], "wa", "v")
    v(lambda: V.transpose(T.lt[:], T.lu[:]), ["lu"], ["lt"])
    for h in range(2):
        vc(T.zr[:, :, h, :], T.zi[:, 0, :, :, :], ["zi0"], [("zr", h, h + 1)])
    vt(T.fa[:, 0, :, 1, :], T.lt[:, 0:16], T.lt[:, 16:32], A.add, ["lt"], ["fa0"])
    for a, b, step, base, by in ((17, 240, 2, 239, -2), (48, 240, 2, 238, -2), (16, 48, 2, 255, -1), (240, 256, 1, 46, -2)):
        op(S, "g", lambda: g.iota(T.plc[:, a:b:step], [[by, len(range(a, b, step))]], base, 0, allow_small_or_imprecise_dtypes=True),
           [], [("plc", a, a + 1)])
    op(S, "g", lambda: g.iota(T.cw[:, FILL[5]:NW], [[0, NW - FILL[5]]], 0, 0, allow_small_or_imprecise_dtypes=True), [],
       [("cw", FILL[5], NW)])

    def rotations():
        for h, b in enumerate(("pa", "pb")):
            for k in range(4):
                mm(T[b][:, 128 * k:128 * k + 128], T.eye[:], T.eye[:], True, False, ["eye"], [b])
                mm(T[b][:, 128 * k:128 * k + 128], T.neye[:], T.ey2[:, :, 4 * h + k + 1:4 * h + k + 17], False, True, ["neye", "ey2"], [b])
            copy(T.sh[:, 4 * h:4 * h + 4, :, :], T[b][:], [b], [("sh", 8 * h + 2, 8 * h + 10)])

    rest = [lambda: vs(T.ey4[:], T.eye[:], 0.25, None, A.mult, None, ["eye"], ["ey4"]),
            lambda: vc(T.p15[:], T.p15i[:], ["p15i"], ["p15"]),
            lambda: vs(T.neye[:], T.eye[:], -1.0, None, A.mult, None, ["eye"], ["neye"]),
            lambda: vc(T.ey2[:, :, 0:16], T.eye[:], ["eye"], [("ey2", 0, 1)]),
            lambda: vc(T.ey2[:, :, 16:32], T.eye[:], ["eye"], [("ey2", 1, 2)]),
            lambda: fill(T.ss[:, 0:16], 2453, ("ss", 0, 16)),
            lambda: vs(T.jn[:], T.jm[:], 15, None, A.bitwise_and, None, ["jm"], ["jn"]),
            lambda: vs(T.tk[:], T.k16[:], T.p15[:, 0:1], None, A.is_gt, None, ["k16", "p15"], ["tk"]),
            lambda: vs(T.dm[:], T.jn[:], 1.0, None, A.add, None, ["jn"], ["dm"]),
            lambda: vt(T.tl[:], T.tk[:], T.k8[:], A.mult, ["tk", "k8"], ["tl"]),
            lambda: vs(T.oh[:], T.t6[:], T.p15[:, 0:1], None, A.is_equal, None, ["t6", "p15"], ["oh"]),
            lambda: vt(T.dm1[:], T.dm[:], T.blk[:], A.mult, ["dm", "blk"], ["dm1"]),
            lambda: vs(T.tk[:], T.tl[:], 1.0, None, A.add, None, ["tl"], ["tk"]),
            lambda: vs(T.bm[:], T.oh[:], 240.0, -120.0, A.mult, A.add, ["oh"], ["bm"]),
            lambda: vs(T.sm[:], T.oh[:, 0:1], 240.0, None, A.mult, None, ["oh"], ["sm"]),
            lambda: fill(T.win[:, 0:WASTE], 0.0, ("win", 0, WASTE)),
            lambda: vs(T.p31[:], T.p15[:], 16.0, None, A.add, None, ["p15"], ["p31"]),
            lambda: vs(T.nbe[:], T.eye[:], -BIG, None, A.mult, None, ["eye"], ["nbe"]),
            lambda: fill(T.hd[:, 0::17], 0.0, ("hd", 0, 1)),
            lambda: fill(T.pd[:, :, 0], 0.0, "pd"),
            lambda: fill(T.n128[:, 0:32], -128.0, "n128"),
            lambda: fill(T.pd[:, :, 16], 1000.0, "pd")]

    def last_constants():
        dma(S, "g", lambda: g.dma_start(T.cw[0:128:16, WASTE:C0], T.c0[:, CUT:8192]), [], [("cw", WASTE, C0)])
        dma(S, "g", lambda: g.dma_start(T.cw[0:128:16, C0:NW], T.c0[:, 0:CUT]), [], [("cw", C0, NW)])
        send(nxt, T.wp[:], T.wf[:], "wp", ["wf"])
        arrival(S, "wp", E, ["wp"])
        for a, base, by in [(None, -16, 0), (0, -256, -16), (14, -496, 16), (15, 0, 0)] + [(a, -496, 0) for a in range(2, 14, 2)]:
            ap, n = (T.e3[:], 272) if a is None else (T.e3[:, a::17], 16)
            op(S, "g", lambda: g.iota(ap, [[by, n]], base, 0, allow_small_or_imprecise_dtypes=True), [],
               ["e3" if a is None else ("e3", a, a + 1)])
        rotations()
        vs(T.ph[:, 272:512], T.plc[:, 16:256], BIG, float(WASTE), A.mult, A.add, ["plc"], ["ph"])

    def routes():
        for k in range(16):
            (vc if k < ROT_V else copy)(T.rot[:, k, :], T.ey2[:, :, k:k + 16], ["ey2"], [("rot", k, k + 1)])
        for k in range(8):
            vs(T.ro[:, k, :], T.dm1[:], T.tk[:, k:k + 1], -BIG, A.is_equal, A.mult, ["dm1", "tk"], [("ro", k, k + 1)])
        fill(T.fw[:], 64.0, "fw")

    def thresholds():
        vc(T.thb[:], T.thi[:], ["thi"], ["thb"])
        mm(T.px[:, 0:1], T.blk[:], T.thb[:], True, True, ["blk", "thb"], ["px"])

    first_answer = [lambda: vs(T.hd[:, 16::17], T.e16[:], BIG, T.p15[:, 0:1], A.mult, A.add, ["e16", "p15"], [("hd", 16, 17)]),
                    lambda: vs(T.lane[:], T.p15[:], 4080.0, None, A.add, None, ["p15"], ["lane"]),
                    lambda: vc(T.mc[:], T.px[:, 0:1], ["px"], ["mc"]),
                    lambda: fill(T.mk[:], 1.0, "mk"),
                    lambda: vs(T.e3[:, 16::17], T.e16[:], -16.0, T.lane[:, 0:1], A.mult, A.add, ["e16", "lane"], [("e3", 16, 17)]),
                    lambda: vc(T.th2[:], T.px[:, 0:1], ["px"], ["th2"]),
                    lambda: fill(T.mk[:, 0::16], 0.0, "mk"),
                    lambda: vs(T.sb[:], T.oh[:, 1:6], T.oh[:, 0:1], -BIG, A.subtract, A.mult, ["oh"], ["sb"]),
                    lambda: vs(T.nb[:], T.oh[:, 0:1], -BIG, None, A.mult, None, ["oh"], ["nb"]),
                    lambda: vs(T.sf[:], T.oh[:, 0:1], -240.0, None, A.mult, None, ["oh"], ["sf"])]

    def sums(t):
        for q in range(8):
            mm(T.pg[:, :, q // 4, :], T.lh[:, q // 4, 3 - q % 4:131 - q % 4], T.zi[:, t, :, q % 4, :], q % 4 == 0, q % 4 == 3,
               ["lh", "zi%d" % t], ["pg"])

    def chain(t):
        def down(a, w, n):
            return lambda: vs(T.ss[:, a:a + w], T.raw[:, 0:w], 0.5 ** n, 2451.5 + 0.5 ** (n + 1), A.mult, A.add, [("raw", 1, 5)],
                              [("ss", a, a + w)])

        def level(k, o):
            c = 2.0 ** (15 - k) - (0.5 - 0.5 ** (k + 1))
            return lambda: vs(o, T.oa[:, :, 1, :], 0.5 ** k, c, A.mult, A.add, ["oa"], [("raw", k, k + 1)])

        def wide(a, b, part):
            return {"ww" + part: lambda: vt(T.ww[:, a:b], T.ss[:, a:b], T.ph[:, a:b], A.mult, [("ss", a, b), "ph"], [("ww", a, b)]),
                    "hh" + part: lambda: vs(T.hh[:, a:b], T.ww[:, a:b], 8191, None, A.bitwise_and, None, [("ww", a, b)], [("hh", a, b)]),
                    "li" + part: lambda: vs(T.li[:, a:b], T.hh[:, a:b], float(WASTE), None, A.add, None, [("hh", a, b)], [("li", a, b)])}

        def named_cells():
            vt(T.hf[:, 16:256], T.hh[:, 16:256], T.ph[:, 272:512], A.add, ["hh", "ph"], ["hf"])
            for m in range(1, 16):
                select(T.hd[:, m::17], slot(T.hf, m), [[0, 16]], A.is_gt, 0.0, 1, 0, ["hf"], [("hd", m, m + 1)])

        def pages():
            mm(T.ph[:, 0:256], T.ck[:], T.ones[:], True, False, ["ck", "ones"], ["ph"])
            vs(T.pp[:], T.oa[:, :, 0, :], 1.0 / 128, -0.5, A.mult, A.add, ["oa"], ["pp"])
            for a in range(16):
                mm(slot(T.ph, a), T.ey4[:], T.pp[:], False, a == 15, ["ey4", "pp"], ["ph"])

        def forward():
            if t < 4:
                vs(T.fw[:, t, :, 1, :], T.oa[:, :, 1, :], 8.0, None, A.mult, None, ["oa"], [("fw", t, t + 1)])

        def sends():
            if t < 4:
                send(nxt, T.fa[:, t + 1, :, :, :], T.fw[:, t, :, :, :], "fa%d" % (t + 1), [("fw", t, t + 1)])
                arrival(S, "fa%d" % (t + 1), E, ["fa%d" % (t + 1)])

        def home():
            if t in (2, 3):
                send(cores[(rank - t + 1) % N], T["zh%d" % (t - 1)][:], T.zn[:, t - 1, :], "h%d" % (t - 1), ["zn%d" % (t - 1)])

        def leaf():
            copy(T.xl[:], T.win[:, 0:NW].indirect(T.li[:, 240:256]), ["win", ("li", 240, 256)], ["xl"])
            mm(T.px[:, 256:512], T.neye[:], T.z1[:, t % 2, :], True, False, ["neye", ("z1", t % 2, t % 2 + 1)], ["px"])
            mm(T.px[:, 256:512], T.eye[:], T.xl[:], False, True, ["eye", "xl"], ["px"])

        def root_pairs():
            for k in range(8):
                mm(T.pq[:, 8 + k, :], T.sh[:, k, :, :], T.pp[:], True, True, ["sh", "pp"], ["pq"])
            for k in range(16):
                out = T.pq[:, 16 + k // 2, 8 * (k % 2):8 * (k % 2) + 8]
                mm(out, T.rot[:, k, :], T.pp[:, 0::2], True, False, ["rot", "pp"], ["pq"])
                mm(out, T.neye[:], T.pp[:, 1::2], False, True, ["neye", "pp"], ["pq"])

        def equal_roots():
            vs(T.er[:], T.pq[:, 8:24, :], 0.0, None, A.is_equal, None, ["pq"], ["er"])
            for k in range(8):
                mm(T.pa[:, 0:16], T.ro[:, k, :], T.er[:, k, :], k == 0, False, ["ro", "er"], ["pa"])
            for k in range(16):
                mm(T.pa[:, 1:16:2], T.nbe[:], T.er[:, 8 + k // 2, 8 * (k % 2):8 * (k % 2) + 8], False, k == 15, ["nbe", "er"], ["pa"])

        def root_list():
            for h, w in enumerate(("p15", "p31")):
                vs(T.rt[:, h::2], T.nr[:, h::2], float(WASTE), T[w][:, 0:1], A.add, A.max, ["nr", w], [("rt", h, h + 1)])

        def root_sums():
            mm(T.pb[:, 0:256], T.xb[:], T.n128[:], True, False, ["xb", "n128"], ["pb"])
            mm(T.pb[:, 0:256], T.xb[:], T.rw[:], False, True, ["xb", "rw"], ["pb"])
            copy(T.rx[:], T.pb[:, 0:256], ["pb"], ["rx"])

        def all_sums(h):
            a, b = WASTE + 4096 * h, ("pg", "pb")[h]
            (copy, vc)[h](T.xo[:, h, :], (T.pg[:, 0:2, :, :], T.pb[:, 256:512])[h], [b], [("xo", h, h + 1)])
            dma(S, "y", lambda: g.sync.dma_start(T.xw[0:128:16, a:a + 4096], T.xo[:, h, :]), [("xo", h, h + 1)], [("xw", a, a + 4096)])

        return {**wide(0, 176, "a"), **wide(176, 256, "b"), "hf": named_cells, "rt": root_list, "rx": root_sums,
                "xo": lambda: all_sums(0), "xp": lambda: all_sums(1),
                "dr": lambda: vc(T.diff[:, 0:256], T.pr[:, 256:512], ["pr"], [("diff", 0, 1)]), "xl": leaf,
                "al": lambda: s(lambda: C.activation(T.ad[:, :, 15, :], T.px[:, 256:512], F.Abs), ["px"], [("ad", 15, 16)]),
                "dl": lambda: vc(T.diff[:, 3840:4096], T.px[:, 256:512], ["px"], [("diff", 15, 16)]),
                "rw": lambda: copy(T.rw[:], T.pr[:, 0:256], ["pr"], ["rw"], bias=127.8, scale=0.5),
                "rv": lambda: vs(T.rw[:], T.pr[:, 0:256], 0.5, 127.8, A.mult, A.add, ["pr"], ["rw"]),
                "lv": lambda: vt(T.diff[:, 3840:4096], T.win[:, 0:NW].indirect(T.li[:, 240:256]), T.z1[:, t % 2, :], A.subtract,
                                 ["win", ("li", 240, 256), ("z1", t % 2, t % 2 + 1)], [("diff", 15, 16)]),
                "av": lambda: s(lambda: C.activation(T.ad[:, :, 15, :], T.diff[:, 3840:4096], F.Abs), [("diff", 15, 16)], [("ad", 15, 16)]),
                "turn": lambda: v(lambda: V.transpose(T.ts[:], T.pg[:, :, 0:2, :]), ["pg"], ["ts"]),
                "oi": lambda: vt(T.oi[:], T.ts[:, :, :, 0, :], T.fa[:, t, :, :, :], A.add, ["ts", "fa%d" % t], ["oi"]),
                "oa": lambda: vs(T.oa[:], T.oi[:], 32767, None, A.bitwise_and, None, ["oi"], ["oa"]),
                "pages": pages, "pairs": root_pairs, "er": equal_roots, "fw": forward, "sends": sends, "home": home,
                "l0": level(0, T.raw[:, 64:80]), "l1": level(1, T.raw[:, 33:64:2]), "l2": level(2, T.raw[:, 32:64:2]),
                "l3": level(3, T.raw[:, 1:32:2]), "l4": level(4, T.raw[:, 0:32:2]),
                "d4": down(112, 64, 4), "d8": down(48, 64, 8), "d10": down(16, 32, 10),
                "low": lambda: vs(T.r12[:], T.raw[:], 4095, None, A.bitwise_and, None, ["raw"], ["r12"]),
                "d0": lambda: vs(T.ss[:, 176:256], T.r12[:], 2452.0, None, A.add, None, ["r12"], [("ss", 176, 256)]),
                "bit": lambda: vs(T.bi[:], T.raw[:], 4096, None, A.bitwise_and, None, ["raw"], ["bi"]),
                "wb": lambda: vt(T.ww[:, 176:256], T.ww[:, 176:256], T.bi[:], A.add, [("ww", 176, 256), "bi"], [("ww", 176, 256)]),
                "nr": lambda: vt(T.nr[:], T.hh[:, 0:16], T.pa[:, 0:16], A.add, [("hh", 0, 16), "pa"], ["nr"])}

    def twice(t):
        zi, z = "zi%d" % t, T.zi[:, t, :, :, :]
        for h in range(2 if t else 0):
            select(T.zr[:, :, h, :], z, [[0, 256]], A.is_gt, 0.0, 1, 0, [zi], [("zr", h, h + 1)])
        if t == 0:
            copy(T.z2[:], T.zr[:], ["zr"], ["z2"])
        else:
            select(T.z2[:], T.zr[:], [[0, 512]], A.is_gt, 0.0, 1, 0, ["zr"], ["z2"])
            select(T.z1[:, t % 2, :], z, [[0, 256]], A.is_gt, 0.0, 1, 0, [zi], [("z1", t % 2, t % 2 + 1)])

    def sigmoids(vals, lst, n):
        return [lambda c=c: s(lambda: C.activation(T.cw[:, 0:NW].indirect(T[lst][:, 2 * c:2 * c + n]),
                                                   T[vals][:, 16 * n * c:16 * n * (c + 1)], F.Sigmoid), [lst, vals], ["cw"])
                for c in range(16 // n)]

    def gather(t, late, ch):
        marks = sigmoids("mv", "rt", 2)

        def two(n):
            for q in (n, n + 1):
                mm((T.pg[:, 0:2, :, :], T.pb[:, 256:512])[q // 16], lane_w("xa", q % 16), T.win[:, WASTE + 256 * q:WASTE + 256 * q + 256],
                   q % 16 == 0, q % 16 == 15, ["xa", "win"], [("pg", "pb")[q // 16]])

        rows = {"M": marks, "C": late, "X": [lambda n=n: two(n) for n in range(0, 32 if t == 4 else 0, 2)]}
        after = {0: AFTER0, 4: AFTER4}.get(t, AFTER)

        def root_counters():
            copy(T.mv[:], T.cw[:, 0:NW].indirect(T.li[:, 0:16]), ["cw", ("li", 0, 16), "sm", "bm"], ["mv"], bias=T.bm[:, t + 1:t + 2],
                 scale=T.sm[:, 0:1])

        ch = {**ch, "mv": root_counters}
        one = ("z1", t % 2, t % 2 + 1)
        if t == 0:
            ch["pairs"]()
        copy(T.xr[:], T.win[:, 0:NW].indirect(T.li[:, 0:16]), ["win", ("li", 0, 16)], ["xr"])
        for h, w in enumerate(("eye", "neye")):
            mm(T.pr[:, 256 * h:256 * h + 256], T[w][:], T.z1[:, t % 2, :], True, False, [w, one], ["pr"])
            mm(T.pr[:, 256 * h:256 * h + 256], T.eye[:], T.xr[:], False, True, ["eye", "xr"], ["pr"])
        play(after.get(0, ""), ch, rows)
        for a in range(1, 15, 2):
            b = a + 2
            for c0, c1 in LAST if a == 13 else [(0, 16)]:
                first = 16 * a + 2 * c0
                d, key = T.diff[:, 16 * first:16 * first + 32 * (c1 - c0)], (a + c0 / 8, a + c1 / 8)
                vt(d, T.win[:, 0:NW].indirect(T.li[:, first:first + 2 * (c1 - c0)]), T.z2[:, 32 * c0:32 * c1], A.subtract,
                   ["win", ("li", 16 * a, 16 * b), "z2"], [("diff",) + key])
                s(lambda: C.activation(T.ad[:, c0:c1, a:b, :], d, F.Abs), [("diff",) + key], [("ad",) + key])
            if b in (5, 9, 13, 15):
                a0, b0 = (b - 4, b) if b < 15 else (13, 16)
                for i in range(16):
                    mm(T.pd[:, :, a0:b0], lane_w("wd", i), T.ad[:, :, a0:b0, i], i == 0, i == 15, ["wd", ("ad", a0, b0)], ["pd"])
            if t == 0 and a == 5:
                thresholds()
            play(after.get(a, ""), ch, rows)
        return marks

    def scatters(t, lst, x, y, sums_):
        if t == 4:
            return [lambda c=c: vc(T.xw[:, 0:NW].indirect(T[lst][:, 2 * c:2 * c + 2]), T[sums_][:, 32 * c:32 * c + 32], [lst, sums_], ["xw"])
                    for c in range(7, -1, -1)]
        return [lambda c=c: vt(T.win[:, 0:NW].indirect(T[lst][:, 2 * c:2 * c + 2]), T[x][:, 32 * c:32 * c + 32],
                               T.n128[:, 0:32] if y == "n128" else T.z1[:, t % 2, 32 * c:32 * c + 32], A.add, [lst, x, y], ["win"])
                for c in range(7, -1, -1)]

    def answer(t, marks):
        zn, one = "zn%d" % t, ("z1", t % 2, t % 2 + 1)

        def new_z():
            vc(T.lo[:], T.sc[:, 16::17], ["sc"], ["lo"])
            s(lambda: C.activation(T.zn[:, t, :], T.diff[:, 0:4096].indirect(T.lo[:]), F.Abs), ["diff", "lo"], [zn])
            if t < 4:
                send(nxt, T.zi[:, t + 1, :, :, :], T.zn[:, t, :], "za%d" % (t + 1), [zn])
                arrival(S, "za%d" % (t + 1), E, ["zi%d" % (t + 1)])
            if t in (0, 4):
                dma(S, "y", lambda: g.sync.dma_start(T.zs[:, 256 * t:256 * t + 256], T.zn[:, t, :]), [zn], [])

        def signs():
            vs(T.j15[:], T.sn[:, 16::17], 240 * BIG, 2.0, A.is_ge, A.mult, ["sn"], ["j15"])
            mm(T.px[:, 0:16], T.ones[:, 0:128], T.j15[:], True, True, ["ones", "j15"], ["px"])

        def count():
            s(lambda: C.activation(T.j15[:], T.px[:, 0:16], F.Copy, accum_out=T.ac[:]), ["px"], ["j15", "ac"])

        def low_part():
            vc(T.hl[:], T.hi[:], ["hi"], ["hl"])
            for k in range(16):
                for h in range(2):
                    mm(T.pr[:, k:128:16], T.rot[:, k, :], T.hl[:, 16 * h:16 * h + 16:2], h == 0, h == 1, ["rot", "hl"], ["pr"])
            for k in range(8):
                for h in range(2):
                    mm(T.pq[:, k, :], T.sh[:, k, :, :], T.hl[:, 16 * h:16 * h + 16], h == 0, h == 1, ["sh", "hl"], ["pq"])

        def odd(n):
            for k in range(0 if n else 4):
                vc(T.rp[:, :, k], T.rn[:, 1::2], ["rn"], [("rp", k, k + 1)])
            if n:
                vc(T.rp[:, :, n:2 * n], T.rp[:, :, 0:n], [("rp", 0, n)], [("rp", n, 2 * n)])

        def sum_list(b, parts):
            for h in range(2 if 0 in parts else 0):
                mm(T[b][:, 0:16], T.eye[:], T.hl[:, 16 * h:16 * h + 16], h == 0, False, ["eye", "hl"], [b])
            for i in range(16 if 1 in parts else 0):
                mm(T[b][:, 0:16], lane_w("wd", i), T.nc[:, i::16], False, False, ["wd", "nc"], [b])
            if 3 in parts:
                mm(T[b][:, 1:16:2], T.nbe[:], T.sa[:, 15::16], False, False, ["nbe", "sa"], [b])
            for k in range(8 if 2 in parts else 0):
                mm(T[b][:, 0:16], T.ro[:, k, :], T.eq[:, k, :], False, k == 7, ["ro", ("eq", 0, 8)], [b])

        def to_list(name, b):
            for h, w in enumerate(("p15", "p31")):
                vs(T[name][:, h::2], T[b][:, h:16:2], T[w][:, 0:1], None, A.max, None, [b, w], [(name, h, h + 1)])

        def new_counters():
            copy(T.nf[:], T.cw[:, 0:NW].indirect(T.nl[:]), ["cw", "nl", "sf", "bm"], ["nf"], bias=T.bm[:, 0:1], scale=T.sf[:, 0:1])

        def once():
            if t == 0:
                sum_weights(19, T.wp[:, 1:2], "wp", "s")

        def weights():
            if t == 1:
                copy(T.xa[:], T.wd[:], ["wd", "wf"], ["xa"], scale=T.wf[:, 0:1])
            if t == 2:
                copy(T.xb[:], T.blk[:], ["blk", "wf"], ["xb"], scale=T.wf[:, 0:1])
                copy(T.n128[:, 32:256], T.ones[:, 32:256], ["ones"], [("n128", 32, 256)], scale=-128.0)

        def named_sums():
            mm(T.px[:, 0:256], T.xb[:], T.z1[:, t % 2, :], True, False, ["xb", one], ["px"])
            mm(T.px[:, 0:256], T.xb[:], T.ys[:], False, True, ["xb", "ys"], ["px"])
            copy(T.nx[:], T.px[:, 0:256], ["px"], ["nx"])

        return {"R": scatters(t, "rt", "rw", "n128", "rx"), "M": marks, "N": scatters(t, "rl", "ys", one, "nx"), "K": first_answer,
                "C": sigmoids("nf", "cl", 2)}, {
            "ms": lambda: vs(T.ms[:], T.pd[:, :, 0:17], T.mc[:, 0:1], None, A.is_gt, None, ["pd", "mc"], ["ms"]),
            "sn": lambda: v(lambda: V.tensor_tensor_scan(T.sn[:], T.hd[:], T.ms[:], 0.0, A.max, A.mult), ["hd", "ms"], ["sn"]),
            "sc": lambda: v(lambda: V.tensor_tensor_scan(T.sc[:], T.ms[:], T.e3[:], 0.0, A.mult, A.add), ["ms", "e3"], ["sc"]),
            "signs": signs, "z": new_z, "count": count, "parts": low_part, "once": once, "xa": weights, "nx": named_sums,
            "odd1": lambda: odd(0), "odd2": lambda: odd(4), "odd3": lambda: odd(8),
            "any": lambda: v(lambda: V.tensor_tensor_scan(T.sa[:], T.mk[:], T.eb[:], 0.0, A.mult, A.max), ["mk", "eb"], ["sa"]),
            "eq": lambda: vs(T.eq[:, 0:8, :], T.pq[:, 0:8, :], 0.0, None, A.is_equal, None, ["pq"], [("eq", 0, 8)]),
            "eq2": lambda: vt(T.eb[:], T.pr[:, 0:128], T.rp[:], A.is_equal, ["pr", "rp"], ["eb"]),
            "pn": lambda: sum_list("pa", (0, 1)), "pa": lambda: sum_list("pa", (2, 3)),
            "rn": lambda: vs(T.rn[:], T.sn[:, 16::17], 16383, None, A.bitwise_and, None, ["sn"], ["rn"]),
            "h7": lambda: vs(T.hi[:, 0:16], T.sn[:, 16::17], 16256, None, A.bitwise_and, None, ["sn"], [("hi", 0, 16)]),
            "l7": lambda: vs(T.hi[:, 16:32], T.sn[:, 16::17], 127, None, A.bitwise_and, None, ["sn"], [("hi", 16, 32)]),
            "nl": lambda: vc(T.nl[:], T.rn[:], ["rn"], ["nl"]),
            "nc": lambda: copy(T.nc[:], T.cw[:, 0:NW].indirect(T.nl[:]), ["cw", "nl", "sb", "nb"], ["nc"], bias=T.nb[:, 0:1],
                               scale=T.sb[:, t:t + 1]),
            "ys": lambda: copy(T.ys[:], T.diff[:, 0:4096].indirect(T.lo[:]), ["diff", "lo"], ["ys"]),
            "nf": new_counters,
            "at": lambda: copy(T.at[:], T.ac[:], ["ac", "th2"], ["at"], bias=T.th2[:, 0:1], scale=0.5),
            "rl": lambda: to_list("rl", "pa"), "pb": lambda: sum_list("pb", (0, 2, 3)), "cl": lambda: to_list("cl", "pb"),
            "q16": lambda: t and vs(T.q16[:], T.ac[:], 1.0 / 32, -0.46875, A.mult, A.add, ["ac"], ["q16"]),
            "mc": lambda: t and vs(T.mc[:], T.q16[:], -16.0, T.at[:, 0:1], A.mult, A.add, ["q16", "at"], ["mc"])}

    sums(0)
    zeros(FILL[3], FILL[4])
    twice(0)
    zeros(FILL[4], FILL[5])
    ch = chain(0)
    play(CHAIN0, ch, {"K": rest})
    last_constants()
    routes()
    late = []
    for t in range(5):
        if t == 4:
            for u, b, sem in ((1, "zh1", "h1"), (2, "zh2", "h2")):
                arrival(S, sem, len(topo.engines(cores[(rank + u) % N], core)), [b])
                dma(S, "y", lambda: g.sync.dma_start(T.zs[:, 256 * u:256 * u + 256], T[b][:]), [b], [])
            dma(S, "y", lambda: g.sync.dma_start(T.zs[:, 768:1024], T.zi[:, 4, :, :, :]), ["zi4"], [])
        marks = gather(t, late, ch)
        rows, calls = answer(t, marks)
        if t < 4:
            ch = chain(t + 1)
            ch.update(twice=lambda: twice(t + 1), sums=lambda: sums(t + 1))
        play(ANSWER + " " + CHAIN if t < 4 else ANSWER4, {**ch, **calls}, rows)
        late = rows["C"]
    dma(S, "s", lambda: C.dma_start(T.cs[:, 0:CUT], T.cw[0:128:16, C0:NW]), ["cw"], [])
    dma(S, "s", lambda: C.dma_start(T.cs[:, CUT:8192], T.cw[0:128:16, WASTE:C0]), ["cw"], [])
    dma(S, "y", lambda: g.sync.dma_start(T.xs[:, 0:CUT], T.xw[0:128:16, C0:NW]), ["xw"], [])
    dma(S, "y", lambda: g.sync.dma_start(T.xs[:, CUT:8192], T.xw[0:128:16, WASTE:C0]), ["xw"], [])
    for sem in SEMAPHORES:
        if S["count"].get(sem, 0):
            need(S, "g", (sem, S["count"][sem], {}))
